import numpy as np
import ml_dtypes


def mxq(x, axis, fmt="e4m3"):
    dtype, down = {"e4m3": (ml_dtypes.float8_e4m3fn, 7), "e5m2": (ml_dtypes.float8_e5m2, 14)}[fmt]
    v = np.moveaxis(np.asarray(x, np.float32).astype(ml_dtypes.bfloat16).astype(np.float64), axis, -1)
    blocks = v.reshape(v.shape[:-1] + (-1, 32))
    amax = np.abs(blocks).max(-1, keepdims=True)
    byte = np.maximum(np.where(amax > 0, np.frexp(amax)[1] - 1 + 127, 0) - down, 1)
    scale = np.exp2(byte - 127.0)
    codes = (blocks / scale).astype(np.float32).astype(dtype).astype(np.float64)
    return np.moveaxis((codes * scale).reshape(v.shape), -1, axis)


WIDE = False


def mx_kscale(k):
    if not WIDE:
        return np.ones(k)
    levels = np.array([10, -10, 5, -5, 0])
    if k % 512:
        return np.exp2(np.random.permutation(np.resize(levels, k // 32))).repeat(32)
    a = np.empty((k // 512, 16))
    for p in range(k // 512):
        a[p, :8] = np.random.permutation(np.resize(levels, 8))
        for g in range(8):
            far = levels[np.abs(levels - a[p, g]) >= 10]
            a[p, g + 8] = far[np.random.randint(len(far))]
    return np.exp2(a.ravel()).repeat(32)


def f64(x):
    return np.asarray(x).astype(np.float64)


def striped(idx):
    return np.tile(idx.reshape(-1, 16).T, (8, 1)).astype(np.uint16)


def unstriped(offs):
    return offs[:16].T.reshape(-1).astype(np.int64)


E2M1 = np.array([0.0, 0.5, 1.0, 1.5, 2.0, 3.0, 4.0, 6.0, -0.0, -0.5, -1.0, -1.5, -2.0, -3.0, -4.0, -6.0])


def pack_weight(w, fmt):
    k, n = w.shape
    w = f64(np.asarray(w, np.float32).astype(ml_dtypes.bfloat16)).reshape(k // 32, 32, n)
    amax = np.abs(w).max(1)
    if fmt == "e4m3":
        byte = np.frexp(amax)[1] - 1 + 127 - 7
    else:
        mant, ex = np.frexp(amax / 6.0)
        byte = np.where(mant > 0.5, ex, ex - 1) + 127
    byte = np.clip(np.where(amax > 0, byte, 1), 1, 254)
    scaled = (w * np.exp2(127.0 - byte)[:, None, :]).reshape(k, n).astype(np.float32)
    by_word = np.ascontiguousarray(scaled.reshape(k // 512, 128, 4, n).transpose(0, 1, 3, 2))
    if fmt == "e4m3":
        words = by_word.astype(ml_dtypes.float8_e4m3fn).view(np.uint8)
    else:
        c = by_word.astype(ml_dtypes.float4_e2m1fn).view(np.uint8) & 0xF
        words = (c[..., 0::2] | (c[..., 1::2] << 4)).reshape(k // 512, 128, 2 * n)
    return np.ascontiguousarray(words), np.ascontiguousarray(byte.astype(np.uint8).reshape(k // 512, 16, n))


def unpack_weight(words, scales, fmt):
    g, _, n = scales.shape
    words = np.ascontiguousarray(words).reshape(g, 128, n, -1)
    if fmt == "e4m3":
        vals = words.view(ml_dtypes.float8_e4m3fn).astype(np.float64)
    else:
        nib = np.empty((g, 128, n, 4), np.uint8)
        nib[..., 0::2] = words & 0xF
        nib[..., 1::2] = words >> 4
        vals = E2M1[nib]
    vals = vals * np.repeat(np.exp2(scales.astype(np.float64) - 127.0), 8, axis=1)[..., None]
    return vals.transpose(0, 1, 3, 2).reshape(g * 512, n)


def gelu(v):
    return 0.5 * v * (1.0 + np.tanh(np.sqrt(2.0 / np.pi) * (v + 0.044715 * v**3)))


K, T, S, T2, H, N = 1536, 2048, 512, 1024, 1024, 512

def setup_inputs():
    n = np.random.standard_normal
    s = mx_kscale(K)[:, None]
    u = mx_kscale(H)[:, None]
    tab_words, tab_scales = pack_weight(n((K, T)) * s, "e4m3")
    tab2_words, tab2_scales = pack_weight(n((K, T)) * s, "e4m3")
    w4_words, w4_scales = pack_weight(n((H, N)) / np.sqrt(H) / u, "e2m1")
    perm = np.random.permutation(T2)
    return {
        "tab_words": tab_words, "tab_scales": tab_scales,
        "tab2_words": tab2_words, "tab2_scales": tab2_scales,
        "w1": (n((K, H)) / np.sqrt(K) / s).astype(np.float32),
        "w4_words": w4_words, "w4_scales": w4_scales,
        "threat": (0.8 * n((H, S))).astype(np.float32),
        "gain": (1.5 * np.exp(0.3 * n(H)) * u[:, 0]).astype(np.float32),
        "wg1": np.exp(0.3 * n((128, S))).astype(np.float32),
        "wg2": np.exp(0.3 * n((128, S))).astype(np.float32),
        "offs": striped(np.random.permutation(T)[:S]),
        "offs2": striped(np.random.permutation(T)[:S]),
        "offs3": striped(perm[:S]),
        "offs4": striped(perm[S:]),
    }

def reference(tab_words, tab_scales, tab2_words, tab2_scales, w1, w4_words, w4_scales,
              threat, gain, wg1, wg2, offs, offs2, offs3, offs4):
    v = unpack_weight(tab_words, tab_scales, "e4m3")[:, unstriped(offs)]
    v2 = unpack_weight(tab2_words, tab2_scales, "e4m3")[:, unstriped(offs2)]
    wq = mxq(f64(w1), 0, "e4m3")
    h1 = 1.0 / (1.0 + np.exp(-(wq.T @ v)))
    h2 = (wq.T @ v2) - f64(threat)
    page = np.zeros((H, T2))
    page[:, unstriped(offs3)] = np.tile(f64(wg1), (H // 128, 1)) * h1
    page[:, unstriped(offs4)] = np.tile(f64(wg2), (H // 128, 1)) * h2
    z = np.maximum(page, 0.0) * f64(gain)[:, None]
    w4 = unpack_weight(w4_words, w4_scales, "e2m1")
    return w4.T @ mxq(z, 0, "e4m3")

@@ -1,0 +1,299 @@
+from contextlib import ExitStack
+
+import concourse.mybir as mybir
+
+K, T, S, T2, H, N = 1536, 2048, 512, 1024, 1024, 512
+FLOPS = 2 * (2 * K * H * S + H * N * T2)
+
+F32 = mybir.dt.float32
+BF16 = mybir.dt.bfloat16
+I32 = mybir.dt.int32
+U32 = mybir.dt.uint32
+U16 = mybir.dt.uint16
+U8 = mybir.dt.uint8
+FP8X4 = mybir.dt.float8_e4m3fn_x4
+FP4X4 = mybir.dt.float4_e2m1fn_x4
+ALU = mybir.AluOpType
+ACT = mybir.ActivationFunctionType
+
+P = 128
+PACK = 4
+K_PASS = P * PACK
+G1 = K // K_PASS
+G2 = H // K_PASS
+HALF = 512
+RING = 3
+W1_CHUNKS = ((0, 128), (128, 128), (256, 256), (512, 512))
+STAGE = 4096
+
+
+def tile_list_turn_order_evaluator_kernel(
+    tc, tab_words, tab_scales, tab2_words, tab2_scales, w1, w4_words, w4_scales,
+    threat, gain, wg1, wg2, offs, offs2, offs3, offs4, out,
+):
+    nc = tc.nc
+    with ExitStack() as ctx:
+        lists = ctx.enter_context(tc.tile_pool(name="lists", bufs=1))
+        keep = ctx.enter_context(tc.tile_pool(name="keep", bufs=1))
+        psum = ctx.enter_context(tc.psum_pool(name="psum", bufs=1))
+
+        def held(shape, dtype, name, place=None):
+            return keep.tile(shape, dtype, name=name, tag=place or name, align_bytes=64)
+
+        def load_list(src, name):
+            tile = lists.tile([P, S // 16], U16, name=name)
+            nc.sync.dma_start(tile[:], src)
+            return tile
+
+        def load_words(src, g, name):
+            tile = held([P, T], U32, f"{name}{g}")
+            nc.sync.dma_start(tile[:].bitcast(I32), src[g].rearrange("p t i -> p (t i)").bitcast(I32))
+            return tile
+
+        def cleared(shape, name):
+            tile = held(shape, U8, name)
+            nc.vector.memset(tile[:].bitcast(I32), 0)
+            return tile
+
+        def load_table_scales(queue, tile, src):
+            for q in range(4):
+                queue.dma_start(tile[32 * q : 32 * q + 4 * G1, :].bitcast(I32), src[:, 4 * q : 4 * q + 4, :].bitcast(I32))
+
+        def load_w1(first, width):
+            tiles = []
+            for g in range(G1):
+                tile = held([P, PACK, width], F32, f"w1_{first}_{g}")
+                rows = w1[g * K_PASS : (g + 1) * K_PASS, first : first + width]
+                nc.sync.dma_start(tile[:], rows.rearrange("(p j) c -> p j c", j=PACK))
+                tiles.append(tile)
+            return tiles
+
+        def load_wg_slots(src, t0, t1, name):
+            tile = held([P, t1 - t0, S], F32, name)
+            rows = src.rearrange("(q t) j -> q t j", t=PACK)[:, t0:t1, :]
+            for q in range(4):
+                nc.sync.dma_start(tile[32 * q : 32 * (q + 1), :, :], rows)
+            return [tile[:, t, :] for t in range(t1 - t0)]
+
+        def load_plain(src, shape, name):
+            tile = held(shape, F32, name)
+            nc.sync.dma_start(tile[:], src)
+            return tile
+
+        tab_planes = cleared([P, T], "tab_planes")
+        tab2_planes = cleared([P, T], "tab2_planes")
+        w4_planes = cleared([P, G2, N], "w4_planes")
+        load_table_scales(nc.scalar, tab_planes, tab_scales)
+
+        warm = held([P, 2], F32, "warm")
+        nc.vector.memset(warm[:, 0:1], 0.0)
+        nc.scalar.activation(warm[:, 1:2], warm[:, 0:1], ACT.Sigmoid)
+
+        ally_list = load_list(offs, "ally_list")
+        tab_tiles = [load_words(tab_words, 0, "tab")]
+        w1_raw = [load_w1(*W1_CHUNKS[0])]
+        tab_tiles.extend(load_words(tab_words, g, "tab") for g in range(1, G1))
+        wg1_rows = load_plain(wg1, [P, S], "wg1_rows")
+        ally_slots = load_list(offs3, "ally_slots")
+        w1_raw.extend(load_w1(*chunk) for chunk in W1_CHUNKS[1:-1])
+        enemy_list = load_list(offs2, "enemy_list")
+        load_table_scales(nc.sync, tab2_planes, tab2_scales)
+        w1_raw.append(load_w1(*W1_CHUNKS[-1]))
+        tab2_tiles = [load_words(tab2_words, g, "tab2") for g in range(G1)]
+        wg1_slots = load_wg_slots(wg1, 0, 1, "wg1_first") + load_wg_slots(wg1, 1, PACK, "wg1_rest")
+        enemy_slots = load_list(offs4, "enemy_slots")
+        wg2_rows = load_plain(wg2, [P, S], "wg2_rows")
+        threat_rows = [load_plain(threat[b * P : (b + 1) * P, :], [P, S], f"threat{b}")[:] for b in range(PACK)]
+        gain_low = held([P, PACK], F32, "gain_low")
+        with nc.allow_non_contiguous_dma(reason="one gain a partition and row tile"):
+            nc.sync.dma_start(gain_low[:], gain[0:K_PASS].rearrange("(b p) -> p b", p=P))
+        gain_high = load_plain(gain[K_PASS:].rearrange("(p t) -> p t", t=PACK), [P, PACK], "gain_high")
+        threat_high = load_plain(threat[K_PASS:, :].rearrange("(p t) j -> p t j", t=PACK), [P, PACK, S], "threat_high")
+        threat_rows.extend(threat_high[:, t, :] for t in range(PACK))
+        wg2_slots = load_wg_slots(wg2, 0, PACK, "wg2_slots")
+        w4_codes = held([P, G2, 2 * N], U8, "w4_codes")
+        nc.sync.dma_start(w4_codes[:].bitcast(I32), w4_words.rearrange("a p c -> p a c").bitcast(I32))
+        for q in range(4):
+            nc.sync.dma_start(
+                w4_planes[32 * q : 32 * q + 4, :, :].bitcast(I32),
+                w4_scales[:, 4 * q : 4 * q + 4, :].rearrange("a r n -> r a n").bitcast(I32),
+            )
+
+        ally_weights = [wg1_rows[:]] * PACK + wg1_slots
+        enemy_weights = [wg2_rows[:]] * PACK + wg2_slots
+
+        banks = [psum.tile([P, HALF], F32, name=f"bank{i}") for i in range(8)]
+        pages = [held([P, T2], F32, f"page{i}") for i in range(2 * PACK)]
+        ring = [held([P, S], F32, f"ring{i}") for i in range(RING)]
+
+        def gather_words(picked, tile, offsets):
+            nc.vector.tensor_copy(picked, tile[:].indirect(offsets[:]))
+
+        def gather_planes(tile, offsets, name, place=None):
+            picked = held([P, S], U8, name, place)
+            nc.vector.tensor_copy(picked[:], tile[:].indirect(offsets[:]))
+            return picked
+
+        w1_codes, w1_planes = {}, {}
+
+        def quantise_w1(c, staged):
+            first, width = W1_CHUNKS[c]
+            for g in range(G1):
+                codes = held([P, width], U32, f"w1_codes{c}_{g}")
+                planes = held([P, width], U8, f"w1_planes{c}_{g}")
+                grouped = staged[g]
+                if first < K_PASS:
+                    nc.scalar.copy(
+                        grouped.rearrange("p (c i j) -> p c j i", i=4, j=PACK),
+                        w1_raw[c][g][:].rearrange("p j (c i) -> p c j i", i=4),
+                    )
+                else:
+                    for rows in (slice(0, P // 2), slice(P // 2, P)):
+                        nc.scalar.copy(
+                            grouped.rearrange("p (t m j) -> p m j t", t=PACK, j=PACK)[:, rows],
+                            w1_raw[c][g][:].rearrange("p j (m t) -> p m j t", t=PACK)[:, rows],
+                        )
+                nc.vector.quantize_mx(out=codes[:].bitcast(FP8X4), scales=planes[:], in_=grouped)
+                for u in range(width // P):
+                    w1_codes[first // P + u, g] = codes[:, u * P : (u + 1) * P]
+                    w1_planes[first // P + u, g] = planes[:, u * P : (u + 1) * P]
+
+        def first_product(i, words, planes, bank):
+            for g in range(G1):
+                nc.tensor.matmul_mx(
+                    out=bank[:], lhsT=w1_codes[i, g].bitcast(FP8X4), lhsT_scale=w1_planes[i, g],
+                    rhs=words[:, g, :].bitcast(FP8X4), rhs_scale=planes[4 * g :, :],
+                    start=(g == 0), stop=(g == G1 - 1),
+                )
+
+        def ally_values(i, step, values):
+            bank = banks[6 + step % 2]
+            first_product(i, ally_words, ally_planes, bank)
+            nc.scalar.activation(values, bank[:], ACT.Sigmoid)
+
+        def enemy_values(i, step, values):
+            bank = banks[6 + step % 2]
+            first_product(i, enemy_words, enemy_planes, bank)
+            nc.vector.tensor_tensor(values, bank[:], threat_rows[i], ALU.subtract)
+            nc.scalar.activation(values, values, ACT.Relu)
+
+        def place_allies(i, values):
+            nc.vector.tensor_tensor(pages[i][:].indirect(ally_slots[:]), values, ally_weights[i], ALU.mult)
+
+        def place_enemies(i, values):
+            nc.vector.tensor_tensor(pages[i][:].indirect(enemy_slots[:]), values, enemy_weights[i], ALU.mult)
+
+        z_codes = [held([P, T2], U32, f"z_codes{a}") for a in range(G2)]
+        z_planes = [held([P, T2], U8, f"z_planes{a}") for a in range(G2)]
+
+        def quantise_z(a, h, grouped):
+            cols = slice(h * HALF, (h + 1) * HALF)
+            nc.vector.quantize_mx(
+                out=z_codes[a][:, cols].bitcast(FP8X4), scales=z_planes[a][:, cols],
+                in_=grouped[:, cols, :].rearrange("p m t -> p (m t)"),
+            )
+
+        def second_product(a, h):
+            cols = slice(h * HALF, (h + 1) * HALF)
+            for nt in range(N // P):
+                nc.tensor.matmul_mx(
+                    out=banks[4 * h + nt][:],
+                    lhsT=w4_codes[:, a, 2 * P * nt : 2 * P * (nt + 1)].bitcast(FP4X4),
+                    lhsT_scale=w4_planes[:, a, P * nt : P * (nt + 1)],
+                    rhs=z_codes[a][:, cols].bitcast(FP8X4), rhs_scale=z_planes[a][:, cols],
+                    start=(a == 0), stop=(a == G2 - 1),
+                )
+
+        def interleave(grouped, by_slot, h, slots):
+            cols = slice(h * HALF, (h + 1) * HALF)
+            nc.scalar.copy(
+                grouped[:, cols, 0:slots].rearrange("p (c i) t -> p c t i", i=4),
+                by_slot[:, 0:slots, cols].rearrange("p t (c i) -> p c t i", i=4),
+            )
+
+        ally_words = held([P, G1, S], U32, "ally_words")
+        gather_words(ally_words[:, 0, :], tab_tiles[0], ally_list)
+        first_stage = held([P, G1, PACK * P], BF16, "first_stage")
+        quantise_w1(0, [first_stage[:, g, :] for g in range(G1)])
+        ally_planes = gather_planes(tab_planes, ally_list, "ally_planes")
+        for g in range(1, G1):
+            gather_words(ally_words[:, g, :], tab_tiles[g], ally_list)
+        stage = held([P, STAGE], BF16, "stage", place=f"tab{G1 - 1}")
+        staged, cursor = {}, 0
+        for c in range(1, len(W1_CHUNKS)):
+            size = PACK * W1_CHUNKS[c][1]
+            staged[c] = []
+            if c == len(W1_CHUNKS) - 1:
+                staged[c].append(held([P, size], BF16, "wide_stage", place=f"w1_{2 * P}_1")[:])
+            while len(staged[c]) < G1:
+                cursor = -(-cursor // size) * size % STAGE
+                staged[c].append(stage[:, cursor : cursor + size])
+                cursor = cursor + size
+        staged[3][G1 - 1] = held([P, PACK * K_PASS], BF16, "last_stage", place=f"w1_{2 * P}_0")[:]
+        for i in range(PACK):
+            if i in (1, 2):
+                quantise_w1(i, staged[i])
+            ally_values(i, i, ring[i % RING][:])
+            place_allies(i, ring[i % RING][:])
+        quantise_w1(3, staged[3])
+        enemy_words = held([P, G1, S], U32, "enemy_words", place=f"w1_{2 * P}_0")
+        enemy_planes = gather_planes(tab2_planes, enemy_list, "enemy_planes", place=f"w1_{2 * P}_{G1 - 1}")
+        for g in range(G1):
+            gather_words(enemy_words[:, g, :], tab2_tiles[g], enemy_list)
+        ally_values(4, 4, ring[4 % RING][:])
+        place_allies(4, ring[4 % RING][:])
+        ally_values(5, 5, ring[5 % RING][:])
+        ally_values(6, 6, ring[6 % RING][:])
+        place_allies(5, ring[5 % RING][:])
+        enemy_values(0, 7, ring[7 % RING][:])
+        place_allies(6, ring[6 % RING][:])
+
+        by_slot = held([P, PACK, T2], BF16, "by_slot", place=f"w1_{K_PASS}_0")
+        grouped_low = held([P, T2, PACK], BF16, "grouped_low", place=f"w1_{K_PASS}_1")
+        grouped_high = held([P, T2, PACK], BF16, "grouped_high", place=f"tab{G1 - 1}")
+        for i in range(2 * PACK - 1):
+            step = 7 + i
+            if i + 1 < 2 * PACK - 1:
+                enemy_values(i + 1, step + 1, ring[(step + 1) % RING][:])
+            place_enemies(i, ring[step % RING][:])
+            if i < PACK:
+                rounded = held([P, T2], BF16, f"rounded{i}")
+                nc.scalar.activation(rounded[:], pages[i][:], ACT.Copy, scale=gain_low[:, i : i + 1])
+                for t in range(PACK):
+                    nc.sync.dma_start(by_slot[32 * i : 32 * (i + 1), t, :], rounded[t:P:PACK, :])
+                if i == PACK - 1:
+                    for h in range(2):
+                        interleave(grouped_low, by_slot, h, PACK)
+            else:
+                t = i - PACK
+                nc.scalar.activation(by_slot[:, t, :], pages[i][:], ACT.Copy, scale=gain_high[:, t : t + 1])
+
+        def freed(h):
+            return grouped_low[:, h * HALF : h * HALF + S // 2, :].rearrange("p m t -> p (m t)").bitcast(F32)
+
+        last = 2 * PACK - 1
+        quantise_z(0, 0, grouped_low)
+        enemy_values(last, 14, freed(0))
+        quantise_z(0, 1, grouped_low)
+        ally_values(last, 15, freed(1))
+        place_enemies(last, freed(0))
+        interleave(grouped_high, by_slot, 0, PACK)
+        interleave(grouped_high, by_slot, 1, PACK - 1)
+        for h in range(2):
+            second_product(0, h)
+        place_allies(last, freed(1))
+
+        last_gain = gain_high[:, PACK - 1 : PACK]
+        nc.vector.tensor_scalar(grouped_high[:, 0:HALF, PACK - 1], pages[last][:, 0:HALF], last_gain, None, ALU.mult)
+        nc.scalar.activation(grouped_high[:, HALF:, PACK - 1], pages[last][:, HALF:], ACT.Copy, scale=last_gain)
+        for h in range(2):
+            quantise_z(1, h, grouped_high)
+            second_product(1, h)
+        for h in range(2):
+            result = held([P, N // P, HALF], F32, f"result{h}", place=f"tab{h}")
+            for nt in range(N // P):
+                if nt % 2 == 0:
+                    nc.scalar.copy(result[:, nt, :], banks[4 * h + nt][:])
+                else:
+                    nc.vector.tensor_copy(result[:, nt, :], banks[4 * h + nt][:])
+                nc.sync.dma_start(out[nt * P : (nt + 1) * P, h * HALF : (h + 1) * HALF], result[:, nt, :])

@@ -1,6 +1,7 @@
 from contextlib import ExitStack
 
 import concourse.mybir as mybir
+from concourse.masks import make_identity
 
 K, T, S, T2, H, N = 1536, 2048, 512, 1024, 1024, 512
 FLOPS = 2 * (2 * K * H * S + H * N * T2)
@@ -22,9 +23,7 @@ K_PASS = P * PACK
 G1 = K // K_PASS
 G2 = H // K_PASS
 HALF = 512
-RING = 3
 W1_CHUNKS = ((0, 128), (128, 128), (256, 256), (512, 512))
-STAGE = 4096
 
 
 def tile_list_turn_order_evaluator_kernel(
@@ -59,10 +58,11 @@ def tile_list_turn_order_evaluator_kernel(
             for q in range(4):
                 queue.dma_start(tile[32 * q : 32 * q + 4 * G1, :].bitcast(I32), src[:, 4 * q : 4 * q + 4, :].bitcast(I32))
 
-        def load_w1(first, width):
+        def load_w1(c, lo=0, hi=G1):
+            first, width = W1_CHUNKS[c]
             tiles = []
-            for g in range(G1):
-                tile = held([P, PACK, width], F32, f"w1_{first}_{g}")
+            for g in range(lo, hi):
+                tile = held([P, PACK, width], F32, f"w1_{c}_{g}")
                 rows = w1[g * K_PASS : (g + 1) * K_PASS, first : first + width]
                 nc.sync.dma_start(tile[:], rows.rearrange("(p j) c -> p j c", j=PACK))
                 tiles.append(tile)
@@ -80,30 +80,43 @@ def tile_list_turn_order_evaluator_kernel(
             nc.sync.dma_start(tile[:], src)
             return tile
 
-        tab_planes = cleared([P, T], "tab_planes")
-        tab2_planes = cleared([P, T], "tab2_planes")
+        def load_threat(b):
+            return load_plain(threat[b * P : (b + 1) * P, :], [P, S], f"threat{b}")[:]
+
+        ally_scales = cleared([P, T], "ally_scales")
+        enemy_scales = cleared([P, T], "enemy_scales")
         w4_planes = cleared([P, G2, N], "w4_planes")
-        load_table_scales(nc.scalar, tab_planes, tab_scales)
+        load_table_scales(nc.scalar, ally_scales, tab_scales)
+        load_table_scales(nc.gpsimd, enemy_scales, tab2_scales)
+        identity = held([P, P], F32, "identity")
+        make_identity(nc, identity[:])
 
         warm = held([P, 2], F32, "warm")
         nc.vector.memset(warm[:, 0:1], 0.0)
         nc.scalar.activation(warm[:, 1:2], warm[:, 0:1], ACT.Sigmoid)
 
         ally_list = load_list(offs, "ally_list")
-        tab_tiles = [load_words(tab_words, 0, "tab")]
-        w1_raw = [load_w1(*W1_CHUNKS[0])]
-        tab_tiles.extend(load_words(tab_words, g, "tab") for g in range(1, G1))
-        wg1_rows = load_plain(wg1, [P, S], "wg1_rows")
+        ally_table = [load_words(tab_words, 0, "ally")]
+        w1_raw = [load_w1(0)]
+        ally_table.extend(load_words(tab_words, g, "ally") for g in range(1, G1))
+        wg1_rows = held([P, S], F32, "wg1_rows")
+        nc.sync.dma_start(wg1_rows[:, 0 : S // 2], wg1[:, 0 : S // 2])
         ally_slots = load_list(offs3, "ally_slots")
-        w1_raw.extend(load_w1(*chunk) for chunk in W1_CHUNKS[1:-1])
+        w1_raw.append(load_w1(1))
+        nc.sync.dma_start(wg1_rows[:, S // 2 :], wg1[:, S // 2 :])
+        w1_raw.append(load_w1(2, 0, 1))
         enemy_list = load_list(offs2, "enemy_list")
-        load_table_scales(nc.sync, tab2_planes, tab2_scales)
-        w1_raw.append(load_w1(*W1_CHUNKS[-1]))
-        tab2_tiles = [load_words(tab2_words, g, "tab2") for g in range(G1)]
-        wg1_slots = load_wg_slots(wg1, 0, 1, "wg1_first") + load_wg_slots(wg1, 1, PACK, "wg1_rest")
+        w1_raw[2].extend(load_w1(2, 1, G1))
+        w1_raw.append(load_w1(3, 0, 1))
+        enemy_table = [load_words(tab2_words, 0, "enemy")]
+        w1_raw[3].extend(load_w1(3, 1, G1))
+        threat_rows = [load_threat(0)]
+        enemy_table.extend(load_words(tab2_words, g, "enemy") for g in range(1, G1))
+        wg1_slots = load_wg_slots(wg1, 0, 1, "wg1_first")
+        wg1_slots.extend(load_wg_slots(wg1, 1, PACK, "wg1_rest"))
         enemy_slots = load_list(offs4, "enemy_slots")
         wg2_rows = load_plain(wg2, [P, S], "wg2_rows")
-        threat_rows = [load_plain(threat[b * P : (b + 1) * P, :], [P, S], f"threat{b}")[:] for b in range(PACK)]
+        threat_rows.extend(load_threat(b) for b in range(1, PACK))
         gain_low = held([P, PACK], F32, "gain_low")
         with nc.allow_non_contiguous_dma(reason="one gain a partition and row tile"):
             nc.sync.dma_start(gain_low[:], gain[0:K_PASS].rearrange("(b p) -> p b", p=P))
@@ -121,179 +134,212 @@ def tile_list_turn_order_evaluator_kernel(
 
         ally_weights = [wg1_rows[:]] * PACK + wg1_slots
         enemy_weights = [wg2_rows[:]] * PACK + wg2_slots
-
         banks = [psum.tile([P, HALF], F32, name=f"bank{i}") for i in range(8)]
-        pages = [held([P, T2], F32, f"page{i}") for i in range(2 * PACK)]
-        ring = [held([P, S], F32, f"ring{i}") for i in range(RING)]
-
-        def gather_words(picked, tile, offsets):
-            nc.vector.tensor_copy(picked, tile[:].indirect(offsets[:]))
-
-        def gather_planes(tile, offsets, name, place=None):
-            picked = held([P, S], U8, name, place)
-            nc.vector.tensor_copy(picked[:], tile[:].indirect(offsets[:]))
-            return picked
-
+        pages = {}
         w1_codes, w1_planes = {}, {}
 
-        def quantise_w1(c, staged):
-            first, width = W1_CHUNKS[c]
-            for g in range(G1):
-                codes = held([P, width], U32, f"w1_codes{c}_{g}")
-                planes = held([P, width], U8, f"w1_planes{c}_{g}")
-                grouped = staged[g]
-                if first < K_PASS:
-                    nc.scalar.copy(
-                        grouped.rearrange("p (c i j) -> p c j i", i=4, j=PACK),
-                        w1_raw[c][g][:].rearrange("p j (c i) -> p c j i", i=4),
-                    )
-                else:
-                    for rows in (slice(0, P // 2), slice(P // 2, P)):
-                        nc.scalar.copy(
-                            grouped.rearrange("p (t m j) -> p m j t", t=PACK, j=PACK)[:, rows],
-                            w1_raw[c][g][:].rearrange("p j (m t) -> p m j t", t=PACK)[:, rows],
-                        )
-                nc.vector.quantize_mx(out=codes[:].bitcast(FP8X4), scales=planes[:], in_=grouped)
-                for u in range(width // P):
-                    w1_codes[first // P + u, g] = codes[:, u * P : (u + 1) * P]
-                    w1_planes[first // P + u, g] = planes[:, u * P : (u + 1) * P]
+        def gather(picked, tile, offsets):
+            nc.vector.tensor_copy(picked, tile[:].indirect(offsets))
 
-        def first_product(i, words, planes, bank):
+        def round_w1(c, g, grouped):
+            if W1_CHUNKS[c][0] < K_PASS:
+                nc.scalar.copy(
+                    grouped.rearrange("p (c i j) -> p c j i", i=4, j=PACK),
+                    w1_raw[c][g][:].rearrange("p j (c i) -> p c j i", i=4),
+                )
+            else:
+                for rows in (slice(0, P // 2), slice(P // 2, P)):
+                    nc.scalar.copy(
+                        grouped.rearrange("p (t m j) -> p m j t", t=PACK, j=PACK)[:, rows],
+                        w1_raw[c][g][:].rearrange("p j (m t) -> p m j t", t=PACK)[:, rows],
+                    )
+
+        def stage_w1(c, lo, hi):
+            size = PACK * W1_CHUNKS[c][1]
+            stage = held([P, (hi - lo) * size], BF16, f"stage{c}_{lo}")
+            for g in range(lo, hi):
+                round_w1(c, g, stage[:, (g - lo) * size : (g - lo + 1) * size])
+            return stage
+
+        def quantise_w1(c, lo, hi, stage=None):
+            first, width = W1_CHUNKS[c]
+            stage = stage_w1(c, lo, hi) if stage is None else stage
+            codes = held([P, (hi - lo) * width], U32, f"w1_codes{c}_{lo}")
+            planes = held([P, (hi - lo) * width], U8, f"w1_planes{c}_{lo}")
+            for g in range(lo, hi):
+                for u in range(width // P):
+                    cols = slice((g - lo) * width + u * P, (g - lo) * width + (u + 1) * P)
+                    w1_codes[first // P + u, g] = codes[:, cols]
+                    w1_planes[first // P + u, g] = planes[:, cols]
+            nc.vector.quantize_mx(out=codes[:].bitcast(FP8X4), scales=planes[:], in_=stage[:])
+
+        def first_product(i, words, planes, bank, cols):
             for g in range(G1):
                 nc.tensor.matmul_mx(
-                    out=bank[:], lhsT=w1_codes[i, g].bitcast(FP8X4), lhsT_scale=w1_planes[i, g],
-                    rhs=words[:, g, :].bitcast(FP8X4), rhs_scale=planes[4 * g :, :],
+                    out=bank, lhsT=w1_codes[i, g].bitcast(FP8X4), lhsT_scale=w1_planes[i, g],
+                    rhs=words[g][:, cols].bitcast(FP8X4), rhs_scale=planes[4 * g :, cols],
                     start=(g == 0), stop=(g == G1 - 1),
                 )
 
-        def ally_values(i, step, values):
-            bank = banks[6 + step % 2]
-            first_product(i, ally_words, ally_planes, bank)
+        every = slice(0, S)
+
+        def ally_values(i, values):
+            bank = banks[i % 2]
+            first_product(i, ally_words, ally_planes, bank[:], every)
             nc.scalar.activation(values, bank[:], ACT.Sigmoid)
 
-        def enemy_values(i, step, values):
-            bank = banks[6 + step % 2]
-            first_product(i, enemy_words, enemy_planes, bank)
-            nc.vector.tensor_tensor(values, bank[:], threat_rows[i], ALU.subtract)
-            nc.scalar.activation(values, values, ACT.Relu)
+        def enemy_values(i, values, negated_place, turned_place):
+            sums, turned_sums, back = banks[2 + i % 2], banks[4 + i % 2], banks[6 + i % 2]
+            first_product(i, enemy_words, enemy_planes, sums[:], every)
+            negated = held([P, S], F32, f"negated{i}", negated_place)
+            nc.scalar.activation(negated[:], sums[:], ACT.Copy, scale=-1.0)
+            blocks = [slice(c * P, (c + 1) * P) for c in range(S // P)]
+            terms = [(threat_rows[i], b) for b in blocks] + [(negated[:], b) for b in blocks]
+            for n, (term, b) in enumerate(terms):
+                nc.tensor.matmul(
+                    turned_sums[:, b], lhsT=term[:, b], rhs=identity[:], is_transpose=True,
+                    start=(n == 0), stop=(n == len(terms) - 1),
+                )
+            turned = held([P, S], F32, f"turned{i}", turned_place)
+            nc.scalar.activation(turned[:], turned_sums[:], ACT.Relu, scale=-1.0)
+            for b in blocks:
+                nc.tensor.transpose(back[:, b], turned[:, b], identity[:])
+            nc.scalar.copy(values, back[:])
 
-        def place_allies(i, values):
-            nc.vector.tensor_tensor(pages[i][:].indirect(ally_slots[:]), values, ally_weights[i], ALU.mult)
+        def place(i, slots, values, weights):
+            nc.vector.tensor_tensor(pages[i][:].indirect(slots), values, weights, ALU.mult)
+
+        def place_allies(i, values, page_place):
+            pages[i] = held([P, T2], F32, f"page{i}", page_place)
+            place(i, ally_slots[:], values, ally_weights[i])
 
         def place_enemies(i, values):
-            nc.vector.tensor_tensor(pages[i][:].indirect(enemy_slots[:]), values, enemy_weights[i], ALU.mult)
+            place(i, enemy_slots[:], values, enemy_weights[i])
 
-        z_codes = [held([P, T2], U32, f"z_codes{a}") for a in range(G2)]
-        z_planes = [held([P, T2], U8, f"z_planes{a}") for a in range(G2)]
-
-        def quantise_z(a, h, grouped):
-            cols = slice(h * HALF, (h + 1) * HALF)
-            nc.vector.quantize_mx(
-                out=z_codes[a][:, cols].bitcast(FP8X4), scales=z_planes[a][:, cols],
-                in_=grouped[:, cols, :].rearrange("p m t -> p (m t)"),
-            )
-
-        def second_product(a, h):
+        def second_product(a, h, codes, planes):
             cols = slice(h * HALF, (h + 1) * HALF)
             for nt in range(N // P):
                 nc.tensor.matmul_mx(
                     out=banks[4 * h + nt][:],
                     lhsT=w4_codes[:, a, 2 * P * nt : 2 * P * (nt + 1)].bitcast(FP4X4),
                     lhsT_scale=w4_planes[:, a, P * nt : P * (nt + 1)],
-                    rhs=z_codes[a][:, cols].bitcast(FP8X4), rhs_scale=z_planes[a][:, cols],
+                    rhs=codes[:, cols].bitcast(FP8X4), rhs_scale=planes[:, cols],
                     start=(a == 0), stop=(a == G2 - 1),
                 )
 
-        def interleave(grouped, by_slot, h, slots):
+        def interleave(grouped, h, slots):
             cols = slice(h * HALF, (h + 1) * HALF)
             nc.scalar.copy(
                 grouped[:, cols, 0:slots].rearrange("p (c i) t -> p c t i", i=4),
                 by_slot[:, 0:slots, cols].rearrange("p t (c i) -> p c t i", i=4),
             )
 
-        ally_words = held([P, G1, S], U32, "ally_words")
-        gather_words(ally_words[:, 0, :], tab_tiles[0], ally_list)
-        first_stage = held([P, G1, PACK * P], BF16, "first_stage")
-        quantise_w1(0, [first_stage[:, g, :] for g in range(G1)])
-        ally_planes = gather_planes(tab_planes, ally_list, "ally_planes")
+        ally_picked = held([P, G1, S], U32, "ally_picked")
+        ally_words = [ally_picked[:, g, :] for g in range(G1)]
+        ally_planes = held([P, S], U8, "ally_planes")
+        gather(ally_words[0], ally_table[0], ally_list[:])
+        gather(ally_planes[:], ally_scales, ally_list[:])
+        quantise_w1(0, 0, 2)
+        quantise_w1(0, 2, G1)
+        gather(ally_words[1], ally_table[1], ally_list[:])
+        low_allies = held([P, 1, S], F32, "low_allies", "ally0")
+        pages[0] = held([P, T2], F32, "page0")
+        halves = [(slice(h * S // 2, (h + 1) * S // 2), slice(h * S // 32, (h + 1) * S // 32)) for h in range(2)]
+        for cols, entries in halves:
+            gather(ally_words[2][:, cols], ally_table[2], ally_list[:, entries])
+        for h, (cols, entries) in enumerate(halves):
+            first_product(0, ally_words, ally_planes, banks[h][:, 0 : S // 2], cols)
+            nc.scalar.activation(low_allies[:, 0, cols], banks[h][:, 0 : S // 2], ACT.Sigmoid)
+        for cols, entries in halves:
+            place(0, ally_slots[:, entries], low_allies[:, 0, cols], wg1_rows[:, cols])
+
+        quantise_w1(1, 0, 2)
+        quantise_w1(1, 2, G1)
+        enemy_planes = held([P, S], U8, "enemy_planes")
+        gather(enemy_planes[:], enemy_scales, enemy_list[:])
+        quantise_w1(2, 0, 2)
+        second = held([P, S], F32, "second", "w1_2_1")
+        ally_values(1, second[:])
+        place_allies(1, second[:], "enemy_scales")
+
+        quantise_w1(2, 2, G1)
+        enemy_first = held([P, S], U32, "enemy_first", "w1_1_2")
+        gather(enemy_first[:], enemy_table[0], enemy_list[:])
+        high_stage = stage_w1(3, 0, 2)
+        third = held([P, S], F32, "third", "w1_3_0")
+        ally_values(2, third[:])
+        place_allies(2, third[:], "stage2_0")
+        fourth = held([P, S], F32, "fourth", "w1_3_1")
+        ally_values(3, fourth[:])
+        quantise_w1(3, 0, 2, high_stage)
+        place_allies(3, fourth[:], "enemy0")
+        quantise_w1(3, 2, G1)
+        enemy_rest = held([P, G1 - 1, S], U32, "enemy_rest", "w1_2_2")
+        enemy_words = [enemy_first[:]] + [enemy_rest[:, g - 1, :] for g in range(1, G1)]
         for g in range(1, G1):
-            gather_words(ally_words[:, g, :], tab_tiles[g], ally_list)
-        stage = held([P, STAGE], BF16, "stage", place=f"tab{G1 - 1}")
-        staged, cursor = {}, 0
-        for c in range(1, len(W1_CHUNKS)):
-            size = PACK * W1_CHUNKS[c][1]
-            staged[c] = []
-            if c == len(W1_CHUNKS) - 1:
-                staged[c].append(held([P, size], BF16, "wide_stage", place=f"w1_{2 * P}_1")[:])
-            while len(staged[c]) < G1:
-                cursor = -(-cursor // size) * size % STAGE
-                staged[c].append(stage[:, cursor : cursor + size])
-                cursor = cursor + size
-        staged[3][G1 - 1] = held([P, PACK * K_PASS], BF16, "last_stage", place=f"w1_{2 * P}_0")[:]
+            gather(enemy_words[g], enemy_table[g], enemy_list[:])
+
+        high_values = held([P, PACK, S], F32, "high_values", "ally1")
+        for t in range(PACK):
+            ally_values(PACK + t, high_values[:, t, :])
+        for t, page_place in enumerate(("stage3_0", "enemy1", "w1_2_0")):
+            place_allies(PACK + t, high_values[:, t, :], page_place)
+
+        low_enemies = held([P, PACK, S], F32, "low_enemies", "ally2")
+        high_enemies = held([P, PACK, S], F32, "high_enemies", "ally0")
+        enemies = [tile[:, t, :] for tile in (low_enemies, high_enemies) for t in range(PACK)]
+        for i in range(2 * PACK):
+            enemy_values(i, enemies[i], f"w1_1_{i % 2}", "w1_3_1" if i == 5 else f"w1_0_{i % 2}")
         for i in range(PACK):
-            if i in (1, 2):
-                quantise_w1(i, staged[i])
-            ally_values(i, i, ring[i % RING][:])
-            place_allies(i, ring[i % RING][:])
-        quantise_w1(3, staged[3])
-        enemy_words = held([P, G1, S], U32, "enemy_words", place=f"w1_{2 * P}_0")
-        enemy_planes = gather_planes(tab2_planes, enemy_list, "enemy_planes", place=f"w1_{2 * P}_{G1 - 1}")
-        for g in range(G1):
-            gather_words(enemy_words[:, g, :], tab2_tiles[g], enemy_list)
-        ally_values(4, 4, ring[4 % RING][:])
-        place_allies(4, ring[4 % RING][:])
-        ally_values(5, 5, ring[5 % RING][:])
-        ally_values(6, 6, ring[6 % RING][:])
-        place_allies(5, ring[5 % RING][:])
-        enemy_values(0, 7, ring[7 % RING][:])
-        place_allies(6, ring[6 % RING][:])
+            place_enemies(i, enemies[i])
 
-        by_slot = held([P, PACK, T2], BF16, "by_slot", place=f"w1_{K_PASS}_0")
-        grouped_low = held([P, T2, PACK], BF16, "grouped_low", place=f"w1_{K_PASS}_1")
-        grouped_high = held([P, T2, PACK], BF16, "grouped_high", place=f"tab{G1 - 1}")
-        for i in range(2 * PACK - 1):
-            step = 7 + i
-            if i + 1 < 2 * PACK - 1:
-                enemy_values(i + 1, step + 1, ring[(step + 1) % RING][:])
-            place_enemies(i, ring[step % RING][:])
-            if i < PACK:
-                rounded = held([P, T2], BF16, f"rounded{i}")
-                nc.scalar.activation(rounded[:], pages[i][:], ACT.Copy, scale=gain_low[:, i : i + 1])
-                for t in range(PACK):
-                    nc.sync.dma_start(by_slot[32 * i : 32 * (i + 1), t, :], rounded[t:P:PACK, :])
-                if i == PACK - 1:
-                    for h in range(2):
-                        interleave(grouped_low, by_slot, h, PACK)
-            else:
-                t = i - PACK
-                nc.scalar.activation(by_slot[:, t, :], pages[i][:], ACT.Copy, scale=gain_high[:, t : t + 1])
-
-        def freed(h):
-            return grouped_low[:, h * HALF : h * HALF + S // 2, :].rearrange("p m t -> p (m t)").bitcast(F32)
-
-        last = 2 * PACK - 1
-        quantise_z(0, 0, grouped_low)
-        enemy_values(last, 14, freed(0))
-        quantise_z(0, 1, grouped_low)
-        ally_values(last, 15, freed(1))
-        place_enemies(last, freed(0))
-        interleave(grouped_high, by_slot, 0, PACK)
-        interleave(grouped_high, by_slot, 1, PACK - 1)
+        rounded = held([P, PACK, T2], BF16, "rounded", "w1_3_1")
+        by_slot = held([P, PACK, T2], BF16, "by_slot", "w1_3_2")
+        for i in range(PACK):
+            nc.scalar.activation(rounded[:, i, :], pages[i][:], ACT.Copy, scale=gain_low[:, i : i + 1])
+            for t in range(PACK):
+                nc.sync.dma_start(by_slot[32 * i : 32 * (i + 1), t, :], rounded[t:P:PACK, i, :])
+        grouped_low = held([P, T2, PACK], BF16, "grouped_low", "w1_3_0")
         for h in range(2):
-            second_product(0, h)
-        place_allies(last, freed(1))
+            interleave(grouped_low, h, PACK)
+        for t in range(PACK - 1):
+            place_enemies(PACK + t, enemies[PACK + t])
+            nc.scalar.activation(by_slot[:, t, :], pages[PACK + t][:], ACT.Copy, scale=gain_high[:, t : t + 1])
+
+        low_codes = held([P, T2], U32, "low_codes", "w1_2_1")
+        low_planes = held([P, T2], U8, "low_planes")
+        nc.vector.quantize_mx(
+            out=low_codes[:].bitcast(FP8X4), scales=low_planes[:], in_=grouped_low[:].rearrange("p m t -> p (m t)"),
+        )
+        for h in range(2):
+            second_product(0, h, low_codes, low_planes)
+        grouped_high = held([P, T2, PACK], BF16, "grouped_high", "w1_3_1")
+        interleave(grouped_high, 1, PACK)
+        interleave(grouped_high, 0, PACK)
+        last = 2 * PACK - 1
+        place_allies(last, high_values[:, PACK - 1, :], "w1_3_0")
+        place_enemies(last, enemies[last])
 
         last_gain = gain_high[:, PACK - 1 : PACK]
         nc.vector.tensor_scalar(grouped_high[:, 0:HALF, PACK - 1], pages[last][:, 0:HALF], last_gain, None, ALU.mult)
         nc.scalar.activation(grouped_high[:, HALF:, PACK - 1], pages[last][:, HALF:], ACT.Copy, scale=last_gain)
+        high_codes = held([P, T2], U32, "high_codes")
+        high_planes = held([P, T2], U8, "high_planes")
         for h in range(2):
-            quantise_z(1, h, grouped_high)
-            second_product(1, h)
-        for h in range(2):
-            result = held([P, N // P, HALF], F32, f"result{h}", place=f"tab{h}")
-            for nt in range(N // P):
-                if nt % 2 == 0:
-                    nc.scalar.copy(result[:, nt, :], banks[4 * h + nt][:])
-                else:
-                    nc.vector.tensor_copy(result[:, nt, :], banks[4 * h + nt][:])
-                nc.sync.dma_start(out[nt * P : (nt + 1) * P, h * HALF : (h + 1) * HALF], result[:, nt, :])
+            cols = slice(h * HALF, (h + 1) * HALF)
+            nc.vector.quantize_mx(
+                out=high_codes[:, cols].bitcast(FP8X4), scales=high_planes[:, cols],
+                in_=grouped_high[:, cols, :].rearrange("p m t -> p (m t)"),
+            )
+            second_product(1, h, high_codes, high_planes)
+        by_scalar = held([P, N // P, HALF], F32, "by_scalar", "ally0")
+        by_vector = held([P, N // P, HALF], F32, "by_vector", "w1_3_1")
+        for b, bank in enumerate(banks):
+            h, nt = divmod(b, N // P)
+            if b % 2 == 0:
+                result = by_scalar[:, b // 2, :]
+                nc.scalar.copy(result, bank[:])
+            else:
+                result = by_vector[:, b // 2, :]
+                nc.vector.tensor_copy(result, bank[:])
+            nc.sync.dma_start(out[nt * P : (nt + 1) * P, h * HALF : (h + 1) * HALF], result)

@@ -23,6 +23,7 @@ K_PASS = P * PACK
 G1 = K // K_PASS
 G2 = H // K_PASS
 HALF = 512
+OUT_PIECES = ((0, 128), (128, 128), (256, 128), (384, 128), (512, 512))
 W1_CHUNKS = ((0, 128), (128, 128), (256, 256), (512, 512))
 
 
@@ -91,10 +92,6 @@ def tile_list_turn_order_evaluator_kernel(
         identity = held([P, P], F32, "identity")
         make_identity(nc, identity[:])
 
-        warm = held([P, 2], F32, "warm")
-        nc.vector.memset(warm[:, 0:1], 0.0)
-        nc.scalar.activation(warm[:, 1:2], warm[:, 0:1], ACT.Sigmoid)
-
         ally_list = load_list(offs, "ally_list")
         ally_table = [load_words(tab_words, 0, "ally")]
         w1_raw = [load_w1(0)]
@@ -124,8 +121,6 @@ def tile_list_turn_order_evaluator_kernel(
         threat_high = load_plain(threat[K_PASS:, :].rearrange("(p t) j -> p t j", t=PACK), [P, PACK, S], "threat_high")
         threat_rows.extend(threat_high[:, t, :] for t in range(PACK))
         wg2_slots = load_wg_slots(wg2, 0, PACK, "wg2_slots")
-        w4_codes = held([P, G2, 2 * N], U8, "w4_codes")
-        nc.sync.dma_start(w4_codes[:].bitcast(I32), w4_words.rearrange("a p c -> p a c").bitcast(I32))
         for q in range(4):
             nc.sync.dma_start(
                 w4_planes[32 * q : 32 * q + 4, :, :].bitcast(I32),
@@ -216,22 +211,27 @@ def tile_list_turn_order_evaluator_kernel(
         def place_enemies(i, values):
             place(i, enemy_slots[:], values, enemy_weights[i])
 
-        def second_product(a, h, codes, planes):
-            cols = slice(h * HALF, (h + 1) * HALF)
+        def out_bank(first, width, nt):
+            if width == HALF:
+                return banks[first // P + nt][:]
+            return banks[first // P][:, nt * P : (nt + 1) * P]
+
+        def second_product(a, first, width, codes, planes):
+            cols = slice(first, first + width)
             for nt in range(N // P):
+                whole = width == HALF
                 nc.tensor.matmul_mx(
-                    out=banks[4 * h + nt][:],
+                    out=out_bank(first, width, nt),
                     lhsT=w4_codes[:, a, 2 * P * nt : 2 * P * (nt + 1)].bitcast(FP4X4),
                     lhsT_scale=w4_planes[:, a, P * nt : P * (nt + 1)],
                     rhs=codes[:, cols].bitcast(FP8X4), rhs_scale=planes[:, cols],
-                    start=(a == 0), stop=(a == G2 - 1),
+                    start=(a == 0 and (whole or nt == 0)), stop=(a == G2 - 1 and (whole or nt == N // P - 1)),
                 )
 
-        def interleave(grouped, h, slots):
-            cols = slice(h * HALF, (h + 1) * HALF)
+        def interleave(grouped, cols):
             nc.scalar.copy(
-                grouped[:, cols, 0:slots].rearrange("p (c i) t -> p c t i", i=4),
-                by_slot[:, 0:slots, cols].rearrange("p t (c i) -> p c t i", i=4),
+                grouped.rearrange("p (c i) t -> p c t i", i=4),
+                by_slot[:, :, cols].rearrange("p t (c i) -> p c t i", i=4),
             )
 
         ally_picked = held([P, G1, S], U32, "ally_picked")
@@ -301,45 +301,63 @@ def tile_list_turn_order_evaluator_kernel(
                 nc.sync.dma_start(by_slot[32 * i : 32 * (i + 1), t, :], rounded[t:P:PACK, i, :])
         grouped_low = held([P, T2, PACK], BF16, "grouped_low", "w1_3_0")
         for h in range(2):
-            interleave(grouped_low, h, PACK)
+            cols = slice(h * HALF, (h + 1) * HALF)
+            interleave(grouped_low[:, cols, :], cols)
         for t in range(PACK - 1):
             place_enemies(PACK + t, enemies[PACK + t])
             nc.scalar.activation(by_slot[:, t, :], pages[PACK + t][:], ACT.Copy, scale=gain_high[:, t : t + 1])
 
+        w4_codes = held([P, G2, 2 * N], U8, "w4_codes", "w1_2_0")
+        nc.sync.dma_start(w4_codes[:].bitcast(I32), w4_words.rearrange("a p c -> p a c").bitcast(I32))
         low_codes = held([P, T2], U32, "low_codes", "w1_2_1")
         low_planes = held([P, T2], U8, "low_planes")
         nc.vector.quantize_mx(
             out=low_codes[:].bitcast(FP8X4), scales=low_planes[:], in_=grouped_low[:].rearrange("p m t -> p (m t)"),
         )
-        for h in range(2):
-            second_product(0, h, low_codes, low_planes)
-        grouped_high = held([P, T2, PACK], BF16, "grouped_high", "w1_3_1")
-        interleave(grouped_high, 1, PACK)
-        interleave(grouped_high, 0, PACK)
+        for first, width in sorted(OUT_PIECES, key=lambda piece: -piece[1]):
+            second_product(0, first, width, low_codes, low_planes)
+        lead, rest, wide = slice(0, P), slice(P, HALF), slice(HALF, T2)
+        grouped_high = {}
+        for cols, spot in ((wide, "w1_3_1"), (rest, "w1_2_2"), (lead, "w1_1_0")):
+            tile = held([P, cols.stop - cols.start, PACK], BF16, f"grouped_high{cols.start}", spot)
+            interleave(tile[:], cols)
+            grouped_high[cols.start] = tile
         last = 2 * PACK - 1
         place_allies(last, high_values[:, PACK - 1, :], "w1_3_0")
         place_enemies(last, enemies[last])
 
         last_gain = gain_high[:, PACK - 1 : PACK]
-        nc.vector.tensor_scalar(grouped_high[:, 0:HALF, PACK - 1], pages[last][:, 0:HALF], last_gain, None, ALU.mult)
-        nc.scalar.activation(grouped_high[:, HALF:, PACK - 1], pages[last][:, HALF:], ACT.Copy, scale=last_gain)
         high_codes = held([P, T2], U32, "high_codes")
         high_planes = held([P, T2], U8, "high_planes")
-        for h in range(2):
-            cols = slice(h * HALF, (h + 1) * HALF)
+
+        def round_last(cols):
+            nc.vector.tensor_scalar(grouped_high[cols.start][:, :, PACK - 1], pages[last][:, cols], last_gain, None, ALU.mult)
+
+        def quantise_high(piece, first, stop):
             nc.vector.quantize_mx(
-                out=high_codes[:, cols].bitcast(FP8X4), scales=high_planes[:, cols],
-                in_=grouped_high[:, cols, :].rearrange("p m t -> p (m t)"),
+                out=high_codes[:, first:stop].bitcast(FP8X4), scales=high_planes[:, first:stop],
+                in_=grouped_high[piece.start][:, first - piece.start : stop - piece.start, :].rearrange("p m t -> p (m t)"),
             )
-            second_product(1, h, high_codes, high_planes)
-        by_scalar = held([P, N // P, HALF], F32, "by_scalar", "ally0")
-        by_vector = held([P, N // P, HALF], F32, "by_vector", "w1_3_1")
+
+        nc.scalar.activation(grouped_high[wide.start][:, :, PACK - 1], pages[last][:, wide], ACT.Copy, scale=last_gain)
+        round_last(lead)
+        round_last(rest)
+        quantise_high(lead, 0, P)
+        quantise_high(rest, P, 2 * P)
+        quantise_high(rest, 2 * P, HALF)
+        quantise_high(wide, HALF, T2)
+        for first, width in OUT_PIECES:
+            second_product(1, first, width, high_codes, high_planes)
+
+        results = held([P, len(banks), HALF], F32, "results")
+        places = [out.rearrange("(n p) m -> p n m", p=P)[:, :, first : first + width] for first, width in OUT_PIECES]
+        places[4:5] = [places[4][:, nt, :] for nt in range(N // P)]
         for b, bank in enumerate(banks):
-            h, nt = divmod(b, N // P)
-            if b % 2 == 0:
-                result = by_scalar[:, b // 2, :]
-                nc.scalar.copy(result, bank[:])
-            else:
-                result = by_vector[:, b // 2, :]
+            result = results[:, b, :]
+            if b in (2, 4, 6):
                 nc.vector.tensor_copy(result, bank[:])
-            nc.sync.dma_start(out[nt * P : (nt + 1) * P, h * HALF : (h + 1) * HALF], result)
+            else:
+                nc.scalar.copy(result, bank[:])
+            if b < 4:
+                result = result.rearrange("p (n m) -> p n m", m=P)
+            nc.sync.dma_start(places[b], result)

@@ -120,7 +120,9 @@ def tile_list_turn_order_evaluator_kernel(
         gain_high = load_plain(gain[K_PASS:].rearrange("(p t) -> p t", t=PACK), [P, PACK], "gain_high")
         threat_high = load_plain(threat[K_PASS:, :].rearrange("(p t) j -> p t j", t=PACK), [P, PACK, S], "threat_high")
         threat_rows.extend(threat_high[:, t, :] for t in range(PACK))
-        wg2_slots = load_wg_slots(wg2, 0, PACK, "wg2_slots")
+        wg2_slots = load_wg_slots(wg2, 0, PACK - 1, "wg2_slots")
+        w4_codes = held([P, G2, 2 * N], U8, "w4_codes")
+        nc.sync.dma_start(w4_codes[:].bitcast(I32), w4_words.rearrange("a p c -> p a c").bitcast(I32))
         for q in range(4):
             nc.sync.dma_start(
                 w4_planes[32 * q : 32 * q + 4, :, :].bitcast(I32),
@@ -228,10 +230,10 @@ def tile_list_turn_order_evaluator_kernel(
                     start=(a == 0 and (whole or nt == 0)), stop=(a == G2 - 1 and (whole or nt == N // P - 1)),
                 )
 
-        def interleave(grouped, cols):
+        def interleave(grouped, first, cols):
             nc.scalar.copy(
                 grouped.rearrange("p (c i) t -> p c t i", i=4),
-                by_slot[:, :, cols].rearrange("p t (c i) -> p c t i", i=4),
+                by_slot[:, first : first + PACK, cols].rearrange("p t (c i) -> p c t i", i=4),
             )
 
         ally_picked = held([P, G1, S], U32, "ally_picked")
@@ -279,8 +281,8 @@ def tile_list_turn_order_evaluator_kernel(
         for g in range(1, G1):
             gather(enemy_words[g], enemy_table[g], enemy_list[:])
 
-        high_values = held([P, PACK, S], F32, "high_values", "ally1")
-        for t in range(PACK):
+        high_values = held([P, PACK - 1, S], F32, "high_values", "ally1")
+        for t in range(PACK - 1):
             ally_values(PACK + t, high_values[:, t, :])
         for t, page_place in enumerate(("stage3_0", "enemy1", "w1_2_0")):
             place_allies(PACK + t, high_values[:, t, :], page_place)
@@ -290,25 +292,31 @@ def tile_list_turn_order_evaluator_kernel(
         enemies = [tile[:, t, :] for tile in (low_enemies, high_enemies) for t in range(PACK)]
         for i in range(2 * PACK):
             enemy_values(i, enemies[i], f"w1_1_{i % 2}", "w1_3_1" if i == 5 else f"w1_0_{i % 2}")
+        eighth = held([P, S], F32, "eighth", "w1_0_0")
+        ally_values(2 * PACK - 1, eighth[:])
         for i in range(PACK):
             place_enemies(i, enemies[i])
 
         rounded = held([P, PACK, T2], BF16, "rounded", "w1_3_1")
-        by_slot = held([P, PACK, T2], BF16, "by_slot", "w1_3_2")
+        by_slot = held([P, PACK + 1, T2], BF16, "by_slot", "w1_3_2")
         for i in range(PACK):
             nc.scalar.activation(rounded[:, i, :], pages[i][:], ACT.Copy, scale=gain_low[:, i : i + 1])
             for t in range(PACK):
-                nc.sync.dma_start(by_slot[32 * i : 32 * (i + 1), t, :], rounded[t:P:PACK, i, :])
+                nc.sync.dma_start(by_slot[32 * i : 32 * (i + 1), t + 1, :], rounded[t:P:PACK, i, :])
         grouped_low = held([P, T2, PACK], BF16, "grouped_low", "w1_3_0")
         for h in range(2):
             cols = slice(h * HALF, (h + 1) * HALF)
-            interleave(grouped_low[:, cols, :], cols)
+            interleave(grouped_low[:, cols, :], 1, cols)
         for t in range(PACK - 1):
             place_enemies(PACK + t, enemies[PACK + t])
             nc.scalar.activation(by_slot[:, t, :], pages[PACK + t][:], ACT.Copy, scale=gain_high[:, t : t + 1])
 
-        w4_codes = held([P, G2, 2 * N], U8, "w4_codes", "w1_2_0")
-        nc.sync.dma_start(w4_codes[:].bitcast(I32), w4_words.rearrange("a p c -> p a c").bitcast(I32))
+        last = 2 * PACK - 1
+        place_allies(last, eighth[:], "enemy2")
+        last_weights = held([P, S], F32, "last_weights", "enemy1")
+        for q in range(4):
+            nc.sync.dma_start(last_weights[32 * q : 32 * (q + 1), :], wg2.rearrange("(q t) j -> q t j", t=PACK)[:, PACK - 1, :])
+        enemy_weights.append(last_weights[:])
         low_codes = held([P, T2], U32, "low_codes", "w1_2_1")
         low_planes = held([P, T2], U8, "low_planes")
         nc.vector.quantize_mx(
@@ -320,10 +328,8 @@ def tile_list_turn_order_evaluator_kernel(
         grouped_high = {}
         for cols, spot in ((wide, "w1_3_1"), (rest, "w1_2_2"), (lead, "w1_1_0")):
             tile = held([P, cols.stop - cols.start, PACK], BF16, f"grouped_high{cols.start}", spot)
-            interleave(tile[:], cols)
+            interleave(tile[:], 0, cols)
             grouped_high[cols.start] = tile
-        last = 2 * PACK - 1
-        place_allies(last, high_values[:, PACK - 1, :], "w1_3_0")
         place_enemies(last, enemies[last])
 
         last_gain = gain_high[:, PACK - 1 : PACK]

@@ -145,11 +145,10 @@ def tile_list_turn_order_evaluator_kernel(
                     w1_raw[c][g][:].rearrange("p j (c i) -> p c j i", i=4),
                 )
             else:
-                for rows in (slice(0, P // 2), slice(P // 2, P)):
-                    nc.scalar.copy(
-                        grouped.rearrange("p (t m j) -> p m j t", t=PACK, j=PACK)[:, rows],
-                        w1_raw[c][g][:].rearrange("p j (m t) -> p m j t", t=PACK)[:, rows],
-                    )
+                nc.scalar.copy(
+                    grouped.rearrange("p (t m j) -> p m j t", t=PACK, j=PACK),
+                    w1_raw[c][g][:].rearrange("p j (m t) -> p m j t", t=PACK),
+                )
 
         def stage_w1(c, lo, hi):
             size = PACK * W1_CHUNKS[c][1]
@@ -355,15 +354,20 @@ def tile_list_turn_order_evaluator_kernel(
         for first, width in OUT_PIECES:
             second_product(1, first, width, high_codes, high_planes)
 
-        results = held([P, len(banks), HALF], F32, "results")
-        places = [out.rearrange("(n p) m -> p n m", p=P)[:, :, first : first + width] for first, width in OUT_PIECES]
-        places[4:5] = [places[4][:, nt, :] for nt in range(N // P)]
+        by_row_tile = out.rearrange("(n p) m -> p n m", p=P)
+        results = held([P, N // P, T2], F32, "results")
         for b, bank in enumerate(banks):
-            result = results[:, b, :]
-            if b in (2, 4, 6):
-                nc.vector.tensor_copy(result, bank[:])
-            else:
-                nc.scalar.copy(result, bank[:])
             if b < 4:
-                result = result.rearrange("p (n m) -> p n m", m=P)
-            nc.sync.dma_start(places[b], result)
+                result, source = results[:, :, b * P : (b + 1) * P], bank[:].rearrange("p (n m) -> p n m", m=P)
+            else:
+                result, source = results[:, b - 4, HALF:], bank[:]
+            if b in (2, 4, 6):
+                nc.vector.tensor_copy(result, source)
+            else:
+                nc.scalar.copy(result, source)
+            if b < 2:
+                nc.sync.dma_start(by_row_tile[:, :, b * P : (b + 1) * P], result)
+            elif b == 3:
+                nc.sync.dma_start(by_row_tile[:, :, 2 * P : HALF], results[:, :, 2 * P : HALF])
+            elif b % 2 == 1:
+                nc.sync.dma_start(by_row_tile[:, b - 5 : b - 3, HALF:], results[:, b - 5 : b - 3, HALF:])

@@ -19,12 +19,18 @@ ACT = mybir.ActivationFunctionType
 
 P = 128
 PACK = 4
+QUADRANTS = 4
 K_PASS = P * PACK
-G1 = K // K_PASS
-G2 = H // K_PASS
-HALF = 512
-OUT_PIECES = ((0, 128), (128, 128), (256, 128), (384, 128), (512, 512))
+K_PASSES = K // K_PASS
+R_PASSES = H // K_PASS
+BANK = 512
+TILES = H // P
+LAST = TILES - 1
+ROW_TILES = N // P
 W1_CHUNKS = ((0, 128), (128, 128), (256, 256), (512, 512))
+HIGH_CHUNK = len(W1_CHUNKS) - 1
+OUT_PIECES = ((0, 128), (128, 128), (256, 128), (384, 128), (512, 512))
+NARROW_BANKS = len(OUT_PIECES) - 1
 
 
 def tile_list_turn_order_evaluator_kernel(
@@ -56,10 +62,11 @@ def tile_list_turn_order_evaluator_kernel(
             return tile
 
         def load_table_scales(queue, tile, src):
-            for q in range(4):
-                queue.dma_start(tile[32 * q : 32 * q + 4 * G1, :].bitcast(I32), src[:, 4 * q : 4 * q + 4, :].bitcast(I32))
+            for q in range(QUADRANTS):
+                rows = tile[32 * q : 32 * q + 4 * K_PASSES, :]
+                queue.dma_start(rows.bitcast(I32), src[:, 4 * q : 4 * q + 4, :].bitcast(I32))
 
-        def load_w1(c, lo=0, hi=G1):
+        def load_w1(c, lo=0, hi=K_PASSES):
             first, width = W1_CHUNKS[c]
             tiles = []
             for g in range(lo, hi):
@@ -69,24 +76,23 @@ def tile_list_turn_order_evaluator_kernel(
                 tiles.append(tile)
             return tiles
 
-        def load_wg_slots(src, t0, t1, name):
-            tile = held([P, t1 - t0, S], F32, name)
+        def load_high_weights(target, src, t0, t1):
             rows = src.rearrange("(q t) j -> q t j", t=PACK)[:, t0:t1, :]
-            for q in range(4):
-                nc.sync.dma_start(tile[32 * q : 32 * (q + 1), :, :], rows)
-            return [tile[:, t, :] for t in range(t1 - t0)]
+            for q in range(QUADRANTS):
+                nc.sync.dma_start(target[32 * q : 32 * (q + 1), :, :], rows)
+            return [target[:, t, :] for t in range(t1 - t0)]
 
         def load_plain(src, shape, name):
             tile = held(shape, F32, name)
             nc.sync.dma_start(tile[:], src)
             return tile
 
-        def load_threat(b):
-            return load_plain(threat[b * P : (b + 1) * P, :], [P, S], f"threat{b}")[:]
+        def load_low_threat(i):
+            return load_plain(threat[i * P : (i + 1) * P, :], [P, S], f"threat{i}")[:]
 
         ally_scales = cleared([P, T], "ally_scales")
         enemy_scales = cleared([P, T], "enemy_scales")
-        w4_planes = cleared([P, G2, N], "w4_planes")
+        w4_planes = cleared([P, R_PASSES, N], "w4_planes")
         load_table_scales(nc.scalar, ally_scales, tab_scales)
         load_table_scales(nc.gpsimd, enemy_scales, tab2_scales)
         identity = held([P, P], F32, "identity")
@@ -95,7 +101,7 @@ def tile_list_turn_order_evaluator_kernel(
         ally_list = load_list(offs, "ally_list")
         ally_table = [load_words(tab_words, 0, "ally")]
         w1_raw = [load_w1(0)]
-        ally_table.extend(load_words(tab_words, g, "ally") for g in range(1, G1))
+        ally_table.extend(load_words(tab_words, g, "ally") for g in range(1, K_PASSES))
         wg1_rows = held([P, S], F32, "wg1_rows")
         nc.sync.dma_start(wg1_rows[:, 0 : S // 2], wg1[:, 0 : S // 2])
         ally_slots = load_list(offs3, "ally_slots")
@@ -103,63 +109,60 @@ def tile_list_turn_order_evaluator_kernel(
         nc.sync.dma_start(wg1_rows[:, S // 2 :], wg1[:, S // 2 :])
         w1_raw.append(load_w1(2, 0, 1))
         enemy_list = load_list(offs2, "enemy_list")
-        w1_raw[2].extend(load_w1(2, 1, G1))
-        w1_raw.append(load_w1(3, 0, 1))
+        w1_raw[2].extend(load_w1(2, 1, K_PASSES))
+        w1_raw.append(load_w1(HIGH_CHUNK, 0, 1))
         enemy_table = [load_words(tab2_words, 0, "enemy")]
-        w1_raw[3].extend(load_w1(3, 1, G1))
-        threat_rows = [load_threat(0)]
-        enemy_table.extend(load_words(tab2_words, g, "enemy") for g in range(1, G1))
-        wg1_slots = load_wg_slots(wg1, 0, 1, "wg1_first")
-        wg1_slots.extend(load_wg_slots(wg1, 1, PACK, "wg1_rest"))
+        w1_raw[HIGH_CHUNK].extend(load_w1(HIGH_CHUNK, 1, K_PASSES))
+        threat_rows = [load_low_threat(0)]
+        enemy_table.extend(load_words(tab2_words, g, "enemy") for g in range(1, K_PASSES))
+        wg1_high = load_high_weights(held([P, 1, S], F32, "wg1_slot0"), wg1, 0, 1)
+        wg1_high.extend(load_high_weights(held([P, PACK - 1, S], F32, "wg1_slots"), wg1, 1, PACK))
         enemy_slots = load_list(offs4, "enemy_slots")
         wg2_rows = load_plain(wg2, [P, S], "wg2_rows")
-        threat_rows.extend(load_threat(b) for b in range(1, PACK))
+        threat_rows.extend(load_low_threat(i) for i in range(1, PACK))
         gain_low = held([P, PACK], F32, "gain_low")
-        with nc.allow_non_contiguous_dma(reason="one gain a partition and row tile"):
-            nc.sync.dma_start(gain_low[:], gain[0:K_PASS].rearrange("(b p) -> p b", p=P))
+        with nc.allow_non_contiguous_dma(reason="one gain a partition and low tile"):
+            nc.sync.dma_start(gain_low[:], gain[0:K_PASS].rearrange("(i p) -> p i", p=P))
         gain_high = load_plain(gain[K_PASS:].rearrange("(p t) -> p t", t=PACK), [P, PACK], "gain_high")
         threat_high = load_plain(threat[K_PASS:, :].rearrange("(p t) j -> p t j", t=PACK), [P, PACK, S], "threat_high")
         threat_rows.extend(threat_high[:, t, :] for t in range(PACK))
-        wg2_slots = load_wg_slots(wg2, 0, PACK - 1, "wg2_slots")
-        w4_codes = held([P, G2, 2 * N], U8, "w4_codes")
+        wg2_high = load_high_weights(held([P, PACK - 1, S], F32, "wg2_slots"), wg2, 0, PACK - 1)
+        w4_codes = held([P, R_PASSES, 2 * N], U8, "w4_codes")
         nc.sync.dma_start(w4_codes[:].bitcast(I32), w4_words.rearrange("a p c -> p a c").bitcast(I32))
-        for q in range(4):
+        for q in range(QUADRANTS):
             nc.sync.dma_start(
                 w4_planes[32 * q : 32 * q + 4, :, :].bitcast(I32),
-                w4_scales[:, 4 * q : 4 * q + 4, :].rearrange("a r n -> r a n").bitcast(I32),
+                w4_scales[:, 4 * q : 4 * q + 4, :].rearrange("a s n -> s a n").bitcast(I32),
             )
 
-        ally_weights = [wg1_rows[:]] * PACK + wg1_slots
-        enemy_weights = [wg2_rows[:]] * PACK + wg2_slots
-        banks = [psum.tile([P, HALF], F32, name=f"bank{i}") for i in range(8)]
+        ally_weights = [wg1_rows[:]] * PACK + wg1_high
+        enemy_weights = [wg2_rows[:]] * PACK + wg2_high
+        banks = [psum.tile([P, BANK], F32, name=f"bank{b}") for b in range(8)]
         pages = {}
         w1_codes, w1_planes = {}, {}
 
-        def gather(picked, tile, offsets):
-            nc.vector.tensor_copy(picked, tile[:].indirect(offsets))
+        def gather(picked, window, offsets):
+            nc.vector.tensor_copy(picked, window[:].indirect(offsets))
 
-        def round_w1(c, g, grouped):
-            if W1_CHUNKS[c][0] < K_PASS:
-                nc.scalar.copy(
-                    grouped.rearrange("p (c i j) -> p c j i", i=4, j=PACK),
-                    w1_raw[c][g][:].rearrange("p j (c i) -> p c j i", i=4),
-                )
-            else:
-                nc.scalar.copy(
-                    grouped.rearrange("p (t m j) -> p m j t", t=PACK, j=PACK),
-                    w1_raw[c][g][:].rearrange("p j (m t) -> p m j t", t=PACK),
-                )
-
-        def stage_w1(c, lo, hi):
+        def group_w1(c, lo, hi):
             size = PACK * W1_CHUNKS[c][1]
-            stage = held([P, (hi - lo) * size], BF16, f"stage{c}_{lo}")
+            staged = held([P, (hi - lo) * size], BF16, f"staged{c}_{lo}")
             for g in range(lo, hi):
-                round_w1(c, g, stage[:, (g - lo) * size : (g - lo + 1) * size])
-            return stage
+                grouped = staged[:, (g - lo) * size : (g - lo + 1) * size]
+                if c < HIGH_CHUNK:
+                    nc.scalar.copy(
+                        grouped.rearrange("p (c i j) -> p c j i", i=4, j=PACK),
+                        w1_raw[c][g][:].rearrange("p j (c i) -> p c j i", i=4),
+                    )
+                else:
+                    nc.scalar.copy(
+                        grouped.rearrange("p (t m j) -> p m j t", t=PACK, j=PACK),
+                        w1_raw[c][g][:].rearrange("p j (m t) -> p m j t", t=PACK),
+                    )
+            return staged
 
-        def quantise_w1(c, lo, hi, stage=None):
+        def quantise_w1(c, lo, hi, staged):
             first, width = W1_CHUNKS[c]
-            stage = stage_w1(c, lo, hi) if stage is None else stage
             codes = held([P, (hi - lo) * width], U32, f"w1_codes{c}_{lo}")
             planes = held([P, (hi - lo) * width], U8, f"w1_planes{c}_{lo}")
             for g in range(lo, hi):
@@ -167,207 +170,208 @@ def tile_list_turn_order_evaluator_kernel(
                     cols = slice((g - lo) * width + u * P, (g - lo) * width + (u + 1) * P)
                     w1_codes[first // P + u, g] = codes[:, cols]
                     w1_planes[first // P + u, g] = planes[:, cols]
-            nc.vector.quantize_mx(out=codes[:].bitcast(FP8X4), scales=planes[:], in_=stage[:])
+            nc.vector.quantize_mx(out=codes[:].bitcast(FP8X4), scales=planes[:], in_=staged[:])
 
-        def first_product(i, words, planes, bank, cols):
-            for g in range(G1):
+        def quantise_early_passes(c):
+            quantise_w1(c, 0, 2, group_w1(c, 0, 2))
+
+        def quantise_last_pass(c):
+            quantise_w1(c, 2, K_PASSES, group_w1(c, 2, K_PASSES))
+
+        def first_product(i, words, planes, sums, cols):
+            for g in range(K_PASSES):
                 nc.tensor.matmul_mx(
-                    out=bank, lhsT=w1_codes[i, g].bitcast(FP8X4), lhsT_scale=w1_planes[i, g],
+                    out=sums, lhsT=w1_codes[i, g].bitcast(FP8X4), lhsT_scale=w1_planes[i, g],
                     rhs=words[g][:, cols].bitcast(FP8X4), rhs_scale=planes[4 * g :, cols],
-                    start=(g == 0), stop=(g == G1 - 1),
+                    start=(g == 0), stop=(g == K_PASSES - 1),
                 )
 
-        every = slice(0, S)
+        all_entries = slice(0, S)
 
         def ally_values(i, values):
-            bank = banks[i % 2]
-            first_product(i, ally_words, ally_planes, bank[:], every)
-            nc.scalar.activation(values, bank[:], ACT.Sigmoid)
+            sums = banks[i % 2]
+            first_product(i, ally_words, ally_planes, sums[:], all_entries)
+            nc.scalar.activation(values, sums[:], ACT.Sigmoid)
 
         def enemy_values(i, values, negated_place, turned_place):
             sums, turned_sums, back = banks[2 + i % 2], banks[4 + i % 2], banks[6 + i % 2]
-            first_product(i, enemy_words, enemy_planes, sums[:], every)
+            first_product(i, enemy_words, enemy_planes, sums[:], all_entries)
             negated = held([P, S], F32, f"negated{i}", negated_place)
             nc.scalar.activation(negated[:], sums[:], ACT.Copy, scale=-1.0)
-            blocks = [slice(c * P, (c + 1) * P) for c in range(S // P)]
-            terms = [(threat_rows[i], b) for b in blocks] + [(negated[:], b) for b in blocks]
-            for n, (term, b) in enumerate(terms):
+            squares = [slice(c * P, (c + 1) * P) for c in range(S // P)]
+            terms = [(threat_rows[i], sq) for sq in squares] + [(negated[:], sq) for sq in squares]
+            for n, (term, sq) in enumerate(terms):
                 nc.tensor.matmul(
-                    turned_sums[:, b], lhsT=term[:, b], rhs=identity[:], is_transpose=True,
+                    turned_sums[:, sq], lhsT=term[:, sq], rhs=identity[:], is_transpose=True,
                     start=(n == 0), stop=(n == len(terms) - 1),
                 )
             turned = held([P, S], F32, f"turned{i}", turned_place)
             nc.scalar.activation(turned[:], turned_sums[:], ACT.Relu, scale=-1.0)
-            for b in blocks:
-                nc.tensor.transpose(back[:, b], turned[:, b], identity[:])
+            for sq in squares:
+                nc.tensor.transpose(back[:, sq], turned[:, sq], identity[:])
             nc.scalar.copy(values, back[:])
 
-        def place(i, slots, values, weights):
-            nc.vector.tensor_tensor(pages[i][:].indirect(slots), values, weights, ALU.mult)
+        def scatter(i, offsets, values, weights):
+            nc.vector.tensor_tensor(pages[i][:].indirect(offsets), values, weights, ALU.mult)
 
         def place_allies(i, values, page_place):
             pages[i] = held([P, T2], F32, f"page{i}", page_place)
-            place(i, ally_slots[:], values, ally_weights[i])
+            scatter(i, ally_slots[:], values, ally_weights[i])
 
-        def place_enemies(i, values):
-            place(i, enemy_slots[:], values, enemy_weights[i])
+        def place_enemies(i):
+            scatter(i, enemy_slots[:], enemies[i], enemy_weights[i])
 
-        def out_bank(first, width, nt):
-            if width == HALF:
-                return banks[first // P + nt][:]
-            return banks[first // P][:, nt * P : (nt + 1) * P]
-
-        def second_product(a, first, width, codes, planes):
+        def last_product(a, first, width, codes, planes):
             cols = slice(first, first + width)
-            for nt in range(N // P):
-                whole = width == HALF
+            wide_piece = width == BANK
+            for nt in range(ROW_TILES):
+                sums = banks[first // P + nt][:] if wide_piece else banks[first // P][:, nt * P : (nt + 1) * P]
                 nc.tensor.matmul_mx(
-                    out=out_bank(first, width, nt),
+                    out=sums,
                     lhsT=w4_codes[:, a, 2 * P * nt : 2 * P * (nt + 1)].bitcast(FP4X4),
                     lhsT_scale=w4_planes[:, a, P * nt : P * (nt + 1)],
                     rhs=codes[:, cols].bitcast(FP8X4), rhs_scale=planes[:, cols],
-                    start=(a == 0 and (whole or nt == 0)), stop=(a == G2 - 1 and (whole or nt == N // P - 1)),
+                    start=(a == 0 and (wide_piece or nt == 0)),
+                    stop=(a == R_PASSES - 1 and (wide_piece or nt == ROW_TILES - 1)),
                 )
 
-        def interleave(grouped, first, cols):
+        def group_z(grouped, first_row, cols):
             nc.scalar.copy(
                 grouped.rearrange("p (c i) t -> p c t i", i=4),
-                by_slot[:, first : first + PACK, cols].rearrange("p t (c i) -> p c t i", i=4),
+                by_slot[:, first_row : first_row + PACK, cols].rearrange("p t (c i) -> p c t i", i=4),
             )
 
-        ally_picked = held([P, G1, S], U32, "ally_picked")
-        ally_words = [ally_picked[:, g, :] for g in range(G1)]
+        ally_picked = held([P, K_PASSES, S], U32, "ally_picked")
+        ally_words = [ally_picked[:, g, :] for g in range(K_PASSES)]
         ally_planes = held([P, S], U8, "ally_planes")
         gather(ally_words[0], ally_table[0], ally_list[:])
         gather(ally_planes[:], ally_scales, ally_list[:])
-        quantise_w1(0, 0, 2)
-        quantise_w1(0, 2, G1)
+        quantise_early_passes(0)
+        quantise_last_pass(0)
         gather(ally_words[1], ally_table[1], ally_list[:])
-        low_allies = held([P, 1, S], F32, "low_allies", "ally0")
+        allies0 = held([P, S], F32, "allies0", "ally0")
         pages[0] = held([P, T2], F32, "page0")
         halves = [(slice(h * S // 2, (h + 1) * S // 2), slice(h * S // 32, (h + 1) * S // 32)) for h in range(2)]
-        for cols, entries in halves:
-            gather(ally_words[2][:, cols], ally_table[2], ally_list[:, entries])
-        for h, (cols, entries) in enumerate(halves):
-            first_product(0, ally_words, ally_planes, banks[h][:, 0 : S // 2], cols)
-            nc.scalar.activation(low_allies[:, 0, cols], banks[h][:, 0 : S // 2], ACT.Sigmoid)
-        for cols, entries in halves:
-            place(0, ally_slots[:, entries], low_allies[:, 0, cols], wg1_rows[:, cols])
+        for entries, list_cols in halves:
+            gather(ally_words[2][:, entries], ally_table[2], ally_list[:, list_cols])
+        for h, (entries, list_cols) in enumerate(halves):
+            first_product(0, ally_words, ally_planes, banks[h][:, 0 : S // 2], entries)
+            nc.scalar.activation(allies0[:, entries], banks[h][:, 0 : S // 2], ACT.Sigmoid)
+        for entries, list_cols in halves:
+            scatter(0, ally_slots[:, list_cols], allies0[:, entries], wg1_rows[:, entries])
 
-        quantise_w1(1, 0, 2)
-        quantise_w1(1, 2, G1)
+        quantise_early_passes(1)
+        quantise_last_pass(1)
         enemy_planes = held([P, S], U8, "enemy_planes")
         gather(enemy_planes[:], enemy_scales, enemy_list[:])
-        quantise_w1(2, 0, 2)
-        second = held([P, S], F32, "second", "w1_2_1")
-        ally_values(1, second[:])
-        place_allies(1, second[:], "enemy_scales")
+        quantise_early_passes(2)
+        allies1 = held([P, S], F32, "allies1", "w1_2_1")
+        ally_values(1, allies1[:])
+        place_allies(1, allies1[:], "enemy_scales")
 
-        quantise_w1(2, 2, G1)
+        quantise_last_pass(2)
         enemy_first = held([P, S], U32, "enemy_first", "w1_1_2")
         gather(enemy_first[:], enemy_table[0], enemy_list[:])
-        high_stage = stage_w1(3, 0, 2)
-        third = held([P, S], F32, "third", "w1_3_0")
-        ally_values(2, third[:])
-        place_allies(2, third[:], "stage2_0")
-        fourth = held([P, S], F32, "fourth", "w1_3_1")
-        ally_values(3, fourth[:])
-        quantise_w1(3, 0, 2, high_stage)
-        place_allies(3, fourth[:], "enemy0")
-        quantise_w1(3, 2, G1)
-        enemy_rest = held([P, G1 - 1, S], U32, "enemy_rest", "w1_2_2")
-        enemy_words = [enemy_first[:]] + [enemy_rest[:, g - 1, :] for g in range(1, G1)]
-        for g in range(1, G1):
+        high_staged = group_w1(HIGH_CHUNK, 0, 2)
+        allies2 = held([P, S], F32, "allies2", "w1_3_0")
+        ally_values(2, allies2[:])
+        place_allies(2, allies2[:], "staged2_0")
+        allies3 = held([P, S], F32, "allies3", "w1_3_1")
+        ally_values(3, allies3[:])
+        quantise_w1(HIGH_CHUNK, 0, 2, high_staged)
+        place_allies(3, allies3[:], "enemy0")
+        quantise_last_pass(HIGH_CHUNK)
+        enemy_rest = held([P, K_PASSES - 1, S], U32, "enemy_rest", "w1_2_2")
+        enemy_words = [enemy_first[:]] + [enemy_rest[:, g - 1, :] for g in range(1, K_PASSES)]
+        for g in range(1, K_PASSES):
             gather(enemy_words[g], enemy_table[g], enemy_list[:])
 
-        high_values = held([P, PACK - 1, S], F32, "high_values", "ally1")
+        high_allies = held([P, PACK - 1, S], F32, "high_allies", "ally1")
         for t in range(PACK - 1):
-            ally_values(PACK + t, high_values[:, t, :])
-        for t, page_place in enumerate(("stage3_0", "enemy1", "w1_2_0")):
-            place_allies(PACK + t, high_values[:, t, :], page_place)
+            ally_values(PACK + t, high_allies[:, t, :])
+        for t, page_place in enumerate(("staged3_0", "enemy1", "w1_2_0")):
+            place_allies(PACK + t, high_allies[:, t, :], page_place)
 
         low_enemies = held([P, PACK, S], F32, "low_enemies", "ally2")
         high_enemies = held([P, PACK, S], F32, "high_enemies", "ally0")
         enemies = [tile[:, t, :] for tile in (low_enemies, high_enemies) for t in range(PACK)]
-        for i in range(2 * PACK):
-            enemy_values(i, enemies[i], f"w1_1_{i % 2}", "w1_3_1" if i == 5 else f"w1_0_{i % 2}")
-        eighth = held([P, S], F32, "eighth", "w1_0_0")
-        ally_values(2 * PACK - 1, eighth[:])
+        gains_wait_for, rounded_place = PACK + 1, "w1_3_1"
+        for i in range(TILES):
+            turned_place = rounded_place if i == gains_wait_for else f"w1_0_{i % 2}"
+            enemy_values(i, enemies[i], f"w1_1_{i % 2}", turned_place)
+        last_allies = held([P, S], F32, "last_allies", "w1_0_0")
+        ally_values(LAST, last_allies[:])
         for i in range(PACK):
-            place_enemies(i, enemies[i])
+            place_enemies(i)
 
-        rounded = held([P, PACK, T2], BF16, "rounded", "w1_3_1")
-        by_slot = held([P, PACK + 1, T2], BF16, "by_slot", "w1_3_2")
+        rounded = held([P, PACK, T2], BF16, "rounded", rounded_place)
+        slot_rows = held([P, (PACK + 1) * T2 + T2 // 2], BF16, "slot_rows", "w1_3_2")
+        by_slot = slot_rows[:, 0 : (PACK + 1) * T2].rearrange("p (t m) -> p t m", m=T2)
         for i in range(PACK):
             nc.scalar.activation(rounded[:, i, :], pages[i][:], ACT.Copy, scale=gain_low[:, i : i + 1])
-            for t in range(PACK):
-                nc.sync.dma_start(by_slot[32 * i : 32 * (i + 1), t + 1, :], rounded[t:P:PACK, i, :])
+            nc.sync.dma_start(by_slot[32 * i : 32 * (i + 1), 1:, :], rounded[:, i, :])
+        left, right = slice(0, T2 // 2), slice(T2 // 2, T2)
         grouped_low = held([P, T2, PACK], BF16, "grouped_low", "w1_3_0")
-        for h in range(2):
-            cols = slice(h * HALF, (h + 1) * HALF)
-            interleave(grouped_low[:, cols, :], 1, cols)
-        for t in range(PACK - 1):
-            place_enemies(PACK + t, enemies[PACK + t])
-            nc.scalar.activation(by_slot[:, t, :], pages[PACK + t][:], ACT.Copy, scale=gain_high[:, t : t + 1])
+        group_z(grouped_low[:, right, :], 1, right)
+        last_weights = slot_rows[:, PACK * T2 + T2 // 2 :].bitcast(F32).rearrange("p (t j) -> p t j", t=1)
+        enemy_weights.extend(load_high_weights(last_weights, wg2, PACK - 1, PACK))
+        group_z(grouped_low[:, left, :], 1, left)
 
-        last = 2 * PACK - 1
-        place_allies(last, eighth[:], "enemy2")
-        last_weights = held([P, S], F32, "last_weights", "enemy1")
-        for q in range(4):
-            nc.sync.dma_start(last_weights[32 * q : 32 * (q + 1), :], wg2.rearrange("(q t) j -> q t j", t=PACK)[:, PACK - 1, :])
-        enemy_weights.append(last_weights[:])
+        for t in range(PACK - 1):
+            place_enemies(PACK + t)
+            nc.scalar.activation(by_slot[:, t, :], pages[PACK + t][:], ACT.Copy, scale=gain_high[:, t : t + 1])
+        place_allies(LAST, last_allies[:], "enemy2")
         low_codes = held([P, T2], U32, "low_codes", "w1_2_1")
         low_planes = held([P, T2], U8, "low_planes")
         nc.vector.quantize_mx(
             out=low_codes[:].bitcast(FP8X4), scales=low_planes[:], in_=grouped_low[:].rearrange("p m t -> p (m t)"),
         )
-        for first, width in sorted(OUT_PIECES, key=lambda piece: -piece[1]):
-            second_product(0, first, width, low_codes, low_planes)
-        lead, rest, wide = slice(0, P), slice(P, HALF), slice(HALF, T2)
+        for first, width in reversed(OUT_PIECES):
+            last_product(0, first, width, low_codes, low_planes)
+        lead, rest = slice(0, P), slice(P, T2 // 2)
         grouped_high = {}
-        for cols, spot in ((wide, "w1_3_1"), (rest, "w1_2_2"), (lead, "w1_1_0")):
-            tile = held([P, cols.stop - cols.start, PACK], BF16, f"grouped_high{cols.start}", spot)
-            interleave(tile[:], 0, cols)
-            grouped_high[cols.start] = tile
-        place_enemies(last, enemies[last])
+        for cols, place in ((right, rounded_place), (rest, "w1_2_2"), (lead, "w1_1_0")):
+            grouped_high[cols.start] = held([P, cols.stop - cols.start, PACK], BF16, f"grouped_high{cols.start}", place)
+            group_z(grouped_high[cols.start][:], 0, cols)
+        place_enemies(LAST)
 
         last_gain = gain_high[:, PACK - 1 : PACK]
         high_codes = held([P, T2], U32, "high_codes")
         high_planes = held([P, T2], U8, "high_planes")
 
-        def round_last(cols):
-            nc.vector.tensor_scalar(grouped_high[cols.start][:, :, PACK - 1], pages[last][:, cols], last_gain, None, ALU.mult)
-
-        def quantise_high(piece, first, stop):
+        def quantise_high(part, first, stop):
+            grouped = grouped_high[part.start][:, first - part.start : stop - part.start, :]
             nc.vector.quantize_mx(
                 out=high_codes[:, first:stop].bitcast(FP8X4), scales=high_planes[:, first:stop],
-                in_=grouped_high[piece.start][:, first - piece.start : stop - piece.start, :].rearrange("p m t -> p (m t)"),
+                in_=grouped.rearrange("p m t -> p (m t)"),
             )
 
-        nc.scalar.activation(grouped_high[wide.start][:, :, PACK - 1], pages[last][:, wide], ACT.Copy, scale=last_gain)
-        round_last(lead)
-        round_last(rest)
+        nc.scalar.activation(grouped_high[right.start][:, :, PACK - 1], pages[LAST][:, right], ACT.Copy, scale=last_gain)
+        for cols in (lead, rest):
+            nc.vector.tensor_scalar(grouped_high[cols.start][:, :, PACK - 1], pages[LAST][:, cols], last_gain, None, ALU.mult)
         quantise_high(lead, 0, P)
         quantise_high(rest, P, 2 * P)
-        quantise_high(rest, 2 * P, HALF)
-        quantise_high(wide, HALF, T2)
+        quantise_high(rest, 2 * P, rest.stop)
+        quantise_high(right, right.start, right.stop)
         for first, width in OUT_PIECES:
-            second_product(1, first, width, high_codes, high_planes)
+            last_product(1, first, width, high_codes, high_planes)
 
         by_row_tile = out.rearrange("(n p) m -> p n m", p=P)
-        results = held([P, N // P, T2], F32, "results")
+        results = held([P, ROW_TILES, T2], F32, "results")
         for b, bank in enumerate(banks):
-            if b < 4:
+            if b < NARROW_BANKS:
                 result, source = results[:, :, b * P : (b + 1) * P], bank[:].rearrange("p (n m) -> p n m", m=P)
             else:
-                result, source = results[:, b - 4, HALF:], bank[:]
-            if b in (2, 4, 6):
+                result, source = results[:, b - NARROW_BANKS, right], bank[:]
+            if b >= 2 and b % 2 == 0:
                 nc.vector.tensor_copy(result, source)
             else:
                 nc.scalar.copy(result, source)
             if b < 2:
                 nc.sync.dma_start(by_row_tile[:, :, b * P : (b + 1) * P], result)
-            elif b == 3:
-                nc.sync.dma_start(by_row_tile[:, :, 2 * P : HALF], results[:, :, 2 * P : HALF])
+            elif b == NARROW_BANKS - 1:
+                pair = slice((b - 1) * P, (b + 1) * P)
+                nc.sync.dma_start(by_row_tile[:, :, pair], results[:, :, pair])
             elif b % 2 == 1:
-                nc.sync.dma_start(by_row_tile[:, b - 5 : b - 3, HALF:], results[:, b - 5 : b - 3, HALF:])
+                pair = slice(b - NARROW_BANKS - 1, b - NARROW_BANKS + 1)
+                nc.sync.dma_start(by_row_tile[:, pair, right], results[:, pair, right])

@@ -113,20 +113,23 @@ def tile_list_turn_order_evaluator_kernel(
         w1_raw.append(load_w1(HIGH_CHUNK, 0, 1))
         enemy_table = [load_words(tab2_words, 0, "enemy")]
         w1_raw[HIGH_CHUNK].extend(load_w1(HIGH_CHUNK, 1, K_PASSES))
-        threat_rows = [load_low_threat(0)]
-        enemy_table.extend(load_words(tab2_words, g, "enemy") for g in range(1, K_PASSES))
+        enemy_table.append(load_words(tab2_words, 1, "enemy"))
         wg1_high = load_high_weights(held([P, 1, S], F32, "wg1_slot0"), wg1, 0, 1)
-        wg1_high.extend(load_high_weights(held([P, PACK - 1, S], F32, "wg1_slots"), wg1, 1, PACK))
+        threat_rows = [load_low_threat(i) for i in range(2)]
+        enemy_table.append(load_words(tab2_words, 2, "enemy"))
+        wg1_high.extend(load_high_weights(held([P, 1, S], F32, "wg1_slot1"), wg1, 1, 2))
+        wg1_high.extend(load_high_weights(held([P, 1, S], F32, "wg1_slot2"), wg1, 2, 3))
+        threat_rows.extend(load_low_threat(i) for i in range(2, PACK))
         enemy_slots = load_list(offs4, "enemy_slots")
         wg2_rows = load_plain(wg2, [P, S], "wg2_rows")
-        threat_rows.extend(load_low_threat(i) for i in range(1, PACK))
         gain_low = held([P, PACK], F32, "gain_low")
         with nc.allow_non_contiguous_dma(reason="one gain a partition and low tile"):
             nc.sync.dma_start(gain_low[:], gain[0:K_PASS].rearrange("(i p) -> p i", p=P))
         gain_high = load_plain(gain[K_PASS:].rearrange("(p t) -> p t", t=PACK), [P, PACK], "gain_high")
-        threat_high = load_plain(threat[K_PASS:, :].rearrange("(p t) j -> p t j", t=PACK), [P, PACK, S], "threat_high")
-        threat_rows.extend(threat_high[:, t, :] for t in range(PACK))
-        wg2_high = load_high_weights(held([P, PACK - 1, S], F32, "wg2_slots"), wg2, 0, PACK - 1)
+        threat_high = load_plain(threat[K_PASS:, :].rearrange("(p t) j -> p (t j)", t=PACK), [P, PACK * S], "threat_high")
+        threat_rows.extend(threat_high[:, t * S : (t + 1) * S] for t in range(PACK))
+        wg2_high = load_high_weights(held([P, PACK, S], F32, "wg2_slots"), wg2, 0, PACK)
+        wg1_high.extend(load_high_weights(held([P, 1, S], F32, "wg1_slot3"), wg1, PACK - 1, PACK))
         w4_codes = held([P, R_PASSES, 2 * N], U8, "w4_codes")
         nc.sync.dma_start(w4_codes[:].bitcast(I32), w4_words.rearrange("a p c -> p a c").bitcast(I32))
         for q in range(QUADRANTS):
@@ -139,7 +142,7 @@ def tile_list_turn_order_evaluator_kernel(
         enemy_weights = [wg2_rows[:]] * PACK + wg2_high
         banks = [psum.tile([P, BANK], F32, name=f"bank{b}") for b in range(8)]
         pages = {}
-        w1_codes, w1_planes = {}, {}
+        w1_codes, w1_planes, w1_runs = {}, {}, {}
 
         def gather(picked, window, offsets):
             nc.vector.tensor_copy(picked, window[:].indirect(offsets))
@@ -166,6 +169,8 @@ def tile_list_turn_order_evaluator_kernel(
             codes = held([P, (hi - lo) * width], U32, f"w1_codes{c}_{lo}")
             planes = held([P, (hi - lo) * width], U8, f"w1_planes{c}_{lo}")
             for g in range(lo, hi):
+                run = slice((g - lo) * width, (g - lo + 1) * width)
+                w1_runs.setdefault((first // K_PASS, g), []).append((first % K_PASS, codes[:, run], planes[:, run]))
                 for u in range(width // P):
                     cols = slice((g - lo) * width + u * P, (g - lo) * width + (u + 1) * P)
                     w1_codes[first // P + u, g] = codes[:, cols]
@@ -177,6 +182,21 @@ def tile_list_turn_order_evaluator_kernel(
 
         def quantise_last_pass(c):
             quantise_w1(c, 2, K_PASSES, group_w1(c, 2, K_PASSES))
+
+        def quantise_high_half(g, h):
+            slots = slice(2 * h, 2 * h + 2)
+            staged = held([P, 2 * K_PASS], BF16, f"staged_half{h}")
+            nc.scalar.copy(
+                staged[:].rearrange("p (t m j) -> p m j t", t=2, j=PACK),
+                w1_raw[HIGH_CHUNK][g][:].rearrange("p j (m t) -> p m j t", t=PACK)[:, :, :, slots],
+            )
+            codes = held([P, 2 * P], U32, f"w1_codes_half{h}")
+            planes = held([P, 2 * P], U8, f"w1_planes_half{h}")
+            w1_runs.setdefault((1, g), []).append((2 * P * h, codes[:], planes[:]))
+            for u in range(2):
+                w1_codes[PACK + 2 * h + u, g] = codes[:, u * P : (u + 1) * P]
+                w1_planes[PACK + 2 * h + u, g] = planes[:, u * P : (u + 1) * P]
+            nc.vector.quantize_mx(out=codes[:].bitcast(FP8X4), scales=planes[:], in_=staged[:])
 
         def first_product(i, words, planes, sums, cols):
             for g in range(K_PASSES):
@@ -193,23 +213,41 @@ def tile_list_turn_order_evaluator_kernel(
             first_product(i, ally_words, ally_planes, sums[:], all_entries)
             nc.scalar.activation(values, sums[:], ACT.Sigmoid)
 
-        def enemy_values(i, values, negated_place, turned_place):
-            sums, turned_sums, back = banks[2 + i % 2], banks[4 + i % 2], banks[6 + i % 2]
-            first_product(i, enemy_words, enemy_planes, sums[:], all_entries)
-            negated = held([P, S], F32, f"negated{i}", negated_place)
-            nc.scalar.activation(negated[:], sums[:], ACT.Copy, scale=-1.0)
-            squares = [slice(c * P, (c + 1) * P) for c in range(S // P)]
-            terms = [(threat_rows[i], sq) for sq in squares] + [(negated[:], sq) for sq in squares]
+        squares = [slice(c * P, (c + 1) * P) for c in range(S // P)]
+
+        def turn_threat(i):
+            turned = banks[1 - i % 2]
+            for sq in squares:
+                nc.tensor.transpose(turned[:, sq], threat_rows[i][:, sq], identity[:])
+            nc.scalar.activation(threat_rows[i], turned[:], ACT.Copy, scale=-1.0)
+
+        def turned_sums(a, places):
+            tiles = []
+            for c, sq in enumerate(squares):
+                sums = banks[((2, 3, 4, 5), (6, 7, 2, 3))[a][c]]
+                runs = [(g, run) for g in range(K_PASSES) for run in w1_runs[a, g]]
+                for n, (g, (first, codes, planes)) in enumerate(runs):
+                    nc.tensor.matmul_mx(
+                        out=sums[:, first : first + codes.shape[1]],
+                        lhsT=enemy_words[g][:, sq].bitcast(FP8X4), lhsT_scale=enemy_planes[4 * g :, sq],
+                        rhs=codes.bitcast(FP8X4), rhs_scale=planes,
+                        start=(n == 0), stop=(n == len(runs) - 1),
+                    )
+                tile = held([P, K_PASS], F32, f"turned_sums{a}_{c}", places[c])
+                nc.scalar.copy(tile[:], sums[:])
+                tiles.append(tile)
+            return tiles
+
+        def turn_back(i, turned):
+            back = banks[2 + i if i < PACK else 4 + i % 2]
+            rows = slice(i % PACK * P, (i % PACK + 1) * P)
+            terms = [(threat_rows[i][:, sq], sq) for sq in squares] + [(turned[c][:, rows], sq) for c, sq in enumerate(squares)]
             for n, (term, sq) in enumerate(terms):
                 nc.tensor.matmul(
-                    turned_sums[:, sq], lhsT=term[:, sq], rhs=identity[:], is_transpose=True,
+                    back[:, sq], lhsT=term, rhs=identity[:], is_transpose=True,
                     start=(n == 0), stop=(n == len(terms) - 1),
                 )
-            turned = held([P, S], F32, f"turned{i}", turned_place)
-            nc.scalar.activation(turned[:], turned_sums[:], ACT.Relu, scale=-1.0)
-            for sq in squares:
-                nc.tensor.transpose(back[:, sq], turned[:, sq], identity[:])
-            nc.scalar.copy(values, back[:])
+            return back
 
         def scatter(i, offsets, values, weights):
             nc.vector.tensor_tensor(pages[i][:].indirect(offsets), values, weights, ALU.mult)
@@ -280,47 +318,56 @@ def tile_list_turn_order_evaluator_kernel(
         ally_values(3, allies3[:])
         quantise_w1(HIGH_CHUNK, 0, 2, high_staged)
         place_allies(3, allies3[:], "enemy0")
-        quantise_last_pass(HIGH_CHUNK)
-        enemy_rest = held([P, K_PASSES - 1, S], U32, "enemy_rest", "w1_2_2")
-        enemy_words = [enemy_first[:]] + [enemy_rest[:, g - 1, :] for g in range(1, K_PASSES)]
-        for g in range(1, K_PASSES):
-            gather(enemy_words[g], enemy_table[g], enemy_list[:])
+        quantise_high_half(K_PASSES - 1, 0)
+        enemy_words = [enemy_first[:], held([P, S], U32, "enemy_second", "staged_half0")[:], held([P, S], U32, "enemy_third")[:]]
+        gather(enemy_words[1], enemy_table[1], enemy_list[:])
+        quantise_high_half(K_PASSES - 1, 1)
 
         high_allies = held([P, PACK - 1, S], F32, "high_allies", "ally1")
         for t in range(PACK - 1):
             ally_values(PACK + t, high_allies[:, t, :])
         for t, page_place in enumerate(("staged3_0", "enemy1", "w1_2_0")):
             place_allies(PACK + t, high_allies[:, t, :], page_place)
+            if t == 0:
+                gather(enemy_words[2], enemy_table[2], enemy_list[:])
 
         low_enemies = held([P, PACK, S], F32, "low_enemies", "ally2")
-        high_enemies = held([P, PACK, S], F32, "high_enemies", "ally0")
-        enemies = [tile[:, t, :] for tile in (low_enemies, high_enemies) for t in range(PACK)]
-        gains_wait_for, rounded_place = PACK + 1, "w1_3_1"
-        for i in range(TILES):
-            turned_place = rounded_place if i == gains_wait_for else f"w1_0_{i % 2}"
-            enemy_values(i, enemies[i], f"w1_1_{i % 2}", turned_place)
-        last_allies = held([P, S], F32, "last_allies", "w1_0_0")
-        ally_values(LAST, last_allies[:])
+        high_enemies = held([P, PACK - 1, S], F32, "high_enemies", "ally0")
+        enemies = [low_enemies[:, t, :] for t in range(PACK)] + [high_enemies[:, t, :] for t in range(PACK - 1)]
+        turned_places = (("w1_0_0", "w1_0_1", "w1_1_0", "w1_1_1"), ("w1_0_2", "staged0_0", "staged1_0", "staged2_2"))
+        for a in range(R_PASSES):
+            ahead = 2 if a == 0 else PACK
+            for i in range(a * PACK, a * PACK + ahead):
+                turn_threat(i)
+            turned = turned_sums(a, turned_places[a])
+            for i in range(a * PACK, (a + 1) * PACK):
+                if 0 < i < PACK - 1:
+                    turn_threat(i + 1)
+                back = turn_back(i, turned)
+                if i < LAST:
+                    nc.scalar.activation(enemies[i], back[:], ACT.Relu)
+        last_allies = threat_rows[LAST]
+        ally_values(LAST, last_allies)
         for i in range(PACK):
             place_enemies(i)
 
-        rounded = held([P, PACK, T2], BF16, "rounded", rounded_place)
-        slot_rows = held([P, (PACK + 1) * T2 + T2 // 2], BF16, "slot_rows", "w1_3_2")
-        by_slot = slot_rows[:, 0 : (PACK + 1) * T2].rearrange("p (t m) -> p t m", m=T2)
+        rounded = [threat_rows[i + 3].bitcast(BF16) for i in range(PACK)]
+        slot_rows = held([P, (PACK + 1) * T2], BF16, "slot_rows", "w1_3_2")
+        by_slot = slot_rows[:].rearrange("p (t m) -> p t m", m=T2)
         for i in range(PACK):
-            nc.scalar.activation(rounded[:, i, :], pages[i][:], ACT.Copy, scale=gain_low[:, i : i + 1])
-            nc.sync.dma_start(by_slot[32 * i : 32 * (i + 1), 1:, :], rounded[:, i, :])
+            nc.scalar.activation(rounded[i], pages[i][:], ACT.Copy, scale=gain_low[:, i : i + 1])
+            nc.sync.dma_start(by_slot[32 * i : 32 * (i + 1), 1:, :], rounded[i])
         left, right = slice(0, T2 // 2), slice(T2 // 2, T2)
         grouped_low = held([P, T2, PACK], BF16, "grouped_low", "w1_3_0")
         group_z(grouped_low[:, right, :], 1, right)
-        last_weights = slot_rows[:, PACK * T2 + T2 // 2 :].bitcast(F32).rearrange("p (t j) -> p t j", t=1)
-        enemy_weights.extend(load_high_weights(last_weights, wg2, PACK - 1, PACK))
         group_z(grouped_low[:, left, :], 1, left)
+        enemies.append(by_slot[:, PACK, :].bitcast(F32))
+        nc.scalar.activation(enemies[LAST], back[:], ACT.Relu)
 
         for t in range(PACK - 1):
             place_enemies(PACK + t)
             nc.scalar.activation(by_slot[:, t, :], pages[PACK + t][:], ACT.Copy, scale=gain_high[:, t : t + 1])
-        place_allies(LAST, last_allies[:], "enemy2")
+        place_allies(LAST, last_allies, "enemy2")
         low_codes = held([P, T2], U32, "low_codes", "w1_2_1")
         low_planes = held([P, T2], U8, "low_planes")
         nc.vector.quantize_mx(
@@ -330,7 +377,7 @@ def tile_list_turn_order_evaluator_kernel(
             last_product(0, first, width, low_codes, low_planes)
         lead, rest = slice(0, P), slice(P, T2 // 2)
         grouped_high = {}
-        for cols, place in ((right, rounded_place), (rest, "w1_2_2"), (lead, "w1_1_0")):
+        for cols, place in ((right, "w1_3_1"), (rest, "w1_2_2"), (lead, "w1_1_0")):
             grouped_high[cols.start] = held([P, cols.stop - cols.start, PACK], BF16, f"grouped_high{cols.start}", place)
             group_z(grouped_high[cols.start][:], 0, cols)
         place_enemies(LAST)

@@ -27,10 +27,9 @@ BANK = 512
 TILES = H // P
 LAST = TILES - 1
 ROW_TILES = N // P
-W1_CHUNKS = ((0, 128), (128, 128), (256, 256), (512, 512))
-HIGH_CHUNK = len(W1_CHUNKS) - 1
-OUT_PIECES = ((0, 128), (128, 128), (256, 128), (384, 128), (512, 512))
-NARROW_BANKS = len(OUT_PIECES) - 1
+KB = 1024
+ALIGN = 64
+SCALAR_SHARE = 512
 
 
 def tile_list_turn_order_evaluator_kernel(
@@ -43,8 +42,22 @@ def tile_list_turn_order_evaluator_kernel(
         keep = ctx.enter_context(tc.tile_pool(name="keep", bufs=1))
         psum = ctx.enter_context(tc.psum_pool(name="psum", bufs=1))
 
-        def held(shape, dtype, name, place=None):
-            return keep.tile(shape, dtype, name=name, tag=place or name, align_bytes=64)
+        width_of = {F32: 4, U32: 4, BF16: 2, U8: 1}
+        starts = {"free": 0}
+
+        def reserve(name, size):
+            starts[name] = starts["free"]
+            starts["free"] = starts["free"] + -(-size // ALIGN) * ALIGN
+
+        def held(shape, dtype, name, over=None, at=0):
+            if over is None:
+                size = width_of[dtype]
+                for extent in shape[1:]:
+                    size = size * extent
+                reserve(name, size)
+            else:
+                starts[name] = starts[over] + at
+            return keep.tile(shape, dtype, name=name, tag=name, align_bytes=ALIGN, offset=starts[name])
 
         def load_list(src, name):
             tile = lists.tile([P, S // 16], U16, name=name)
@@ -66,29 +79,35 @@ def tile_list_turn_order_evaluator_kernel(
                 rows = tile[32 * q : 32 * q + 4 * K_PASSES, :]
                 queue.dma_start(rows.bitcast(I32), src[:, 4 * q : 4 * q + 4, :].bitcast(I32))
 
-        def load_w1(c, lo=0, hi=K_PASSES):
-            first, width = W1_CHUNKS[c]
-            tiles = []
-            for g in range(lo, hi):
-                tile = held([P, PACK, width], F32, f"w1_{c}_{g}")
-                rows = w1[g * K_PASS : (g + 1) * K_PASS, first : first + width]
-                nc.sync.dma_start(tile[:], rows.rearrange("(p j) c -> p j c", j=PACK))
-                tiles.append(tile)
-            return tiles
+        def load_w1(first, width, g, name, over=None, at=0):
+            tile = held([P, PACK * width], F32, name, over, at)
+            rows = w1[g * K_PASS : (g + 1) * K_PASS, first : first + width]
+            nc.sync.dma_start(tile[:].rearrange("p (j c) -> p j c", j=PACK), rows.rearrange("(p j) c -> p j c", j=PACK))
+            return tile[:].rearrange("p (j c) -> p j c", j=PACK)
 
-        def load_high_weights(target, src, t0, t1):
-            rows = src.rearrange("(q t) j -> q t j", t=PACK)[:, t0:t1, :]
-            for q in range(QUADRANTS):
-                nc.sync.dma_start(target[32 * q : 32 * (q + 1), :, :], rows)
-            return [target[:, t, :] for t in range(t1 - t0)]
+        def load_low_w1(i):
+            tiles = [load_w1(i * P, P, g, f"raw{i}_{g}") for g in range(K_PASSES - 1)]
+            reserve(f"round{i}", 6 * KB if i == 3 else 2 * KB)
+            return tiles + [load_w1(i * P, P, 2, f"raw{i}_2", f"round{i}", 2 * KB if i == 3 else 0)]
 
-        def load_plain(src, shape, name):
-            tile = held(shape, F32, name)
+        def load_plain(src, shape, name, over=None, at=0):
+            tile = held(shape, F32, name, over, at)
             nc.sync.dma_start(tile[:], src)
             return tile
 
-        def load_low_threat(i):
-            return load_plain(threat[i * P : (i + 1) * P, :], [P, S], f"threat{i}")[:]
+        def load_high_weights(src, t, name):
+            target = held([P, S], F32, name)
+            rows = src.rearrange("(q t) j -> q t j", t=PACK)[:, t, :]
+            for q in range(QUADRANTS):
+                nc.sync.dma_start(target[32 * q : 32 * (q + 1), :], rows)
+            return target[:]
+
+        def load_threat(i):
+            if i < PACK:
+                rows = threat[i * P : (i + 1) * P, :]
+            else:
+                rows = threat[K_PASS:, :].rearrange("(p t) j -> p t j", t=PACK)[:, i - PACK, :]
+            return load_plain(rows, [P, S], f"threat{i}", f"threat_place{i}" if 1 < i < PACK else None)[:]
 
         ally_scales = cleared([P, T], "ally_scales")
         enemy_scales = cleared([P, T], "enemy_scales")
@@ -100,36 +119,42 @@ def tile_list_turn_order_evaluator_kernel(
 
         ally_list = load_list(offs, "ally_list")
         ally_table = [load_words(tab_words, 0, "ally")]
-        w1_raw = [load_w1(0)]
+        raw_low = [load_low_w1(0)]
+        enemy_list = load_list(offs2, "enemy_list")
         ally_table.extend(load_words(tab_words, g, "ally") for g in range(1, K_PASSES))
         wg1_rows = held([P, S], F32, "wg1_rows")
-        nc.sync.dma_start(wg1_rows[:, 0 : S // 2], wg1[:, 0 : S // 2])
+        nc.sync.dma_start(wg1_rows[:, 0 : 2 * P], wg1[:, 0 : 2 * P])
         ally_slots = load_list(offs3, "ally_slots")
-        w1_raw.append(load_w1(1))
-        nc.sync.dma_start(wg1_rows[:, S // 2 :], wg1[:, S // 2 :])
-        w1_raw.append(load_w1(2, 0, 1))
-        enemy_list = load_list(offs2, "enemy_list")
-        w1_raw[2].extend(load_w1(2, 1, K_PASSES))
-        w1_raw.append(load_w1(HIGH_CHUNK, 0, 1))
-        enemy_table = [load_words(tab2_words, 0, "enemy")]
-        w1_raw[HIGH_CHUNK].extend(load_w1(HIGH_CHUNK, 1, K_PASSES))
-        enemy_table.append(load_words(tab2_words, 1, "enemy"))
-        wg1_high = load_high_weights(held([P, 1, S], F32, "wg1_slot0"), wg1, 0, 1)
-        threat_rows = [load_low_threat(i) for i in range(2)]
-        enemy_table.append(load_words(tab2_words, 2, "enemy"))
-        wg1_high.extend(load_high_weights(held([P, 1, S], F32, "wg1_slot1"), wg1, 1, 2))
-        wg1_high.extend(load_high_weights(held([P, 1, S], F32, "wg1_slot2"), wg1, 2, 3))
-        threat_rows.extend(load_low_threat(i) for i in range(2, PACK))
+        raw_low.append(load_low_w1(1))
+        nc.sync.dma_start(wg1_rows[:, 2 * P :], wg1[:, 2 * P :])
+        raw_low.append(load_low_w1(2))
+        enemy_table = [load_words(tab2_words, g, "enemy") for g in range(K_PASSES - 1)]
+        raw_low.append(load_low_w1(3))
+        threat_rows = [load_threat(i) for i in range(2)]
+        enemy_table.append(load_words(tab2_words, K_PASSES - 1, "enemy"))
+        reserve("wg2_place", 2 * KB)
+        for i in range(2, PACK):
+            reserve(f"threat_place{i}", 2 * KB)
+        reserve("slot_place", KB)
+        raw_high = [load_w1(K_PASS, K_PASS, 0, "high0")]
+        wg2_rows = load_plain(wg2, [P, S], "wg2_rows", "wg2_place")
         enemy_slots = load_list(offs4, "enemy_slots")
-        wg2_rows = load_plain(wg2, [P, S], "wg2_rows")
+        threat_rows.extend(load_threat(i) for i in range(2, PACK))
+        raw_high.extend(load_w1(K_PASS, K_PASS, g, f"high{g}") for g in range(1, K_PASSES))
         gain_low = held([P, PACK], F32, "gain_low")
         with nc.allow_non_contiguous_dma(reason="one gain a partition and low tile"):
             nc.sync.dma_start(gain_low[:], gain[0:K_PASS].rearrange("(i p) -> p i", p=P))
         gain_high = load_plain(gain[K_PASS:].rearrange("(p t) -> p t", t=PACK), [P, PACK], "gain_high")
-        threat_high = load_plain(threat[K_PASS:, :].rearrange("(p t) j -> p (t j)", t=PACK), [P, PACK * S], "threat_high")
-        threat_rows.extend(threat_high[:, t * S : (t + 1) * S] for t in range(PACK))
-        wg2_high = load_high_weights(held([P, PACK, S], F32, "wg2_slots"), wg2, 0, PACK)
-        wg1_high.extend(load_high_weights(held([P, 1, S], F32, "wg1_slot3"), wg1, PACK - 1, PACK))
+        ally_weights = [wg1_rows[:]] * PACK
+        enemy_weights = [wg2_rows[:]] * PACK
+        threat_rows.extend(load_threat(PACK + t) for t in range(PACK))
+        for t in range(PACK):
+            if t < PACK - 1:
+                ally_weights.append(load_high_weights(wg1, t, f"wg1_slot{t}"))
+            if t > 0:
+                enemy_weights.append(load_high_weights(wg2, t - 1, f"wg2_slot{t - 1}"))
+        ally_weights.append(load_high_weights(wg1, PACK - 1, "wg1_slot3"))
+        enemy_weights.append(load_high_weights(wg2, PACK - 1, "wg2_slot3"))
         w4_codes = held([P, R_PASSES, 2 * N], U8, "w4_codes")
         nc.sync.dma_start(w4_codes[:].bitcast(I32), w4_words.rearrange("a p c -> p a c").bitcast(I32))
         for q in range(QUADRANTS):
@@ -138,110 +163,97 @@ def tile_list_turn_order_evaluator_kernel(
                 w4_scales[:, 4 * q : 4 * q + 4, :].rearrange("a s n -> s a n").bitcast(I32),
             )
 
-        ally_weights = [wg1_rows[:]] * PACK + wg1_high
-        enemy_weights = [wg2_rows[:]] * PACK + wg2_high
         banks = [psum.tile([P, BANK], F32, name=f"bank{b}") for b in range(8)]
         pages = {}
-        w1_codes, w1_planes, w1_runs = {}, {}, {}
+        w1_codes, w1_planes, pair_codes, pair_planes, turned_squares = {}, {}, {}, {}, {}
+        squares = [slice(c * P, (c + 1) * P) for c in range(S // P)]
+        all_entries = slice(0, S)
+
+        def list_cols(entries):
+            return slice(entries.start // 16, entries.stop // 16)
 
         def gather(picked, window, offsets):
             nc.vector.tensor_copy(picked, window[:].indirect(offsets))
 
-        def group_w1(c, lo, hi):
-            size = PACK * W1_CHUNKS[c][1]
-            staged = held([P, (hi - lo) * size], BF16, f"staged{c}_{lo}")
-            for g in range(lo, hi):
-                grouped = staged[:, (g - lo) * size : (g - lo + 1) * size]
-                if c < HIGH_CHUNK:
-                    nc.scalar.copy(
-                        grouped.rearrange("p (c i j) -> p c j i", i=4, j=PACK),
-                        w1_raw[c][g][:].rearrange("p j (c i) -> p c j i", i=4),
-                    )
-                else:
-                    nc.scalar.copy(
-                        grouped.rearrange("p (t m j) -> p m j t", t=PACK, j=PACK),
-                        w1_raw[c][g][:].rearrange("p j (m t) -> p m j t", t=PACK),
-                    )
-            return staged
+        def quantise_w1(first_tile, count, g, staged):
+            pair = first_tile // 2
+            if first_tile % 2 == 0:
+                pair_codes[pair, g] = held([P, 2 * P], U32, f"w1_codes{pair}_{g}")
+                pair_planes[pair, g] = held([P, 2 * P], U8, f"w1_planes{pair}_{g}")
+                for u in range(2):
+                    w1_codes[first_tile + u, g] = pair_codes[pair, g][:, u * P : (u + 1) * P]
+                    w1_planes[first_tile + u, g] = pair_planes[pair, g][:, u * P : (u + 1) * P]
+            cols = slice(first_tile % 2 * P, (first_tile % 2 + count) * P)
+            nc.vector.quantize_mx(out=pair_codes[pair, g][:, cols].bitcast(FP8X4), scales=pair_planes[pair, g][:, cols], in_=staged[:])
 
-        def quantise_w1(c, lo, hi, staged):
-            first, width = W1_CHUNKS[c]
-            codes = held([P, (hi - lo) * width], U32, f"w1_codes{c}_{lo}")
-            planes = held([P, (hi - lo) * width], U8, f"w1_planes{c}_{lo}")
-            for g in range(lo, hi):
-                run = slice((g - lo) * width, (g - lo + 1) * width)
-                w1_runs.setdefault((first // K_PASS, g), []).append((first % K_PASS, codes[:, run], planes[:, run]))
-                for u in range(width // P):
-                    cols = slice((g - lo) * width + u * P, (g - lo) * width + (u + 1) * P)
-                    w1_codes[first // P + u, g] = codes[:, cols]
-                    w1_planes[first // P + u, g] = planes[:, cols]
-            nc.vector.quantize_mx(out=codes[:].bitcast(FP8X4), scales=planes[:], in_=staged[:])
+        def low_w1(i):
+            for g in range(K_PASSES):
+                staged = held([P, K_PASS], BF16, f"staged{i}_{g}", f"raw{i - 1}_{min(g, 1)}" if i else None, KB * (g // 2))
+                nc.scalar.copy(
+                    staged[:].rearrange("p (c i j) -> p c j i", i=4, j=PACK),
+                    raw_low[i][g].rearrange("p j (c i) -> p c j i", i=4),
+                )
+                quantise_w1(i, 1, g, staged)
 
-        def quantise_early_passes(c):
-            quantise_w1(c, 0, 2, group_w1(c, 0, 2))
-
-        def quantise_last_pass(c):
-            quantise_w1(c, 2, K_PASSES, group_w1(c, 2, K_PASSES))
-
-        def quantise_high_half(g, h):
-            slots = slice(2 * h, 2 * h + 2)
-            staged = held([P, 2 * K_PASS], BF16, f"staged_half{h}")
+        def high_w1(h, g, over, at=0):
+            staged = held([P, 2 * K_PASS], BF16, f"staged_high{h}_{g}", over, at)
             nc.scalar.copy(
                 staged[:].rearrange("p (t m j) -> p m j t", t=2, j=PACK),
-                w1_raw[HIGH_CHUNK][g][:].rearrange("p j (m t) -> p m j t", t=PACK)[:, :, :, slots],
+                raw_high[g].rearrange("p j (m t) -> p m j t", t=PACK)[:, :, :, 2 * h : 2 * h + 2],
             )
-            codes = held([P, 2 * P], U32, f"w1_codes_half{h}")
-            planes = held([P, 2 * P], U8, f"w1_planes_half{h}")
-            w1_runs.setdefault((1, g), []).append((2 * P * h, codes[:], planes[:]))
-            for u in range(2):
-                w1_codes[PACK + 2 * h + u, g] = codes[:, u * P : (u + 1) * P]
-                w1_planes[PACK + 2 * h + u, g] = planes[:, u * P : (u + 1) * P]
-            nc.vector.quantize_mx(out=codes[:].bitcast(FP8X4), scales=planes[:], in_=staged[:])
+            quantise_w1(PACK + 2 * h, 2, g, staged)
 
-        def first_product(i, words, planes, sums, cols):
-            for g in range(K_PASSES):
+        def ally_values(i, values, bank, entries):
+            count = entries.stop - entries.start
+            runs = ((0, P), (P, count)) if count == 3 * P else ((0, count),)
+            steps = [(g, run) for g in range(K_PASSES) for run in runs]
+            for n, (g, (lo, hi)) in enumerate(steps):
+                cols = slice(entries.start + lo, entries.start + hi)
                 nc.tensor.matmul_mx(
-                    out=sums, lhsT=w1_codes[i, g].bitcast(FP8X4), lhsT_scale=w1_planes[i, g],
-                    rhs=words[g][:, cols].bitcast(FP8X4), rhs_scale=planes[4 * g :, cols],
-                    start=(g == 0), stop=(g == K_PASSES - 1),
+                    out=bank[:, lo:hi], lhsT=w1_codes[i, g].bitcast(FP8X4), lhsT_scale=w1_planes[i, g],
+                    rhs=ally_words[g][:, cols].bitcast(FP8X4), rhs_scale=ally_planes[4 * g :, cols],
+                    start=(n == 0), stop=(n == len(steps) - 1),
                 )
+            nc.scalar.activation(values, bank[:, 0:count], ACT.Sigmoid)
 
-        all_entries = slice(0, S)
+        def scatter(i, offsets, values, weights):
+            nc.vector.tensor_tensor(pages[i][:].indirect(offsets), values, weights, ALU.mult)
 
-        def ally_values(i, values):
-            sums = banks[i % 2]
-            first_product(i, ally_words, ally_planes, sums[:], all_entries)
-            nc.scalar.activation(values, sums[:], ACT.Sigmoid)
-
-        squares = [slice(c * P, (c + 1) * P) for c in range(S // P)]
+        def place_allies(i, values_over, values_at, page_over, page_at):
+            values = held([P, S], F32, f"allies{i}", values_over, values_at)
+            ally_values(i, values[:], banks[(0, 0, 0, 0, 4, 5, 5, 4)[i]], all_entries)
+            pages[i] = held([P, T2], F32, f"page{i}", page_over, page_at)
+            scatter(i, ally_slots[:], values[:], ally_weights[i])
 
         def turn_threat(i):
-            turned = banks[1 - i % 2]
+            turned = banks[(6, 1, 6, 1, 6, 7, 2, 3)[i]]
             for sq in squares:
                 nc.tensor.transpose(turned[:, sq], threat_rows[i][:, sq], identity[:])
             nc.scalar.activation(threat_rows[i], turned[:], ACT.Copy, scale=-1.0)
 
-        def turned_sums(a, places):
-            tiles = []
-            for c, sq in enumerate(squares):
-                sums = banks[((2, 3, 4, 5), (6, 7, 2, 3))[a][c]]
-                runs = [(g, run) for g in range(K_PASSES) for run in w1_runs[a, g]]
-                for n, (g, (first, codes, planes)) in enumerate(runs):
+        def turned_sums(pair, groups):
+            for h, (bank, members, place) in enumerate(groups):
+                width = 2 * P * len(members)
+                steps = [(g, n) for g in range(K_PASSES) for n in range(len(members))]
+                for step, (g, n) in enumerate(steps):
+                    sq = squares[members[n]]
                     nc.tensor.matmul_mx(
-                        out=sums[:, first : first + codes.shape[1]],
+                        out=banks[bank][:, 2 * P * n : 2 * P * (n + 1)],
                         lhsT=enemy_words[g][:, sq].bitcast(FP8X4), lhsT_scale=enemy_planes[4 * g :, sq],
-                        rhs=codes.bitcast(FP8X4), rhs_scale=planes,
-                        start=(n == 0), stop=(n == len(runs) - 1),
+                        rhs=pair_codes[pair, g][:].bitcast(FP8X4), rhs_scale=pair_planes[pair, g][:],
+                        start=(step == 0), stop=(step == len(steps) - 1),
                     )
-                tile = held([P, K_PASS], F32, f"turned_sums{a}_{c}", places[c])
-                nc.scalar.copy(tile[:], sums[:])
-                tiles.append(tile)
-            return tiles
+                tile = held([P, width], F32, f"turned_sums{pair}_{h}", *place)
+                nc.scalar.copy(tile[:], banks[bank][:, 0:width])
+                for n, c in enumerate(members):
+                    for u in range(2):
+                        turned_squares[2 * pair + u, c] = tile[:, (2 * n + u) * P : (2 * n + u + 1) * P]
 
-        def turn_back(i, turned):
-            back = banks[2 + i if i < PACK else 4 + i % 2]
-            rows = slice(i % PACK * P, (i % PACK + 1) * P)
-            terms = [(threat_rows[i][:, sq], sq) for sq in squares] + [(turned[c][:, rows], sq) for c, sq in enumerate(squares)]
+        def turn_back(i, members=range(PACK), bank=None):
+            back = banks[(4, 5, 4, 5, 5, 4, 4, 6)[i] if bank is None else bank]
+            terms = [(threat_rows[i][:, squares[c]], squares[c]) for c in members[:-1]]
+            terms.extend((turned_squares[i, c], squares[c]) for c in members)
+            terms.append((threat_rows[i][:, squares[members[-1]]], squares[members[-1]]))
             for n, (term, sq) in enumerate(terms):
                 nc.tensor.matmul(
                     back[:, sq], lhsT=term, rhs=identity[:], is_transpose=True,
@@ -249,21 +261,16 @@ def tile_list_turn_order_evaluator_kernel(
                 )
             return back
 
-        def scatter(i, offsets, values, weights):
-            nc.vector.tensor_tensor(pages[i][:].indirect(offsets), values, weights, ALU.mult)
+        def place_enemies(i, back, values):
+            nc.scalar.activation(values, back[:], ACT.Relu)
+            scatter(i, enemy_slots[:], values, enemy_weights[i])
 
-        def place_allies(i, values, page_place):
-            pages[i] = held([P, T2], F32, f"page{i}", page_place)
-            scatter(i, ally_slots[:], values, ally_weights[i])
+        narrow = [slice(BANK + n * P, BANK + (n + 1) * P) for n in range((T2 - BANK) // P)]
 
-        def place_enemies(i):
-            scatter(i, enemy_slots[:], enemies[i], enemy_weights[i])
-
-        def last_product(a, first, width, codes, planes):
-            cols = slice(first, first + width)
-            wide_piece = width == BANK
+        def last_product(a, cols, codes, planes):
+            wide_piece = cols.start == 0
             for nt in range(ROW_TILES):
-                sums = banks[first // P + nt][:] if wide_piece else banks[first // P][:, nt * P : (nt + 1) * P]
+                sums = banks[len(narrow) + nt][:] if wide_piece else banks[narrow.index(cols)][:, nt * P : (nt + 1) * P]
                 nc.tensor.matmul_mx(
                     out=sums,
                     lhsT=w4_codes[:, a, 2 * P * nt : 2 * P * (nt + 1)].bitcast(FP4X4),
@@ -279,146 +286,169 @@ def tile_list_turn_order_evaluator_kernel(
                 by_slot[:, first_row : first_row + PACK, cols].rearrange("p t (c i) -> p c t i", i=4),
             )
 
-        ally_picked = held([P, K_PASSES, S], U32, "ally_picked")
-        ally_words = [ally_picked[:, g, :] for g in range(K_PASSES)]
+        ally_words = [held([P, S], U32, f"ally_picked{g}")[:] for g in range(K_PASSES)]
         ally_planes = held([P, S], U8, "ally_planes")
+        enemy_planes = held([P, S], U8, "enemy_planes")
         gather(ally_words[0], ally_table[0], ally_list[:])
         gather(ally_planes[:], ally_scales, ally_list[:])
-        quantise_early_passes(0)
-        quantise_last_pass(0)
-        gather(ally_words[1], ally_table[1], ally_list[:])
-        allies0 = held([P, S], F32, "allies0", "ally0")
-        pages[0] = held([P, T2], F32, "page0")
-        halves = [(slice(h * S // 2, (h + 1) * S // 2), slice(h * S // 32, (h + 1) * S // 32)) for h in range(2)]
-        for entries, list_cols in halves:
-            gather(ally_words[2][:, entries], ally_table[2], ally_list[:, list_cols])
-        for h, (entries, list_cols) in enumerate(halves):
-            first_product(0, ally_words, ally_planes, banks[h][:, 0 : S // 2], entries)
-            nc.scalar.activation(allies0[:, entries], banks[h][:, 0 : S // 2], ACT.Sigmoid)
-        for entries, list_cols in halves:
-            scatter(0, ally_slots[:, list_cols], allies0[:, entries], wg1_rows[:, entries])
-
-        quantise_early_passes(1)
-        quantise_last_pass(1)
-        enemy_planes = held([P, S], U8, "enemy_planes")
+        low_w1(0)
         gather(enemy_planes[:], enemy_scales, enemy_list[:])
-        quantise_early_passes(2)
-        allies1 = held([P, S], F32, "allies1", "w1_2_1")
-        ally_values(1, allies1[:])
-        place_allies(1, allies1[:], "enemy_scales")
+        gather(ally_words[1], ally_table[1], ally_list[:])
+        parts = (slice(0, P), slice(P, 2 * P), slice(2 * P, S))
+        for entries in (parts[0], slice(P, S)):
+            gather(ally_words[2][:, entries], ally_table[2], ally_list[:, list_cols(entries)])
+        pages[0] = held([P, T2], F32, "page0", "ally1", 0)
+        for n, entries in enumerate(parts):
+            count = entries.stop - entries.start
+            if n == 2:
+                low_w1(1)
+                values = held([P, count], F32, "allies0_2", "raw1_2", KB)
+            else:
+                values = held([P, count], F32, f"allies0_{n}")
+            ally_values(0, values[:], banks[(0, 6, 1)[n]], entries)
+            scatter(0, ally_slots[:, list_cols(entries)], values[:], wg1_rows[:, entries])
 
-        quantise_last_pass(2)
-        enemy_first = held([P, S], U32, "enemy_first", "w1_1_2")
-        gather(enemy_first[:], enemy_table[0], enemy_list[:])
-        high_staged = group_w1(HIGH_CHUNK, 0, 2)
-        allies2 = held([P, S], F32, "allies2", "w1_3_0")
-        ally_values(2, allies2[:])
-        place_allies(2, allies2[:], "staged2_0")
-        allies3 = held([P, S], F32, "allies3", "w1_3_1")
-        ally_values(3, allies3[:])
-        quantise_w1(HIGH_CHUNK, 0, 2, high_staged)
-        place_allies(3, allies3[:], "enemy0")
-        quantise_high_half(K_PASSES - 1, 0)
-        enemy_words = [enemy_first[:], held([P, S], U32, "enemy_second", "staged_half0")[:], held([P, S], U32, "enemy_third")[:]]
-        gather(enemy_words[1], enemy_table[1], enemy_list[:])
-        quantise_high_half(K_PASSES - 1, 1)
+        def allies_in_halves(i, cut, values_at, page_over, page_at):
+            pages[i] = held([P, T2], F32, f"page{i}", page_over, page_at)
+            for n, entries in enumerate((slice(0, cut), slice(cut, S))):
+                count = entries.stop - entries.start
+                if n == 1:
+                    low_w1(i + 1)
+                    values = held([P, count], F32, f"allies{i}_1", f"raw{i + 1}_2", KB // 4)
+                else:
+                    values = held([P, count], F32, f"allies{i}_0", "ally2", values_at)
+                ally_values(i, values[:], banks[((0, 7), (6, 1))[i - 1][n]], entries)
+                scatter(i, ally_slots[:, list_cols(entries)], values[:], wg1_rows[:, entries])
 
-        high_allies = held([P, PACK - 1, S], F32, "high_allies", "ally1")
-        for t in range(PACK - 1):
-            ally_values(PACK + t, high_allies[:, t, :])
-        for t, page_place in enumerate(("staged3_0", "enemy1", "w1_2_0")):
-            place_allies(PACK + t, high_allies[:, t, :], page_place)
-            if t == 0:
-                gather(enemy_words[2], enemy_table[2], enemy_list[:])
+        allies_in_halves(1, 2 * P, 0, "ally1", 4 * KB)
+        enemy_picked = held([P, K_PASSES * S], U32, "enemy_picked", "ally0")
+        enemy_words = [enemy_picked[:, g * S : (g + 1) * S] for g in range(K_PASSES)]
+        for g in range(K_PASSES - 1):
+            gather(enemy_words[g], enemy_table[g], enemy_list[:])
+        allies_in_halves(2, 2 * P, KB, "enemy1", 0)
+        for sq in squares:
+            gather(enemy_words[2][:, sq], enemy_table[2], enemy_list[:, list_cols(sq)])
+        place_allies(3, "ally2", 2 * KB, "enemy2", 0)
 
-        low_enemies = held([P, PACK, S], F32, "low_enemies", "ally2")
-        high_enemies = held([P, PACK - 1, S], F32, "high_enemies", "ally0")
-        enemies = [low_enemies[:, t, :] for t in range(PACK)] + [high_enemies[:, t, :] for t in range(PACK - 1)]
-        turned_places = (("w1_0_0", "w1_0_1", "w1_1_0", "w1_1_1"), ("w1_0_2", "staged0_0", "staged1_0", "staged2_2"))
-        for a in range(R_PASSES):
-            ahead = 2 if a == 0 else PACK
-            for i in range(a * PACK, a * PACK + ahead):
-                turn_threat(i)
-            turned = turned_sums(a, turned_places[a])
-            for i in range(a * PACK, (a + 1) * PACK):
-                if 0 < i < PACK - 1:
-                    turn_threat(i + 1)
-                back = turn_back(i, turned)
-                if i < LAST:
-                    nc.scalar.activation(enemies[i], back[:], ACT.Relu)
-        last_allies = threat_rows[LAST]
-        ally_values(LAST, last_allies)
+        def enemy_values(i, over, at=0):
+            return held([P, S], F32, f"enemies{i}", over, at)[:]
+
+        rounded = {}
+
+        def low_gain(i, target):
+            rounded[i] = target
+            nc.scalar.activation(target, pages[i][:], ACT.Copy, scale=gain_low[:, i : i + 1])
+
+        def rounded_rows(i, over, at=0):
+            return held([P, T2], BF16, f"rounded{i}", over, at)[:]
+
+        turn_threat(0)
+        turn_threat(1)
+        turned_sums(0, ((2, (0, 1), ("round3", KB // 4)), (3, (2,), ("round3", 4 * KB - KB // 4)), (7, (3,), ("round3", 5 * KB - KB // 4))))
+        values = enemy_values(0, "ally_scales")
+        for members, bank in ((range(PACK - 1), 4), (range(PACK - 1, PACK), 0)):
+            cols = slice(members[0] * P, (members[-1] + 1) * P)
+            nc.scalar.activation(values[:, cols], turn_back(0, members, bank)[:, cols], ACT.Relu)
+        scatter(0, enemy_slots[:], values, enemy_weights[0])
+        back = turn_back(1)
+        high_w1(0, 0, "threat0")
+        place_enemies(1, back, enemy_values(1, "enemy_scales"))
+        turn_threat(2)
+        turn_threat(3)
+        turned_sums(1, ((2, (0, 1), ("turned_sums0_0", 0)), (3, (2, 3), ("turned_sums0_1", 0))))
+        place_enemies(2, turn_back(2), enemy_values(2, "raw0_0"))
+        back = turn_back(3)
+        high_w1(0, 1, "threat1")
+        high_w1(0, 2, "raw2_2")
+        high_w1(1, 2, "raw0_1")
+        place_enemies(3, back, enemy_values(3, "high2"))
+        low_gain(0, rounded_rows(0, "threat2"))
+        low_gain(1, rounded_rows(1, "threat3"))
+        low_gain(2, rounded_rows(2, "high2", 6 * KB))
+        place_allies(4, "raw2_0", 0, "enemy0", 0)
+        for g in range(K_PASSES - 1):
+            high_w1(1, g, "high2", (g + 1) * 2 * KB)
+        place_allies(5, "high1", 2 * KB, "enemy0", 4 * KB)
+        slot_rows = held([P, S + (PACK + 1) * T2], BF16, "slot_rows", "slot_place")
+        by_slot = slot_rows[:, S:].rearrange("p (t m) -> p t m", m=T2)
+        turn_threat(4)
+        turned_sums(2, ((2, (0, 1), ("raw3_1", 0)), (3, (2, 3), ("raw0_2", 0))))
+        place_enemies(4, turn_back(4), enemy_values(4, "high1", 4 * KB))
+        low_gain(3, by_slot[:, PACK, :])
         for i in range(PACK):
-            place_enemies(i)
-
-        rounded = [threat_rows[i + 3].bitcast(BF16) for i in range(PACK)]
-        slot_rows = held([P, (PACK + 1) * T2], BF16, "slot_rows", "w1_3_2")
-        by_slot = slot_rows[:].rearrange("p (t m) -> p t m", m=T2)
-        for i in range(PACK):
-            nc.scalar.activation(rounded[i], pages[i][:], ACT.Copy, scale=gain_low[:, i : i + 1])
-            nc.sync.dma_start(by_slot[32 * i : 32 * (i + 1), 1:, :], rounded[i])
-        left, right = slice(0, T2 // 2), slice(T2 // 2, T2)
-        grouped_low = held([P, T2, PACK], BF16, "grouped_low", "w1_3_0")
-        group_z(grouped_low[:, right, :], 1, right)
-        group_z(grouped_low[:, left, :], 1, left)
-        enemies.append(by_slot[:, PACK, :].bitcast(F32))
-        nc.scalar.activation(enemies[LAST], back[:], ACT.Relu)
-
-        for t in range(PACK - 1):
-            place_enemies(PACK + t)
-            nc.scalar.activation(by_slot[:, t, :], pages[PACK + t][:], ACT.Copy, scale=gain_high[:, t : t + 1])
-        place_allies(LAST, last_allies, "enemy2")
-        low_codes = held([P, T2], U32, "low_codes", "w1_2_1")
+            nc.sync.dma_start(by_slot[32 * i : 32 * (i + 1), 0:PACK, :], rounded[i])
+        for i in range(PACK + 1, TILES):
+            turn_threat(i)
+        place_allies(6, "high1", 6 * KB, "enemy1", 0)
+        place_enemies(5, turn_back(5), enemy_values(5, "rounded0"))
+        turned_sums(3, ((2, (0, 1), ("raw1_0", 0)), (3, (2, 3), ("raw1_1", 0))))
+        place_enemies(6, turn_back(6), enemy_values(6, "rounded1"))
+        wide, late = slice(0, BANK), slice(BANK + 2 * P, T2)
+        grouped_low = held([P, T2, PACK], BF16, "grouped_low")
+        low_codes = held([P, T2], U32, "low_codes")
         low_planes = held([P, T2], U8, "low_planes")
-        nc.vector.quantize_mx(
-            out=low_codes[:].bitcast(FP8X4), scales=low_planes[:], in_=grouped_low[:].rearrange("p m t -> p (m t)"),
-        )
-        for first, width in reversed(OUT_PIECES):
-            last_product(0, first, width, low_codes, low_planes)
-        lead, rest = slice(0, P), slice(P, T2 // 2)
-        grouped_high = {}
-        for cols, place in ((right, "w1_3_1"), (rest, "w1_2_2"), (lead, "w1_1_0")):
-            grouped_high[cols.start] = held([P, cols.stop - cols.start, PACK], BF16, f"grouped_high{cols.start}", place)
-            group_z(grouped_high[cols.start][:], 0, cols)
-        place_enemies(LAST)
 
-        last_gain = gain_high[:, PACK - 1 : PACK]
-        high_codes = held([P, T2], U32, "high_codes")
-        high_planes = held([P, T2], U8, "high_planes")
-
-        def quantise_high(part, first, stop):
-            grouped = grouped_high[part.start][:, first - part.start : stop - part.start, :]
+        def quantise_z(codes, planes, grouped, cols):
             nc.vector.quantize_mx(
-                out=high_codes[:, first:stop].bitcast(FP8X4), scales=high_planes[:, first:stop],
-                in_=grouped.rearrange("p m t -> p (m t)"),
+                out=codes[:, cols].bitcast(FP8X4), scales=planes[:, cols], in_=grouped.rearrange("p m t -> p (m t)"),
             )
 
-        nc.scalar.activation(grouped_high[right.start][:, :, PACK - 1], pages[LAST][:, right], ACT.Copy, scale=last_gain)
-        for cols in (lead, rest):
-            nc.vector.tensor_scalar(grouped_high[cols.start][:, :, PACK - 1], pages[LAST][:, cols], last_gain, None, ALU.mult)
-        quantise_high(lead, 0, P)
-        quantise_high(rest, P, 2 * P)
-        quantise_high(rest, 2 * P, rest.stop)
-        quantise_high(right, right.start, right.stop)
-        for first, width in OUT_PIECES:
-            last_product(1, first, width, high_codes, high_planes)
+        group_z(grouped_low[:, BANK:, :], 0, slice(BANK, T2))
+        place_allies(LAST, "raw2_1", 0, "enemy1", 4 * KB)
+        back = turn_back(LAST)
+        group_z(grouped_low[:, wide, :], 0, wide)
+        last_enemies = slot_rows[:, 0 : 2 * S].bitcast(F32)
+        nc.scalar.activation(last_enemies, back[:], ACT.Relu)
+        quantise_z(low_codes, low_planes, grouped_low[:], slice(0, T2))
+        for cols in [wide] + narrow:
+            last_product(0, cols, low_codes, low_planes)
+
+        for t in range(PACK - 1):
+            nc.scalar.activation(by_slot[:, 1 + t, :], pages[PACK + t][:], ACT.Copy, scale=gain_high[:, t : t + 1])
+        grouped_high = {}
+        right = slice(BANK, T2)
+        for cols in (wide, right):
+            grouped_high[cols.start] = held([P, cols.stop - cols.start, PACK], BF16, f"grouped_high{cols.start}", "ally1", 8 * cols.start)
+            group_z(grouped_high[cols.start][:], 1, cols)
+        scatter(LAST, enemy_slots[:], last_enemies, enemy_weights[LAST])
+
+        last_gain = gain_high[:, PACK - 1 : PACK]
+        high_codes = held([P, T2], U32, "high_codes", "page3")
+        high_planes = held([P, T2], U8, "high_planes")
+
+        def round_last(part, cols):
+            grouped = grouped_high[part.start][:, cols.start - part.start : cols.stop - part.start, PACK - 1]
+            nc.vector.tensor_scalar(grouped, pages[LAST][:, cols], last_gain, None, ALU.mult)
+
+        def quantise_high(part, cols):
+            quantise_z(high_codes, high_planes, grouped_high[part.start][:, cols.start - part.start : cols.stop - part.start, :], cols)
+
+        nc.scalar.activation(grouped_high[0][:, 0:SCALAR_SHARE, PACK - 1], pages[LAST][:, 0:SCALAR_SHARE], ACT.Copy, scale=last_gain)
+        round_last(right, narrow[0])
+        round_last(right, slice(narrow[1].start, narrow[2].stop))
+        quantise_high(right, narrow[0])
+        round_last(right, narrow[3])
+        quantise_high(right, narrow[1])
+        quantise_high(right, late)
+        quantise_high(wide, wide)
+        for cols in narrow + [wide]:
+            last_product(1, cols, high_codes, high_planes)
 
         by_row_tile = out.rearrange("(n p) m -> p n m", p=P)
         results = held([P, ROW_TILES, T2], F32, "results")
         for b, bank in enumerate(banks):
-            if b < NARROW_BANKS:
-                result, source = results[:, :, b * P : (b + 1) * P], bank[:].rearrange("p (n m) -> p n m", m=P)
+            if b < len(narrow):
+                result, source = results[:, :, narrow[b]], bank[:].rearrange("p (n m) -> p n m", m=P)
             else:
-                result, source = results[:, b - NARROW_BANKS, right], bank[:]
+                result, source = results[:, b - len(narrow), wide], bank[:]
             if b >= 2 and b % 2 == 0:
                 nc.vector.tensor_copy(result, source)
             else:
                 nc.scalar.copy(result, source)
             if b < 2:
-                nc.sync.dma_start(by_row_tile[:, :, b * P : (b + 1) * P], result)
-            elif b == NARROW_BANKS - 1:
-                pair = slice((b - 1) * P, (b + 1) * P)
-                nc.sync.dma_start(by_row_tile[:, :, pair], results[:, :, pair])
+                nc.sync.dma_start(by_row_tile[:, :, narrow[b]], result)
+            elif b == len(narrow) - 1:
+                nc.sync.dma_start(by_row_tile[:, :, late], results[:, :, late])
             elif b % 2 == 1:
-                pair = slice(b - NARROW_BANKS - 1, b - NARROW_BANKS + 1)
-                nc.sync.dma_start(by_row_tile[:, pair, right], results[:, pair, right])
+                pair = slice(b - len(narrow) - 1, b - len(narrow) + 1)
+                nc.sync.dma_start(by_row_tile[:, pair, wide], results[:, pair, wide])

@@ -186,8 +186,8 @@ def tile_list_turn_order_evaluator_kernel(
             cols = slice(first_tile % 2 * P, (first_tile % 2 + count) * P)
             nc.vector.quantize_mx(out=pair_codes[pair, g][:, cols].bitcast(FP8X4), scales=pair_planes[pair, g][:, cols], in_=staged[:])
 
-        def low_w1(i):
-            for g in range(K_PASSES):
+        def low_w1(i, lo=0, hi=K_PASSES):
+            for g in range(lo, hi):
                 staged = held([P, K_PASS], BF16, f"staged{i}_{g}", f"raw{i - 1}_{min(g, 1)}" if i else None, KB * (g // 2))
                 nc.scalar.copy(
                     staged[:].rearrange("p (c i j) -> p c j i", i=4, j=PACK),
@@ -308,26 +308,28 @@ def tile_list_turn_order_evaluator_kernel(
             ally_values(0, values[:], banks[(0, 6, 1)[n]], entries)
             scatter(0, ally_slots[:, list_cols(entries)], values[:], wg1_rows[:, entries])
 
-        def allies_in_halves(i, cut, values_at, page_over, page_at):
+        def allies_in_halves(i, cut, values_over, values_at, page_over, page_at):
             pages[i] = held([P, T2], F32, f"page{i}", page_over, page_at)
             for n, entries in enumerate((slice(0, cut), slice(cut, S))):
                 count = entries.stop - entries.start
+                if n == 0 and i == 2:
+                    low_w1(i + 1, 0, 1)
                 if n == 1:
-                    low_w1(i + 1)
+                    low_w1(i + 1, i - 1)
                     values = held([P, count], F32, f"allies{i}_1", f"raw{i + 1}_2", KB // 4)
                 else:
-                    values = held([P, count], F32, f"allies{i}_0", "ally2", values_at)
+                    values = held([P, count], F32, f"allies{i}_0", values_over, values_at)
                 ally_values(i, values[:], banks[((0, 7), (6, 1))[i - 1][n]], entries)
                 scatter(i, ally_slots[:, list_cols(entries)], values[:], wg1_rows[:, entries])
 
-        allies_in_halves(1, 2 * P, 0, "ally1", 4 * KB)
+        allies_in_halves(1, 2 * P, "ally2", 0, "ally1", 4 * KB)
         enemy_picked = held([P, K_PASSES * S], U32, "enemy_picked", "ally0")
         enemy_words = [enemy_picked[:, g * S : (g + 1) * S] for g in range(K_PASSES)]
         for g in range(K_PASSES - 1):
             gather(enemy_words[g], enemy_table[g], enemy_list[:])
-        allies_in_halves(2, 2 * P, KB, "enemy1", 0)
-        for sq in squares:
-            gather(enemy_words[2][:, sq], enemy_table[2], enemy_list[:, list_cols(sq)])
+        allies_in_halves(2, 2 * P, "raw3_0", 0, None, 0)
+        for entries in (slice(0, 2 * P), squares[2], squares[3]):
+            gather(enemy_words[2][:, entries], enemy_table[2], enemy_list[:, list_cols(entries)])
         place_allies(3, "ally2", 2 * KB, "enemy2", 0)
 
         def enemy_values(i, over, at=0):

@@ -221,7 +221,7 @@ def tile_list_turn_order_evaluator_kernel(
 
         def place_allies(i, values_over, values_at, page_over, page_at):
             values = held([P, S], F32, f"allies{i}", values_over, values_at)
-            ally_values(i, values[:], banks[(0, 0, 0, 0, 4, 5, 5, 4)[i]], all_entries)
+            ally_values(i, values[:], banks[(0, 0, 6, 6, 4, 5, 5, 4)[i]], all_entries)
             pages[i] = held([P, T2], F32, f"page{i}", page_over, page_at)
             scatter(i, ally_slots[:], values[:], ally_weights[i])
 
@@ -300,37 +300,27 @@ def tile_list_turn_order_evaluator_kernel(
         pages[0] = held([P, T2], F32, "page0", "ally1", 0)
         for n, entries in enumerate(parts):
             count = entries.stop - entries.start
-            if n == 2:
-                low_w1(1)
-                values = held([P, count], F32, "allies0_2", "raw1_2", KB)
+            if n == 0:
+                values = held([P, count], F32, "allies0_0")
             else:
-                values = held([P, count], F32, f"allies0_{n}")
+                low_w1(1, n - 1, 2 * n - 1)
+                values = held([P, count], F32, f"allies0_{n}", f"raw1_{2 * n - 2}", KB)
             ally_values(0, values[:], banks[(0, 6, 1)[n]], entries)
             scatter(0, ally_slots[:, list_cols(entries)], values[:], wg1_rows[:, entries])
 
-        def allies_in_halves(i, cut, values_over, values_at, page_over, page_at):
-            pages[i] = held([P, T2], F32, f"page{i}", page_over, page_at)
-            for n, entries in enumerate((slice(0, cut), slice(cut, S))):
-                count = entries.stop - entries.start
-                if n == 0 and i == 2:
-                    low_w1(i + 1, 0, 1)
-                if n == 1:
-                    low_w1(i + 1, i - 1)
-                    values = held([P, count], F32, f"allies{i}_1", f"raw{i + 1}_2", KB // 4)
-                else:
-                    values = held([P, count], F32, f"allies{i}_0", values_over, values_at)
-                ally_values(i, values[:], banks[((0, 7), (6, 1))[i - 1][n]], entries)
-                scatter(i, ally_slots[:, list_cols(entries)], values[:], wg1_rows[:, entries])
-
-        allies_in_halves(1, 2 * P, "ally2", 0, "ally1", 4 * KB)
+        place_allies(1, "ally2", 0, "ally1", 4 * KB)
+        low_w1(2)
         enemy_picked = held([P, K_PASSES * S], U32, "enemy_picked", "ally0")
         enemy_words = [enemy_picked[:, g * S : (g + 1) * S] for g in range(K_PASSES)]
         for g in range(K_PASSES - 1):
             gather(enemy_words[g], enemy_table[g], enemy_list[:])
-        allies_in_halves(2, 2 * P, "raw3_0", 0, None, 0)
+        low_w1(3, 0, 2)
+        place_allies(2, "raw3_1", 0, None, 0)
+        low_w1(3, 2)
         for entries in (slice(0, 2 * P), squares[2], squares[3]):
             gather(enemy_words[2][:, entries], enemy_table[2], enemy_list[:, list_cols(entries)])
-        place_allies(3, "ally2", 2 * KB, "enemy2", 0)
+        turn_threat(0)
+        place_allies(3, "ally2", 2 * KB, "ally2", 4 * KB)
 
         def enemy_values(i, over, at=0):
             return held([P, S], F32, f"enemies{i}", over, at)[:]
@@ -344,7 +334,6 @@ def tile_list_turn_order_evaluator_kernel(
         def rounded_rows(i, over, at=0):
             return held([P, T2], BF16, f"rounded{i}", over, at)[:]
 
-        turn_threat(0)
         turn_threat(1)
         turned_sums(0, ((2, (0, 1), ("round3", KB // 4)), (3, (2,), ("round3", 4 * KB - KB // 4)), (7, (3,), ("round3", 5 * KB - KB // 4))))
         values = enemy_values(0, "ally_scales")
@@ -374,7 +363,7 @@ def tile_list_turn_order_evaluator_kernel(
         slot_rows = held([P, S + (PACK + 1) * T2], BF16, "slot_rows", "slot_place")
         by_slot = slot_rows[:, S:].rearrange("p (t m) -> p t m", m=T2)
         turn_threat(4)
-        turned_sums(2, ((2, (0, 1), ("raw3_1", 0)), (3, (2, 3), ("raw0_2", 0))))
+        turned_sums(2, ((2, (0, 1), ("raw3_0", 0)), (3, (2, 3), ("raw0_2", 0))))
         place_enemies(4, turn_back(4), enemy_values(4, "high1", 4 * KB))
         low_gain(3, by_slot[:, PACK, :])
         for i in range(PACK):

@@ -314,9 +314,12 @@ def tile_list_turn_order_evaluator_kernel(
         enemy_words = [enemy_picked[:, g * S : (g + 1) * S] for g in range(K_PASSES)]
         for g in range(K_PASSES - 1):
             gather(enemy_words[g], enemy_table[g], enemy_list[:])
-        low_w1(3, 0, 2)
-        place_allies(2, "raw3_1", 0, None, 0)
-        low_w1(3, 2)
+        pages[2] = held([P, T2], F32, "page2")
+        for n, entries in enumerate((slice(0, S // 2), slice(S // 2, S))):
+            low_w1(3, n, 2 * n + 1)
+            values = held([P, S // 2], F32, f"allies2_{n}", f"raw3_{2 * n}", KB // 4)
+            ally_values(2, values[:], banks[(6, 1)[n]], entries)
+            scatter(2, ally_slots[:, list_cols(entries)], values[:], wg1_rows[:, entries])
         for entries in (slice(0, 2 * P), squares[2], squares[3]):
             gather(enemy_words[2][:, entries], enemy_table[2], enemy_list[:, list_cols(entries)])
         turn_threat(0)
@@ -363,7 +366,7 @@ def tile_list_turn_order_evaluator_kernel(
         slot_rows = held([P, S + (PACK + 1) * T2], BF16, "slot_rows", "slot_place")
         by_slot = slot_rows[:, S:].rearrange("p (t m) -> p t m", m=T2)
         turn_threat(4)
-        turned_sums(2, ((2, (0, 1), ("raw3_0", 0)), (3, (2, 3), ("raw0_2", 0))))
+        turned_sums(2, ((2, (0, 1), ("raw3_1", 0)), (3, (2, 3), ("raw0_2", 0))))
         place_enemies(4, turn_back(4), enemy_values(4, "high1", 4 * KB))
         low_gain(3, by_slot[:, PACK, :])
         for i in range(PACK):
@@ -374,7 +377,7 @@ def tile_list_turn_order_evaluator_kernel(
         place_enemies(5, turn_back(5), enemy_values(5, "rounded0"))
         turned_sums(3, ((2, (0, 1), ("raw1_0", 0)), (3, (2, 3), ("raw1_1", 0))))
         place_enemies(6, turn_back(6), enemy_values(6, "rounded1"))
-        wide, late = slice(0, BANK), slice(BANK + 2 * P, T2)
+        wide, early, late = slice(0, BANK), slice(BANK, BANK + 2 * P), slice(BANK + 2 * P, T2)
         grouped_low = held([P, T2, PACK], BF16, "grouped_low")
         low_codes = held([P, T2], U32, "low_codes")
         low_planes = held([P, T2], U8, "low_planes")
@@ -384,14 +387,16 @@ def tile_list_turn_order_evaluator_kernel(
                 out=codes[:, cols].bitcast(FP8X4), scales=planes[:, cols], in_=grouped.rearrange("p m t -> p (m t)"),
             )
 
-        group_z(grouped_low[:, BANK:, :], 0, slice(BANK, T2))
+        group_z(grouped_low[:, early, :], 0, early)
         place_allies(LAST, "raw2_1", 0, "enemy1", 4 * KB)
         back = turn_back(LAST)
         group_z(grouped_low[:, wide, :], 0, wide)
-        last_enemies = slot_rows[:, 0 : 2 * S].bitcast(F32)
+        group_z(grouped_low[:, late, :], 0, late)
+        last_enemies = by_slot[:, 0, :].bitcast(F32)
         nc.scalar.activation(last_enemies, back[:], ACT.Relu)
-        quantise_z(low_codes, low_planes, grouped_low[:], slice(0, T2))
-        for cols in [wide] + narrow:
+        for cols in (early, wide, late):
+            quantise_z(low_codes, low_planes, grouped_low[:, cols, :], cols)
+        for cols in narrow[:2] + [wide] + narrow[2:]:
             last_product(0, cols, low_codes, low_planes)
 
         for t in range(PACK - 1):

@@ -120,8 +120,9 @@ def tile_list_turn_order_evaluator_kernel(
         ally_list = load_list(offs, "ally_list")
         ally_table = [load_words(tab_words, 0, "ally")]
         raw_low = [load_low_w1(0)]
+        ally_table.append(load_words(tab_words, 1, "ally"))
         enemy_list = load_list(offs2, "enemy_list")
-        ally_table.extend(load_words(tab_words, g, "ally") for g in range(1, K_PASSES))
+        ally_table.append(load_words(tab_words, 2, "ally"))
         wg1_rows = held([P, S], F32, "wg1_rows")
         nc.sync.dma_start(wg1_rows[:, 0 : 2 * P], wg1[:, 0 : 2 * P])
         ally_slots = load_list(offs3, "ally_slots")
@@ -130,15 +131,16 @@ def tile_list_turn_order_evaluator_kernel(
         raw_low.append(load_low_w1(2))
         enemy_table = [load_words(tab2_words, g, "enemy") for g in range(K_PASSES - 1)]
         raw_low.append(load_low_w1(3))
-        threat_rows = [load_threat(i) for i in range(2)]
+        threat_rows = [load_threat(0)]
+        enemy_slots = load_list(offs4, "enemy_slots")
         enemy_table.append(load_words(tab2_words, K_PASSES - 1, "enemy"))
+        threat_rows.append(load_threat(1))
         reserve("wg2_place", 2 * KB)
         for i in range(2, PACK):
             reserve(f"threat_place{i}", 2 * KB)
-        reserve("slot_place", KB)
+        reserve("slot_place", 3 * KB // 2)
         raw_high = [load_w1(K_PASS, K_PASS, 0, "high0")]
         wg2_rows = load_plain(wg2, [P, S], "wg2_rows", "wg2_place")
-        enemy_slots = load_list(offs4, "enemy_slots")
         threat_rows.extend(load_threat(i) for i in range(2, PACK))
         raw_high.extend(load_w1(K_PASS, K_PASS, g, f"high{g}") for g in range(1, K_PASSES))
         gain_low = held([P, PACK], F32, "gain_low")
@@ -226,7 +228,7 @@ def tile_list_turn_order_evaluator_kernel(
             scatter(i, ally_slots[:], values[:], ally_weights[i])
 
         def turn_threat(i):
-            turned = banks[(6, 1, 6, 1, 6, 7, 2, 3)[i]]
+            turned = banks[(6, 2, 6, 1, 6, 7, 2, 3)[i]]
             for sq in squares:
                 nc.tensor.transpose(turned[:, sq], threat_rows[i][:, sq], identity[:])
             nc.scalar.activation(threat_rows[i], turned[:], ACT.Copy, scale=-1.0)
@@ -275,7 +277,7 @@ def tile_list_turn_order_evaluator_kernel(
                     out=sums,
                     lhsT=w4_codes[:, a, 2 * P * nt : 2 * P * (nt + 1)].bitcast(FP4X4),
                     lhsT_scale=w4_planes[:, a, P * nt : P * (nt + 1)],
-                    rhs=codes[:, cols].bitcast(FP8X4), rhs_scale=planes[:, cols],
+                    rhs=codes.bitcast(FP8X4), rhs_scale=planes,
                     start=(a == 0 and (wide_piece or nt == 0)),
                     stop=(a == R_PASSES - 1 and (wide_piece or nt == ROW_TILES - 1)),
                 )
@@ -292,8 +294,8 @@ def tile_list_turn_order_evaluator_kernel(
         gather(ally_words[0], ally_table[0], ally_list[:])
         gather(ally_planes[:], ally_scales, ally_list[:])
         low_w1(0)
-        gather(enemy_planes[:], enemy_scales, enemy_list[:])
         gather(ally_words[1], ally_table[1], ally_list[:])
+        gather(enemy_planes[:], enemy_scales, enemy_list[:])
         parts = (slice(0, P), slice(P, 2 * P), slice(2 * P, S))
         for entries in (parts[0], slice(P, S)):
             gather(ally_words[2][:, entries], ally_table[2], ally_list[:, list_cols(entries)])
@@ -337,13 +339,13 @@ def tile_list_turn_order_evaluator_kernel(
         def rounded_rows(i, over, at=0):
             return held([P, T2], BF16, f"rounded{i}", over, at)[:]
 
-        turn_threat(1)
         turned_sums(0, ((2, (0, 1), ("round3", KB // 4)), (3, (2,), ("round3", 4 * KB - KB // 4)), (7, (3,), ("round3", 5 * KB - KB // 4))))
         values = enemy_values(0, "ally_scales")
         for members, bank in ((range(PACK - 1), 4), (range(PACK - 1, PACK), 0)):
             cols = slice(members[0] * P, (members[-1] + 1) * P)
             nc.scalar.activation(values[:, cols], turn_back(0, members, bank)[:, cols], ACT.Relu)
         scatter(0, enemy_slots[:], values, enemy_weights[0])
+        turn_threat(1)
         back = turn_back(1)
         high_w1(0, 0, "threat0")
         place_enemies(1, back, enemy_values(1, "enemy_scales"))
@@ -363,8 +365,8 @@ def tile_list_turn_order_evaluator_kernel(
         for g in range(K_PASSES - 1):
             high_w1(1, g, "high2", (g + 1) * 2 * KB)
         place_allies(5, "high1", 2 * KB, "enemy0", 4 * KB)
-        slot_rows = held([P, S + (PACK + 1) * T2], BF16, "slot_rows", "slot_place")
-        by_slot = slot_rows[:, S:].rearrange("p (t m) -> p t m", m=T2)
+        slot_rows = held([P, 6 * P + (PACK + 1) * T2], BF16, "slot_rows", "slot_place")
+        by_slot = slot_rows[:, 6 * P :].rearrange("p (t m) -> p t m", m=T2)
         turn_threat(4)
         turned_sums(2, ((2, (0, 1), ("raw3_1", 0)), (3, (2, 3), ("raw0_2", 0))))
         place_enemies(4, turn_back(4), enemy_values(4, "high1", 4 * KB))
@@ -378,26 +380,27 @@ def tile_list_turn_order_evaluator_kernel(
         turned_sums(3, ((2, (0, 1), ("raw1_0", 0)), (3, (2, 3), ("raw1_1", 0))))
         place_enemies(6, turn_back(6), enemy_values(6, "rounded1"))
         wide, early, late = slice(0, BANK), slice(BANK, BANK + 2 * P), slice(BANK + 2 * P, T2)
-        grouped_low = held([P, T2, PACK], BF16, "grouped_low")
-        low_codes = held([P, T2], U32, "low_codes")
+        grouped_low = {
+            cols.start: held([P, cols.stop - cols.start, PACK], BF16, f"grouped_low{cols.start}") for cols in (wide, early, late)
+        }
+        low_codes = held([P, late.start], U32, "low_codes")
         low_planes = held([P, T2], U8, "low_planes")
 
-        def quantise_z(codes, planes, grouped, cols):
-            nc.vector.quantize_mx(
-                out=codes[:, cols].bitcast(FP8X4), scales=planes[:, cols], in_=grouped.rearrange("p m t -> p (m t)"),
-            )
+        def quantise_z(codes, planes, grouped):
+            nc.vector.quantize_mx(out=codes.bitcast(FP8X4), scales=planes, in_=grouped.rearrange("p m t -> p (m t)"))
 
-        group_z(grouped_low[:, early, :], 0, early)
+        group_z(grouped_low[early.start][:], 0, early)
         place_allies(LAST, "raw2_1", 0, "enemy1", 4 * KB)
         back = turn_back(LAST)
-        group_z(grouped_low[:, wide, :], 0, wide)
-        group_z(grouped_low[:, late, :], 0, late)
-        last_enemies = by_slot[:, 0, :].bitcast(F32)
+        group_z(grouped_low[late.start][:], 0, late)
+        for cols in (slice(0, 2 * P), slice(2 * P, BANK)):
+            group_z(grouped_low[0][:, cols, :], 0, cols)
+        last_enemies = slot_rows[:, 0 : 2 * S].bitcast(F32)
         nc.scalar.activation(last_enemies, back[:], ACT.Relu)
-        for cols in (early, wide, late):
-            quantise_z(low_codes, low_planes, grouped_low[:, cols, :], cols)
-        for cols in narrow[:2] + [wide] + narrow[2:]:
-            last_product(0, cols, low_codes, low_planes)
+        for cols in (early, wide):
+            quantise_z(low_codes[:, cols], low_planes[:, cols], grouped_low[cols.start][:])
+        for cols in narrow[:2] + [wide]:
+            last_product(0, cols, low_codes[:, cols], low_planes[:, cols])
 
         for t in range(PACK - 1):
             nc.scalar.activation(by_slot[:, 1 + t, :], pages[PACK + t][:], ACT.Copy, scale=gain_high[:, t : t + 1])
@@ -407,6 +410,10 @@ def tile_list_turn_order_evaluator_kernel(
             grouped_high[cols.start] = held([P, cols.stop - cols.start, PACK], BF16, f"grouped_high{cols.start}", "ally1", 8 * cols.start)
             group_z(grouped_high[cols.start][:], 1, cols)
         scatter(LAST, enemy_slots[:], last_enemies, enemy_weights[LAST])
+        late_codes = held([P, 2 * P], U32, "late_codes", "grouped_low0")[:]
+        quantise_z(late_codes, low_planes[:, late], grouped_low[late.start][:])
+        for n, cols in enumerate(narrow[2:]):
+            last_product(0, cols, late_codes[:, n * P : (n + 1) * P], low_planes[:, cols])
 
         last_gain = gain_high[:, PACK - 1 : PACK]
         high_codes = held([P, T2], U32, "high_codes", "page3")
@@ -417,7 +424,8 @@ def tile_list_turn_order_evaluator_kernel(
             nc.vector.tensor_scalar(grouped, pages[LAST][:, cols], last_gain, None, ALU.mult)
 
         def quantise_high(part, cols):
-            quantise_z(high_codes, high_planes, grouped_high[part.start][:, cols.start - part.start : cols.stop - part.start, :], cols)
+            grouped = grouped_high[part.start][:, cols.start - part.start : cols.stop - part.start, :]
+            quantise_z(high_codes[:, cols], high_planes[:, cols], grouped)
 
         nc.scalar.activation(grouped_high[0][:, 0:SCALAR_SHARE, PACK - 1], pages[LAST][:, 0:SCALAR_SHARE], ACT.Copy, scale=last_gain)
         round_last(right, narrow[0])
@@ -428,7 +436,7 @@ def tile_list_turn_order_evaluator_kernel(
         quantise_high(right, late)
         quantise_high(wide, wide)
         for cols in narrow + [wide]:
-            last_product(1, cols, high_codes, high_planes)
+            last_product(1, cols, high_codes[:, cols], high_planes[:, cols])
 
         by_row_tile = out.rearrange("(n p) m -> p n m", p=P)
         results = held([P, ROW_TILES, T2], F32, "results")

@@ -69,9 +69,9 @@ def tile_list_turn_order_evaluator_kernel(
             nc.sync.dma_start(tile[:].bitcast(I32), src[g].rearrange("p t i -> p (t i)").bitcast(I32))
             return tile
 
-        def cleared(shape, name):
+        def cleared(engine, shape, name):
             tile = held(shape, U8, name)
-            nc.vector.memset(tile[:].bitcast(I32), 0)
+            engine.memset(tile[:].bitcast(I32), 0)
             return tile
 
         def load_table_scales(queue, tile, src):
@@ -109,9 +109,9 @@ def tile_list_turn_order_evaluator_kernel(
                 rows = threat[K_PASS:, :].rearrange("(p t) j -> p t j", t=PACK)[:, i - PACK, :]
             return load_plain(rows, [P, S], f"threat{i}", f"threat_place{i}" if 1 < i < PACK else None)[:]
 
-        ally_scales = cleared([P, T], "ally_scales")
-        enemy_scales = cleared([P, T], "enemy_scales")
-        w4_planes = cleared([P, R_PASSES, N], "w4_planes")
+        ally_scales = cleared(nc.vector, [P, T], "ally_scales")
+        enemy_scales = cleared(nc.gpsimd, [P, T], "enemy_scales")
+        w4_planes = cleared(nc.vector, [P, R_PASSES, N], "w4_planes")
         load_table_scales(nc.scalar, ally_scales, tab_scales)
         load_table_scales(nc.gpsimd, enemy_scales, tab2_scales)
         identity = held([P, P], F32, "identity")
@@ -120,9 +120,8 @@ def tile_list_turn_order_evaluator_kernel(
         ally_list = load_list(offs, "ally_list")
         ally_table = [load_words(tab_words, 0, "ally")]
         raw_low = [load_low_w1(0)]
-        ally_table.append(load_words(tab_words, 1, "ally"))
         enemy_list = load_list(offs2, "enemy_list")
-        ally_table.append(load_words(tab_words, 2, "ally"))
+        ally_table.extend(load_words(tab_words, g, "ally") for g in range(1, K_PASSES))
         wg1_rows = held([P, S], F32, "wg1_rows")
         nc.sync.dma_start(wg1_rows[:, 0 : 2 * P], wg1[:, 0 : 2 * P])
         ally_slots = load_list(offs3, "ally_slots")
@@ -294,8 +293,8 @@ def tile_list_turn_order_evaluator_kernel(
         gather(ally_words[0], ally_table[0], ally_list[:])
         gather(ally_planes[:], ally_scales, ally_list[:])
         low_w1(0)
-        gather(ally_words[1], ally_table[1], ally_list[:])
         gather(enemy_planes[:], enemy_scales, enemy_list[:])
+        gather(ally_words[1], ally_table[1], ally_list[:])
         parts = (slice(0, P), slice(P, 2 * P), slice(2 * P, S))
         for entries in (parts[0], slice(P, S)):
             gather(ally_words[2][:, entries], ally_table[2], ally_list[:, list_cols(entries)])

@@ -30,6 +30,7 @@ ROW_TILES = N // P
 KB = 1024
 ALIGN = 64
 SCALAR_SHARE = 512
+PART = 192
 
 
 def tile_list_turn_order_evaluator_kernel(
@@ -123,10 +124,10 @@ def tile_list_turn_order_evaluator_kernel(
         enemy_list = load_list(offs2, "enemy_list")
         ally_table.extend(load_words(tab_words, g, "ally") for g in range(1, K_PASSES))
         wg1_rows = held([P, S], F32, "wg1_rows")
-        nc.sync.dma_start(wg1_rows[:, 0 : 2 * P], wg1[:, 0 : 2 * P])
+        nc.sync.dma_start(wg1_rows[:, 0 : P + PART], wg1[:, 0 : P + PART])
         ally_slots = load_list(offs3, "ally_slots")
         raw_low.append(load_low_w1(1))
-        nc.sync.dma_start(wg1_rows[:, 2 * P :], wg1[:, 2 * P :])
+        nc.sync.dma_start(wg1_rows[:, P + PART :], wg1[:, P + PART :])
         raw_low.append(load_low_w1(2))
         enemy_table = [load_words(tab2_words, g, "enemy") for g in range(K_PASSES - 1)]
         raw_low.append(load_low_w1(3))
@@ -204,7 +205,7 @@ def tile_list_turn_order_evaluator_kernel(
             )
             quantise_w1(PACK + 2 * h, 2, g, staged)
 
-        def ally_values(i, values, bank, entries):
+        def ally_sums(i, bank, entries):
             count = entries.stop - entries.start
             runs = ((0, P), (P, count)) if count == 3 * P else ((0, count),)
             steps = [(g, run) for g in range(K_PASSES) for run in runs]
@@ -215,14 +216,17 @@ def tile_list_turn_order_evaluator_kernel(
                     rhs=ally_words[g][:, cols].bitcast(FP8X4), rhs_scale=ally_planes[4 * g :, cols],
                     start=(n == 0), stop=(n == len(steps) - 1),
                 )
-            nc.scalar.activation(values, bank[:, 0:count], ACT.Sigmoid)
+
+        def ally_values(i, values, bank, entries):
+            ally_sums(i, bank, entries)
+            nc.scalar.activation(values, bank[:, 0 : entries.stop - entries.start], ACT.Sigmoid)
 
         def scatter(i, offsets, values, weights):
             nc.vector.tensor_tensor(pages[i][:].indirect(offsets), values, weights, ALU.mult)
 
         def place_allies(i, values_over, values_at, page_over, page_at):
             values = held([P, S], F32, f"allies{i}", values_over, values_at)
-            ally_values(i, values[:], banks[(0, 0, 6, 6, 4, 5, 5, 4)[i]], all_entries)
+            ally_values(i, values[:], banks[(0, 0, 1, 6, 4, 5, 5, 4)[i]], all_entries)
             pages[i] = held([P, T2], F32, f"page{i}", page_over, page_at)
             scatter(i, ally_slots[:], values[:], ally_weights[i])
 
@@ -295,22 +299,29 @@ def tile_list_turn_order_evaluator_kernel(
         low_w1(0)
         gather(enemy_planes[:], enemy_scales, enemy_list[:])
         gather(ally_words[1], ally_table[1], ally_list[:])
-        parts = (slice(0, P), slice(P, 2 * P), slice(2 * P, S))
+        parts = (slice(0, P), slice(P, P + PART), slice(P + PART, S))
         for entries in (parts[0], slice(P, S)):
             gather(ally_words[2][:, entries], ally_table[2], ally_list[:, list_cols(entries)])
         pages[0] = held([P, T2], F32, "page0", "ally1", 0)
-        for n, entries in enumerate(parts):
-            count = entries.stop - entries.start
-            if n == 0:
-                values = held([P, count], F32, "allies0_0")
-            else:
-                low_w1(1, n - 1, 2 * n - 1)
-                values = held([P, count], F32, f"allies0_{n}", f"raw1_{2 * n - 2}", KB)
-            ally_values(0, values[:], banks[(0, 6, 1)[n]], entries)
+        values = held([P, P], F32, "allies0_0")
+        ally_values(0, values[:], banks[0], parts[0])
+        scatter(0, ally_slots[:, list_cols(parts[0])], values[:], wg1_rows[:, parts[0]])
+        ally_sums(0, banks[6], slice(P, S))
+        for n, entries in enumerate(parts[1:]):
+            low_w1(1, n, 2 * n + 1)
+            values = held([P, PART], F32, f"allies0_{n + 1}", f"raw1_{2 * n}", KB)
+            nc.scalar.activation(values[:], banks[6][:, entries.start - P : entries.stop - P], ACT.Sigmoid)
             scatter(0, ally_slots[:, list_cols(entries)], values[:], wg1_rows[:, entries])
 
-        place_allies(1, "ally2", 0, "ally1", 4 * KB)
-        low_w1(2)
+        pages[1] = held([P, T2], F32, "page1", "ally1", 4 * KB)
+        for n, entries in enumerate((slice(0, S // 2), slice(S // 2, S))):
+            if n == 0:
+                values = held([P, S // 2], F32, "allies1_0", "ally2")
+            else:
+                low_w1(2)
+                values = held([P, S // 2], F32, "allies1_1", "raw2_2", KB)
+            ally_values(1, values[:], banks[(0, 1)[n]], entries)
+            scatter(1, ally_slots[:, list_cols(entries)], values[:], wg1_rows[:, entries])
         enemy_picked = held([P, K_PASSES * S], U32, "enemy_picked", "ally0")
         enemy_words = [enemy_picked[:, g * S : (g + 1) * S] for g in range(K_PASSES)]
         for g in range(K_PASSES - 1):

@@ -29,7 +29,7 @@ LAST = TILES - 1
 ROW_TILES = N // P
 KB = 1024
 ALIGN = 64
-SCALAR_SHARE = 512
+SCALAR_SHARE = 384
 PART = 192
 
 
@@ -270,7 +270,7 @@ def tile_list_turn_order_evaluator_kernel(
             nc.scalar.activation(values, back[:], ACT.Relu)
             scatter(i, enemy_slots[:], values, enemy_weights[i])
 
-        narrow = [slice(BANK + n * P, BANK + (n + 1) * P) for n in range((T2 - BANK) // P)]
+        narrow = [slice(T2 - (n + 1) * P, T2 - n * P) for n in range((T2 - BANK) // P)]
 
         def last_product(a, cols, codes, planes):
             wide_piece = cols.start == 0
@@ -332,7 +332,7 @@ def tile_list_turn_order_evaluator_kernel(
             values = held([P, S // 2], F32, f"allies2_{n}", f"raw3_{2 * n}", KB // 4)
             ally_values(2, values[:], banks[(6, 1)[n]], entries)
             scatter(2, ally_slots[:, list_cols(entries)], values[:], wg1_rows[:, entries])
-        for entries in (slice(0, 2 * P), squares[2], squares[3]):
+        for entries in (slice(0, S // 2), slice(S // 2, S)):
             gather(enemy_words[2][:, entries], enemy_table[2], enemy_list[:, list_cols(entries)])
         turn_threat(0)
         place_allies(3, "ally2", 2 * KB, "ally2", 4 * KB)
@@ -349,11 +349,11 @@ def tile_list_turn_order_evaluator_kernel(
         def rounded_rows(i, over, at=0):
             return held([P, T2], BF16, f"rounded{i}", over, at)[:]
 
-        turned_sums(0, ((2, (0, 1), ("round3", KB // 4)), (3, (2,), ("round3", 4 * KB - KB // 4)), (7, (3,), ("round3", 5 * KB - KB // 4))))
+        turned_sums(0, ((2, (0, 1), ("round3", KB // 4)), (3, (2, 3), ("round3", 4 * KB - KB // 4))))
         values = enemy_values(0, "ally_scales")
-        for members, bank in ((range(PACK - 1), 4), (range(PACK - 1, PACK), 0)):
-            cols = slice(members[0] * P, (members[-1] + 1) * P)
-            nc.scalar.activation(values[:, cols], turn_back(0, members, bank)[:, cols], ACT.Relu)
+        for members, bank in ((range(2), 4), (range(2, PACK), 0)):
+            entries = slice(members[0] * P, (members[-1] + 1) * P)
+            nc.scalar.activation(values[:, entries], turn_back(0, members, bank)[:, entries], ACT.Relu)
         scatter(0, enemy_slots[:], values, enemy_weights[0])
         turn_threat(1)
         back = turn_back(1)
@@ -389,11 +389,12 @@ def tile_list_turn_order_evaluator_kernel(
         place_enemies(5, turn_back(5), enemy_values(5, "rounded0"))
         turned_sums(3, ((2, (0, 1), ("raw1_0", 0)), (3, (2, 3), ("raw1_1", 0))))
         place_enemies(6, turn_back(6), enemy_values(6, "rounded1"))
-        wide, early, late = slice(0, BANK), slice(BANK, BANK + 2 * P), slice(BANK + 2 * P, T2)
+        wide, late, early = slice(0, BANK), slice(BANK, BANK + 2 * P), slice(BANK + 2 * P, T2)
         grouped_low = {
             cols.start: held([P, cols.stop - cols.start, PACK], BF16, f"grouped_low{cols.start}") for cols in (wide, early, late)
         }
-        low_codes = held([P, late.start], U32, "low_codes")
+        low_codes = held([P, BANK], U32, "low_codes")
+        early_codes = held([P, 2 * P], U32, "early_codes")
         low_planes = held([P, T2], U8, "low_planes")
 
         def quantise_z(codes, planes, grouped):
@@ -407,23 +408,24 @@ def tile_list_turn_order_evaluator_kernel(
             group_z(grouped_low[0][:, cols, :], 0, cols)
         last_enemies = slot_rows[:, 0 : 2 * S].bitcast(F32)
         nc.scalar.activation(last_enemies, back[:], ACT.Relu)
-        for cols in (early, wide):
-            quantise_z(low_codes[:, cols], low_planes[:, cols], grouped_low[cols.start][:])
-        for cols in narrow[:2] + [wide]:
-            last_product(0, cols, low_codes[:, cols], low_planes[:, cols])
+        quantise_z(early_codes[:], low_planes[:, early], grouped_low[early.start][:])
+        quantise_z(low_codes[:], low_planes[:, wide], grouped_low[0][:])
+        for cols in narrow[:2]:
+            last_product(0, cols, early_codes[:, cols.start - early.start : cols.stop - early.start], low_planes[:, cols])
+        last_product(0, wide, low_codes[:], low_planes[:, wide])
 
         for t in range(PACK - 1):
             nc.scalar.activation(by_slot[:, 1 + t, :], pages[PACK + t][:], ACT.Copy, scale=gain_high[:, t : t + 1])
         grouped_high = {}
-        right = slice(BANK, T2)
-        for cols in (wide, right):
+        left, middle = slice(0, SCALAR_SHARE), slice(SCALAR_SHARE, early.start)
+        for cols in (early, left, middle):
             grouped_high[cols.start] = held([P, cols.stop - cols.start, PACK], BF16, f"grouped_high{cols.start}", "ally1", 8 * cols.start)
             group_z(grouped_high[cols.start][:], 1, cols)
         scatter(LAST, enemy_slots[:], last_enemies, enemy_weights[LAST])
         late_codes = held([P, 2 * P], U32, "late_codes", "grouped_low0")[:]
         quantise_z(late_codes, low_planes[:, late], grouped_low[late.start][:])
-        for n, cols in enumerate(narrow[2:]):
-            last_product(0, cols, late_codes[:, n * P : (n + 1) * P], low_planes[:, cols])
+        for cols in narrow[2:]:
+            last_product(0, cols, late_codes[:, cols.start - late.start : cols.stop - late.start], low_planes[:, cols])
 
         last_gain = gain_high[:, PACK - 1 : PACK]
         high_codes = held([P, T2], U32, "high_codes", "page3")
@@ -438,13 +440,16 @@ def tile_list_turn_order_evaluator_kernel(
             quantise_z(high_codes[:, cols], high_planes[:, cols], grouped)
 
         nc.scalar.activation(grouped_high[0][:, 0:SCALAR_SHARE, PACK - 1], pages[LAST][:, 0:SCALAR_SHARE], ACT.Copy, scale=last_gain)
-        round_last(right, narrow[0])
-        round_last(right, slice(narrow[1].start, narrow[2].stop))
-        quantise_high(right, narrow[0])
-        round_last(right, narrow[3])
-        quantise_high(right, narrow[1])
-        quantise_high(right, late)
-        quantise_high(wide, wide)
+        rest = slice(SCALAR_SHARE, BANK)
+        for cols in narrow[:2]:
+            round_last(early, cols)
+        for cols in narrow[:2]:
+            quantise_high(early, cols)
+        for cols in (late, rest):
+            round_last(middle, cols)
+        for cols in (late, rest):
+            quantise_high(middle, cols)
+        quantise_high(left, left)
         for cols in narrow + [wide]:
             last_product(1, cols, high_codes[:, cols], high_planes[:, cols])
 
@@ -455,14 +460,12 @@ def tile_list_turn_order_evaluator_kernel(
                 result, source = results[:, :, narrow[b]], bank[:].rearrange("p (n m) -> p n m", m=P)
             else:
                 result, source = results[:, b - len(narrow), wide], bank[:]
-            if b >= 2 and b % 2 == 0:
+            if b >= 3 and b % 2 == 1:
                 nc.vector.tensor_copy(result, source)
             else:
                 nc.scalar.copy(result, source)
-            if b < 2:
+            if b < len(narrow):
                 nc.sync.dma_start(by_row_tile[:, :, narrow[b]], result)
-            elif b == len(narrow) - 1:
-                nc.sync.dma_start(by_row_tile[:, :, late], results[:, :, late])
             elif b % 2 == 1:
                 pair = slice(b - len(narrow) - 1, b - len(narrow) + 1)
                 nc.sync.dma_start(by_row_tile[:, pair, wide], results[:, pair, wide])

from contextlib import ExitStack

import concourse.mybir as mybir
from concourse.masks import make_identity

K, T, S, T2, H, N = 1536, 2048, 512, 1024, 1024, 512
FLOPS = 2 * (2 * K * H * S + H * N * T2)

F32 = mybir.dt.float32
BF16 = mybir.dt.bfloat16
I32 = mybir.dt.int32
U32 = mybir.dt.uint32
U16 = mybir.dt.uint16
U8 = mybir.dt.uint8
FP8X4 = mybir.dt.float8_e4m3fn_x4
FP4X4 = mybir.dt.float4_e2m1fn_x4
ALU = mybir.AluOpType
ACT = mybir.ActivationFunctionType

P = 128
PACK = 4
QUADRANTS = 4
K_PASS = P * PACK
K_PASSES = K // K_PASS
R_PASSES = H // K_PASS
BANK = 512
TILES = H // P
LAST = TILES - 1
ROW_TILES = N // P
KB = 1024
ALIGN = 64
SCALAR_SHARE = 384
PART = 192


def tile_list_turn_order_evaluator_kernel(
    tc, tab_words, tab_scales, tab2_words, tab2_scales, w1, w4_words, w4_scales,
    threat, gain, wg1, wg2, offs, offs2, offs3, offs4, out,
):
    nc = tc.nc
    with ExitStack() as ctx:
        lists = ctx.enter_context(tc.tile_pool(name="lists", bufs=1))
        keep = ctx.enter_context(tc.tile_pool(name="keep", bufs=1))
        psum = ctx.enter_context(tc.psum_pool(name="psum", bufs=1))

        width_of = {F32: 4, U32: 4, BF16: 2, U8: 1}
        starts = {"free": 0}

        def reserve(name, size):
            starts[name] = starts["free"]
            starts["free"] = starts["free"] + -(-size // ALIGN) * ALIGN

        def held(shape, dtype, name, over=None, at=0):
            if over is None:
                size = width_of[dtype]
                for extent in shape[1:]:
                    size = size * extent
                reserve(name, size)
            else:
                starts[name] = starts[over] + at
            return keep.tile(shape, dtype, name=name, tag=name, align_bytes=ALIGN, offset=starts[name])

        def load_list(src, name):
            tile = lists.tile([P, S // 16], U16, name=name)
            nc.sync.dma_start(tile[:], src)
            return tile

        def load_words(src, g, name):
            tile = held([P, T], U32, f"{name}{g}")
            nc.sync.dma_start(tile[:].bitcast(I32), src[g].rearrange("p t i -> p (t i)").bitcast(I32))
            return tile

        def cleared(engine, shape, name):
            tile = held(shape, U8, name)
            engine.memset(tile[:].bitcast(I32), 0)
            return tile

        def load_table_scales(queue, tile, src):
            for q in range(QUADRANTS):
                rows = tile[32 * q : 32 * q + 4 * K_PASSES, :]
                queue.dma_start(rows.bitcast(I32), src[:, 4 * q : 4 * q + 4, :].bitcast(I32))

        def load_w1(first, width, g, name, over=None, at=0):
            tile = held([P, PACK * width], F32, name, over, at)
            rows = w1[g * K_PASS : (g + 1) * K_PASS, first : first + width]
            nc.sync.dma_start(tile[:].rearrange("p (j c) -> p j c", j=PACK), rows.rearrange("(p j) c -> p j c", j=PACK))
            return tile[:].rearrange("p (j c) -> p j c", j=PACK)

        def load_low_w1(i):
            tiles = [load_w1(i * P, P, g, f"raw{i}_{g}") for g in range(K_PASSES - 1)]
            reserve(f"round{i}", 6 * KB if i == 3 else 2 * KB)
            return tiles + [load_w1(i * P, P, 2, f"raw{i}_2", f"round{i}", 2 * KB if i == 3 else 0)]

        def load_plain(src, shape, name, over=None, at=0):
            tile = held(shape, F32, name, over, at)
            nc.sync.dma_start(tile[:], src)
            return tile

        def load_high_weights(src, t, name):
            target = held([P, S], F32, name)
            rows = src.rearrange("(q t) j -> q t j", t=PACK)[:, t, :]
            for q in range(QUADRANTS):
                nc.sync.dma_start(target[32 * q : 32 * (q + 1), :], rows)
            return target[:]

        def load_threat(i):
            if i < PACK:
                rows = threat[i * P : (i + 1) * P, :]
            else:
                rows = threat[K_PASS:, :].rearrange("(p t) j -> p t j", t=PACK)[:, i - PACK, :]
            return load_plain(rows, [P, S], f"threat{i}", f"threat_place{i}" if 1 < i < PACK else None)[:]

        ally_scales = cleared(nc.vector, [P, T], "ally_scales")
        enemy_scales = cleared(nc.gpsimd, [P, T], "enemy_scales")
        w4_planes = cleared(nc.vector, [P, R_PASSES, N], "w4_planes")
        load_table_scales(nc.scalar, ally_scales, tab_scales)
        load_table_scales(nc.gpsimd, enemy_scales, tab2_scales)
        identity = held([P, P], F32, "identity")
        make_identity(nc, identity[:])

        ally_list = load_list(offs, "ally_list")
        ally_table = [load_words(tab_words, 0, "ally")]
        raw_low = [load_low_w1(0)]
        enemy_list = load_list(offs2, "enemy_list")
        ally_table.extend(load_words(tab_words, g, "ally") for g in range(1, K_PASSES))
        wg1_rows = held([P, S], F32, "wg1_rows")
        nc.sync.dma_start(wg1_rows[:, 0 : P + PART], wg1[:, 0 : P + PART])
        ally_slots = load_list(offs3, "ally_slots")
        raw_low.append(load_low_w1(1))
        nc.sync.dma_start(wg1_rows[:, P + PART :], wg1[:, P + PART :])
        raw_low.append(load_low_w1(2))
        enemy_table = [load_words(tab2_words, g, "enemy") for g in range(K_PASSES - 1)]
        raw_low.append(load_low_w1(3))
        threat_rows = [load_threat(0)]
        enemy_slots = load_list(offs4, "enemy_slots")
        enemy_table.append(load_words(tab2_words, K_PASSES - 1, "enemy"))
        threat_rows.append(load_threat(1))
        reserve("wg2_place", 2 * KB)
        for i in range(2, PACK):
            reserve(f"threat_place{i}", 2 * KB)
        reserve("slot_place", 3 * KB // 2)
        raw_high = [load_w1(K_PASS, K_PASS, 0, "high0")]
        wg2_rows = load_plain(wg2, [P, S], "wg2_rows", "wg2_place")
        threat_rows.extend(load_threat(i) for i in range(2, PACK))
        raw_high.extend(load_w1(K_PASS, K_PASS, g, f"high{g}") for g in range(1, K_PASSES))
        gain_low = held([P, PACK], F32, "gain_low")
        with nc.allow_non_contiguous_dma(reason="one gain a partition and low tile"):
            nc.sync.dma_start(gain_low[:], gain[0:K_PASS].rearrange("(i p) -> p i", p=P))
        gain_high = load_plain(gain[K_PASS:].rearrange("(p t) -> p t", t=PACK), [P, PACK], "gain_high")
        ally_weights = [wg1_rows[:]] * PACK
        enemy_weights = [wg2_rows[:]] * PACK
        threat_rows.extend(load_threat(PACK + t) for t in range(PACK))
        for t in range(PACK):
            if t < PACK - 1:
                ally_weights.append(load_high_weights(wg1, t, f"wg1_slot{t}"))
            if t > 0:
                enemy_weights.append(load_high_weights(wg2, t - 1, f"wg2_slot{t - 1}"))
        ally_weights.append(load_high_weights(wg1, PACK - 1, "wg1_slot3"))
        enemy_weights.append(load_high_weights(wg2, PACK - 1, "wg2_slot3"))
        w4_codes = held([P, R_PASSES, 2 * N], U8, "w4_codes")
        nc.sync.dma_start(w4_codes[:].bitcast(I32), w4_words.rearrange("a p c -> p a c").bitcast(I32))
        for q in range(QUADRANTS):
            nc.sync.dma_start(
                w4_planes[32 * q : 32 * q + 4, :, :].bitcast(I32),
                w4_scales[:, 4 * q : 4 * q + 4, :].rearrange("a s n -> s a n").bitcast(I32),
            )

        banks = [psum.tile([P, BANK], F32, name=f"bank{b}") for b in range(8)]
        pages = {}
        w1_codes, w1_planes, pair_codes, pair_planes, turned_squares = {}, {}, {}, {}, {}
        squares = [slice(c * P, (c + 1) * P) for c in range(S // P)]
        all_entries = slice(0, S)

        def list_cols(entries):
            return slice(entries.start // 16, entries.stop // 16)

        def gather(picked, window, offsets):
            nc.vector.tensor_copy(picked, window[:].indirect(offsets))

        def quantise_w1(first_tile, count, g, staged):
            pair = first_tile // 2
            if first_tile % 2 == 0:
                pair_codes[pair, g] = held([P, 2 * P], U32, f"w1_codes{pair}_{g}")
                pair_planes[pair, g] = held([P, 2 * P], U8, f"w1_planes{pair}_{g}")
                for u in range(2):
                    w1_codes[first_tile + u, g] = pair_codes[pair, g][:, u * P : (u + 1) * P]
                    w1_planes[first_tile + u, g] = pair_planes[pair, g][:, u * P : (u + 1) * P]
            cols = slice(first_tile % 2 * P, (first_tile % 2 + count) * P)
            nc.vector.quantize_mx(out=pair_codes[pair, g][:, cols].bitcast(FP8X4), scales=pair_planes[pair, g][:, cols], in_=staged[:])

        def low_w1(i, lo=0, hi=K_PASSES):
            for g in range(lo, hi):
                staged = held([P, K_PASS], BF16, f"staged{i}_{g}", f"raw{i - 1}_{min(g, 1)}" if i else None, KB * (g // 2))
                nc.scalar.copy(
                    staged[:].rearrange("p (c i j) -> p c j i", i=4, j=PACK),
                    raw_low[i][g].rearrange("p j (c i) -> p c j i", i=4),
                )
                quantise_w1(i, 1, g, staged)

        def high_w1(h, g, over, at=0):
            staged = held([P, 2 * K_PASS], BF16, f"staged_high{h}_{g}", over, at)
            nc.scalar.copy(
                staged[:].rearrange("p (t m j) -> p m j t", t=2, j=PACK),
                raw_high[g].rearrange("p j (m t) -> p m j t", t=PACK)[:, :, :, 2 * h : 2 * h + 2],
            )
            quantise_w1(PACK + 2 * h, 2, g, staged)

        def ally_sums(i, bank, entries):
            count = entries.stop - entries.start
            runs = ((0, P), (P, count)) if count == 3 * P else ((0, count),)
            steps = [(g, run) for g in range(K_PASSES) for run in runs]
            for n, (g, (lo, hi)) in enumerate(steps):
                cols = slice(entries.start + lo, entries.start + hi)
                nc.tensor.matmul_mx(
                    out=bank[:, lo:hi], lhsT=w1_codes[i, g].bitcast(FP8X4), lhsT_scale=w1_planes[i, g],
                    rhs=ally_words[g][:, cols].bitcast(FP8X4), rhs_scale=ally_planes[4 * g :, cols],
                    start=(n == 0), stop=(n == len(steps) - 1),
                )

        def ally_values(i, values, bank, entries):
            ally_sums(i, bank, entries)
            nc.scalar.activation(values, bank[:, 0 : entries.stop - entries.start], ACT.Sigmoid)

        def scatter(i, offsets, values, weights):
            nc.vector.tensor_tensor(pages[i][:].indirect(offsets), values, weights, ALU.mult)

        def place_allies(i, values_over, values_at, page_over, page_at):
            values = held([P, S], F32, f"allies{i}", values_over, values_at)
            ally_values(i, values[:], banks[(0, 0, 1, 6, 4, 5, 5, 4)[i]], all_entries)
            pages[i] = held([P, T2], F32, f"page{i}", page_over, page_at)
            scatter(i, ally_slots[:], values[:], ally_weights[i])

        def turn_threat(i):
            turned = banks[(6, 2, 6, 1, 6, 7, 2, 3)[i]]
            for sq in squares:
                nc.tensor.transpose(turned[:, sq], threat_rows[i][:, sq], identity[:])
            nc.scalar.activation(threat_rows[i], turned[:], ACT.Copy, scale=-1.0)

        def turned_sums(pair, groups):
            for h, (bank, members, place) in enumerate(groups):
                width = 2 * P * len(members)
                steps = [(g, n) for g in range(K_PASSES) for n in range(len(members))]
                for step, (g, n) in enumerate(steps):
                    sq = squares[members[n]]
                    nc.tensor.matmul_mx(
                        out=banks[bank][:, 2 * P * n : 2 * P * (n + 1)],
                        lhsT=enemy_words[g][:, sq].bitcast(FP8X4), lhsT_scale=enemy_planes[4 * g :, sq],
                        rhs=pair_codes[pair, g][:].bitcast(FP8X4), rhs_scale=pair_planes[pair, g][:],
                        start=(step == 0), stop=(step == len(steps) - 1),
                    )
                tile = held([P, width], F32, f"turned_sums{pair}_{h}", *place)
                nc.scalar.copy(tile[:], banks[bank][:, 0:width])
                for n, c in enumerate(members):
                    for u in range(2):
                        turned_squares[2 * pair + u, c] = tile[:, (2 * n + u) * P : (2 * n + u + 1) * P]

        def turn_back(i, members=range(PACK), bank=None):
            back = banks[(4, 5, 4, 5, 5, 4, 4, 6)[i] if bank is None else bank]
            terms = [(threat_rows[i][:, squares[c]], squares[c]) for c in members[:-1]]
            terms.extend((turned_squares[i, c], squares[c]) for c in members)
            terms.append((threat_rows[i][:, squares[members[-1]]], squares[members[-1]]))
            for n, (term, sq) in enumerate(terms):
                nc.tensor.matmul(
                    back[:, sq], lhsT=term, rhs=identity[:], is_transpose=True,
                    start=(n == 0), stop=(n == len(terms) - 1),
                )
            return back

        def place_enemies(i, back, values):
            nc.scalar.activation(values, back[:], ACT.Relu)
            scatter(i, enemy_slots[:], values, enemy_weights[i])

        narrow = [slice(T2 - (n + 1) * P, T2 - n * P) for n in range((T2 - BANK) // P)]

        def last_product(a, cols, codes, planes):
            wide_piece = cols.start == 0
            for nt in range(ROW_TILES):
                sums = banks[len(narrow) + nt][:] if wide_piece else banks[narrow.index(cols)][:, nt * P : (nt + 1) * P]
                nc.tensor.matmul_mx(
                    out=sums,
                    lhsT=w4_codes[:, a, 2 * P * nt : 2 * P * (nt + 1)].bitcast(FP4X4),
                    lhsT_scale=w4_planes[:, a, P * nt : P * (nt + 1)],
                    rhs=codes.bitcast(FP8X4), rhs_scale=planes,
                    start=(a == 0 and (wide_piece or nt == 0)),
                    stop=(a == R_PASSES - 1 and (wide_piece or nt == ROW_TILES - 1)),
                )

        def group_z(grouped, first_row, cols):
            nc.scalar.copy(
                grouped.rearrange("p (c i) t -> p c t i", i=4),
                by_slot[:, first_row : first_row + PACK, cols].rearrange("p t (c i) -> p c t i", i=4),
            )

        ally_words = [held([P, S], U32, f"ally_picked{g}")[:] for g in range(K_PASSES)]
        ally_planes = held([P, S], U8, "ally_planes")
        enemy_planes = held([P, S], U8, "enemy_planes")
        gather(ally_words[0], ally_table[0], ally_list[:])
        gather(ally_planes[:], ally_scales, ally_list[:])
        low_w1(0)
        gather(enemy_planes[:], enemy_scales, enemy_list[:])
        gather(ally_words[1], ally_table[1], ally_list[:])
        parts = (slice(0, P), slice(P, P + PART), slice(P + PART, S))
        for entries in (parts[0], slice(P, S)):
            gather(ally_words[2][:, entries], ally_table[2], ally_list[:, list_cols(entries)])
        pages[0] = held([P, T2], F32, "page0", "ally1", 0)
        values = held([P, P], F32, "allies0_0")
        ally_values(0, values[:], banks[0], parts[0])
        scatter(0, ally_slots[:, list_cols(parts[0])], values[:], wg1_rows[:, parts[0]])
        ally_sums(0, banks[6], slice(P, S))
        for n, entries in enumerate(parts[1:]):
            low_w1(1, n, 2 * n + 1)
            values = held([P, PART], F32, f"allies0_{n + 1}", f"raw1_{2 * n}", KB)
            nc.scalar.activation(values[:], banks[6][:, entries.start - P : entries.stop - P], ACT.Sigmoid)
            scatter(0, ally_slots[:, list_cols(entries)], values[:], wg1_rows[:, entries])

        pages[1] = held([P, T2], F32, "page1", "ally1", 4 * KB)
        for n, entries in enumerate((slice(0, S // 2), slice(S // 2, S))):
            if n == 0:
                values = held([P, S // 2], F32, "allies1_0", "ally2")
            else:
                low_w1(2)
                values = held([P, S // 2], F32, "allies1_1", "raw2_2", KB)
            ally_values(1, values[:], banks[(0, 1)[n]], entries)
            scatter(1, ally_slots[:, list_cols(entries)], values[:], wg1_rows[:, entries])
        enemy_picked = held([P, K_PASSES * S], U32, "enemy_picked", "ally0")
        enemy_words = [enemy_picked[:, g * S : (g + 1) * S] for g in range(K_PASSES)]
        for g in range(K_PASSES - 1):
            gather(enemy_words[g], enemy_table[g], enemy_list[:])
        pages[2] = held([P, T2], F32, "page2")
        for n, entries in enumerate((slice(0, S // 2), slice(S // 2, S))):
            low_w1(3, n, 2 * n + 1)
            values = held([P, S // 2], F32, f"allies2_{n}", f"raw3_{2 * n}", KB // 4)
            ally_values(2, values[:], banks[(6, 1)[n]], entries)
            scatter(2, ally_slots[:, list_cols(entries)], values[:], wg1_rows[:, entries])
        for entries in (slice(0, S // 2), slice(S // 2, S)):
            gather(enemy_words[2][:, entries], enemy_table[2], enemy_list[:, list_cols(entries)])
        turn_threat(0)
        place_allies(3, "ally2", 2 * KB, "ally2", 4 * KB)

        def enemy_values(i, over, at=0):
            return held([P, S], F32, f"enemies{i}", over, at)[:]

        rounded = {}

        def low_gain(i, target):
            rounded[i] = target
            nc.scalar.activation(target, pages[i][:], ACT.Copy, scale=gain_low[:, i : i + 1])

        def rounded_rows(i, over, at=0):
            return held([P, T2], BF16, f"rounded{i}", over, at)[:]

        turned_sums(0, ((2, (0, 1), ("round3", KB // 4)), (3, (2, 3), ("round3", 4 * KB - KB // 4))))
        values = enemy_values(0, "ally_scales")
        for members, bank in ((range(2), 4), (range(2, PACK), 0)):
            entries = slice(members[0] * P, (members[-1] + 1) * P)
            nc.scalar.activation(values[:, entries], turn_back(0, members, bank)[:, entries], ACT.Relu)
        scatter(0, enemy_slots[:], values, enemy_weights[0])
        turn_threat(1)
        back = turn_back(1)
        high_w1(0, 0, "threat0")
        place_enemies(1, back, enemy_values(1, "enemy_scales"))
        turn_threat(2)
        turn_threat(3)
        turned_sums(1, ((2, (0, 1), ("turned_sums0_0", 0)), (3, (2, 3), ("turned_sums0_1", 0))))
        place_enemies(2, turn_back(2), enemy_values(2, "raw0_0"))
        back = turn_back(3)
        high_w1(0, 1, "threat1")
        high_w1(0, 2, "raw2_2")
        high_w1(1, 2, "raw0_1")
        place_enemies(3, back, enemy_values(3, "high2"))
        low_gain(0, rounded_rows(0, "threat2"))
        low_gain(1, rounded_rows(1, "threat3"))
        low_gain(2, rounded_rows(2, "high2", 6 * KB))
        place_allies(4, "raw2_0", 0, "enemy0", 0)
        for g in range(K_PASSES - 1):
            high_w1(1, g, "high2", (g + 1) * 2 * KB)
        place_allies(5, "high1", 2 * KB, "enemy0", 4 * KB)
        slot_rows = held([P, 6 * P + (PACK + 1) * T2], BF16, "slot_rows", "slot_place")
        by_slot = slot_rows[:, 6 * P :].rearrange("p (t m) -> p t m", m=T2)
        turn_threat(4)
        turned_sums(2, ((2, (0, 1), ("raw3_1", 0)), (3, (2, 3), ("raw0_2", 0))))
        place_enemies(4, turn_back(4), enemy_values(4, "high1", 4 * KB))
        low_gain(3, by_slot[:, PACK, :])
        for i in range(PACK):
            nc.sync.dma_start(by_slot[32 * i : 32 * (i + 1), 0:PACK, :], rounded[i])
        for i in range(PACK + 1, TILES):
            turn_threat(i)
        place_allies(6, "high1", 6 * KB, "enemy1", 0)
        place_enemies(5, turn_back(5), enemy_values(5, "rounded0"))
        turned_sums(3, ((2, (0, 1), ("raw1_0", 0)), (3, (2, 3), ("raw1_1", 0))))
        place_enemies(6, turn_back(6), enemy_values(6, "rounded1"))
        wide, late, early = slice(0, BANK), slice(BANK, BANK + 2 * P), slice(BANK + 2 * P, T2)
        grouped_low = {
            cols.start: held([P, cols.stop - cols.start, PACK], BF16, f"grouped_low{cols.start}") for cols in (wide, early, late)
        }
        low_codes = held([P, BANK], U32, "low_codes")
        early_codes = held([P, 2 * P], U32, "early_codes")
        low_planes = held([P, T2], U8, "low_planes")

        def quantise_z(codes, planes, grouped):
            nc.vector.quantize_mx(out=codes.bitcast(FP8X4), scales=planes, in_=grouped.rearrange("p m t -> p (m t)"))

        group_z(grouped_low[early.start][:], 0, early)
        place_allies(LAST, "raw2_1", 0, "enemy1", 4 * KB)
        back = turn_back(LAST)
        group_z(grouped_low[late.start][:], 0, late)
        for cols in (slice(0, 2 * P), slice(2 * P, BANK)):
            group_z(grouped_low[0][:, cols, :], 0, cols)
        last_enemies = slot_rows[:, 0 : 2 * S].bitcast(F32)
        nc.scalar.activation(last_enemies, back[:], ACT.Relu)
        quantise_z(early_codes[:], low_planes[:, early], grouped_low[early.start][:])
        quantise_z(low_codes[:], low_planes[:, wide], grouped_low[0][:])
        for cols in narrow[:2]:
            last_product(0, cols, early_codes[:, cols.start - early.start : cols.stop - early.start], low_planes[:, cols])
        last_product(0, wide, low_codes[:], low_planes[:, wide])

        for t in range(PACK - 1):
            nc.scalar.activation(by_slot[:, 1 + t, :], pages[PACK + t][:], ACT.Copy, scale=gain_high[:, t : t + 1])
        grouped_high = {}
        left, middle = slice(0, SCALAR_SHARE), slice(SCALAR_SHARE, early.start)
        for cols in (early, left, middle):
            grouped_high[cols.start] = held([P, cols.stop - cols.start, PACK], BF16, f"grouped_high{cols.start}", "ally1", 8 * cols.start)
            group_z(grouped_high[cols.start][:], 1, cols)
        scatter(LAST, enemy_slots[:], last_enemies, enemy_weights[LAST])
        late_codes = held([P, 2 * P], U32, "late_codes", "grouped_low0")[:]
        quantise_z(late_codes, low_planes[:, late], grouped_low[late.start][:])
        for cols in narrow[2:]:
            last_product(0, cols, late_codes[:, cols.start - late.start : cols.stop - late.start], low_planes[:, cols])

        last_gain = gain_high[:, PACK - 1 : PACK]
        high_codes = held([P, T2], U32, "high_codes", "page3")
        high_planes = held([P, T2], U8, "high_planes")

        def round_last(part, cols):
            grouped = grouped_high[part.start][:, cols.start - part.start : cols.stop - part.start, PACK - 1]
            nc.vector.tensor_scalar(grouped, pages[LAST][:, cols], last_gain, None, ALU.mult)

        def quantise_high(part, cols):
            grouped = grouped_high[part.start][:, cols.start - part.start : cols.stop - part.start, :]
            quantise_z(high_codes[:, cols], high_planes[:, cols], grouped)

        nc.scalar.activation(grouped_high[0][:, 0:SCALAR_SHARE, PACK - 1], pages[LAST][:, 0:SCALAR_SHARE], ACT.Copy, scale=last_gain)
        rest = slice(SCALAR_SHARE, BANK)
        for cols in narrow[:2]:
            round_last(early, cols)
        for cols in narrow[:2]:
            quantise_high(early, cols)
        for cols in (late, rest):
            round_last(middle, cols)
        for cols in (late, rest):
            quantise_high(middle, cols)
        quantise_high(left, left)
        for cols in narrow + [wide]:
            last_product(1, cols, high_codes[:, cols], high_planes[:, cols])

        by_row_tile = out.rearrange("(n p) m -> p n m", p=P)
        results = held([P, ROW_TILES, T2], F32, "results")
        for b, bank in enumerate(banks):
            if b < len(narrow):
                result, source = results[:, :, narrow[b]], bank[:].rearrange("p (n m) -> p n m", m=P)
            else:
                result, source = results[:, b - len(narrow), wide], bank[:]
            if b >= 3 and b % 2 == 1:
                nc.vector.tensor_copy(result, source)
            else:
                nc.scalar.copy(result, source)
            if b < len(narrow):
                nc.sync.dma_start(by_row_tile[:, :, narrow[b]], result)
            elif b % 2 == 1:
                pair = slice(b - len(narrow) - 1, b - len(narrow) + 1)
                nc.sync.dma_start(by_row_tile[:, pair, wide], results[:, pair, wide])
